import numpy as np, ml_dtypes
CORES = [48,51,52,55]
N = 4
BF = ml_dtypes.bfloat16
def gentries(a):
    return np.ascontiguousarray(a.reshape(8, 16, -1).transpose(0, 2, 1)).reshape(8, -1)
def gtable(e):
    e = np.asarray(e); return np.ascontiguousarray(e.reshape(8, -1, 16).transpose(0, 2, 1)).reshape(128, -1).astype(np.int32)
V, K, RO, TH, NR, A = 3840, 256, 5, 11, 9, 1
EPS = 0.5
P = V // 16
def kinds(rng):
    i = np.arange(V); cut = rng.random(V) < 0.04; cut[0] = True
    last = np.maximum.accumulate(np.where(cut, i, 0)); v = rng.integers(0, P, V)
    return (v[last] + i - last) % P
def names(rng, kd):
    o = np.argsort(kd, kind="stable"); n = np.bincount(kd, minlength=P); s = np.add.accumulate(n) - n
    b = np.zeros((N, 8, 16, P), np.int64)
    for k in range(P):
        new = o[np.minimum(s[k] + (rng.random((N, 8, 16)) * n[k]).astype(np.int64), V - 1)]
        nxt = (b[..., k - 1] + 1) % V
        b[..., k] = np.where((kd[nxt] == k) & (rng.random((N, 8, 16)) < 0.85), nxt, new) if k else new
    return b
def blur(rng, r, lev):
    u = rng.random(r.shape, dtype=np.float32)
    r = np.where(u < lev, r + rng.integers(-3, 4, r.shape), r)
    return np.where(u < 0.3 * lev, rng.integers(0, V, r.shape), r) % V
def parts(rng, lev=(0.0, 0.15, 0.35, 0.8), dev=(0.1, 0.3, 0.6, 1.0)):
    kd = kinds(rng); b = names(rng, kd)
    r = blur(rng, b[..., kd], rng.choice(np.array(lev), (N, 8, 1, V)))
    x = rng.standard_normal((N, 8, 16, P), dtype=np.float32)[..., kd]
    x = x + rng.choice(np.array(dev), (N, 8, 1, V)).astype(np.float32) * rng.standard_normal((N, 8, 16, V), dtype=np.float32)
    return kd, b, x, r, rng.integers(0, V, (N, 8, K))
def pack(x, r, w):
    x = np.clip(x, -4.0, 4.0); x = np.where(np.abs(x) < 2.0 ** -19, 0.0, x)
    return {"x": np.ascontiguousarray(x.reshape(N, 128, V)).astype(np.float32).astype(BF), "rec": np.ascontiguousarray(r.reshape(N, 128, V)).astype(np.int32), "w0": np.stack([gtable(a) for a in w])}
def setup_inputs(rng):
    kd, b, x, r, w = parts(rng)
    return pack(x, r, w)
def setup_inputs_spread(rng):
    kd, b, x, r, w = parts(rng, (0.0, 0.05, 0.4, 1.0), (0.02, 0.1, 0.5, 1.2))
    x = x * np.exp2(rng.integers(-1, 2, (N, 8, 1, V))).astype(np.float32)
    far = (rng.random((N, 8, 1, V)) < 0.7) & (np.arange(N) % 2 == 1)[:, None, None, None]
    x = x + np.where(far, 2.5, 0.0).astype(np.float32) * rng.standard_normal((N, 8, 16, V), dtype=np.float32)
    w = np.minimum((V * rng.random((N, 8, K)) ** 2).astype(np.int64), V - 1)
    return pack(x, r, w)
def setup_inputs_ends(rng):
    kd, b, x, r, w = parts(rng)
    pat = rng.choice(np.array([0, V - 1]), (N, 8, 16, 1)); pat[:, :, 0] = 0; pat[:, :, 15] = V - 1
    val = np.where(rng.random(r.shape, dtype=np.float32) < 0.2, V - 1 - pat, pat); kind = rng.integers(0, 4, (N, 8, 1, V))
    val = np.where(kind == 0, 0, np.where(kind == 1, V - 1, val))
    r = np.where(rng.random((N, 8, 1, V)) < 0.78, val, r)
    x = np.where(rng.random((N, 8, 1, V)) < 0.78, np.where(x < 0, -4.0, 4.0), x)
    xp = rng.choice(np.array([-4.0, 4.0]), (N, 8, 16)); pl = pat[..., 0]
    o1 = np.argsort(rng.random((N, 8, 16)), axis=2); o2 = np.argsort(rng.random((N, 8, 16)), axis=2)
    for v in [V - 1] + list(range(RO + 2)):
        n1 = rng.choice(np.array([0, 0, 16 - TH, 16 - TH, 17 - TH, 16]), (N, 8, 1)); n2 = rng.choice(np.array([0, 16 - NR, 16 - NR, 17 - NR]), (N, 8, 1))
        if v == V - 1: n1 = n1 * 0; n2 = n2 * 0
        r[..., v] = np.where(o1 < n1, V - 1 - pl, pl); x[..., v] = np.where(o2 < n2, -xp, xp)
    w = np.where(rng.random((N, 8, K)) < 0.75, rng.choice(np.array([0, V - 1]), (N, 8, K)), w)
    w[..., 0] = V - 1; w[..., 1] = 0; w[..., K - 1] = V - 1
    return pack(x, r, w)
def setup_inputs_corners(rng):
    kd, b, x, r, w = parts(rng); i = np.arange(V)
    for q in range(N):
        o = rng.permutation(8)
        for g in range(8):
            if o[g] == 0: r[q, g] = i
            if o[g] == 1: r[q, g] = 0
            if o[g] == 2: r[q, g] = V - 1
            if 3 <= o[g] <= 5: r[q, g] = (i + (int(o[g]) - 2)) % V
    w = np.where(rng.random((N, 8, K)) < 0.5, rng.choice(np.array([0, 1, 2, V - 3, V - 2, V - 1]), (N, 8, K)), w)
    w[..., 0] = V - 1; w[..., K - 1] = V - 1
    return pack(x, r, w)
def setup_inputs_ties(rng):
    kd = kinds(rng); b = names(rng, kd); c = b[..., kd]
    o = np.argsort(rng.random(c.shape, dtype=np.float32), axis=2); kind = rng.choice(np.array([0, 1, 2]), (N, 8, 1, V), p=[0.5, 0.3, 0.2])
    far = np.where(kind == 0, 0, np.where(kind == 1, 16 - TH, 17 - TH)); sg = rng.choice(np.array([-1, 1]), (N, 8, 1, V))
    s = np.where(o < far, 3 * sg, np.where((kind > 0) & (o % 2 == 1), 2 * sg, 0))
    r = c + s; r = np.where((r < 0) | (r >= V), c - s, r)
    x = 0.25 * rng.integers(-8, 9, (N, 8, 16, P))[..., kd]
    o = np.argsort(rng.random(c.shape, dtype=np.float32), axis=2); kind = rng.choice(np.array([0, 1, 2]), (N, 8, 1, V), p=[0.4, 0.3, 0.3])
    far = np.where(kind == 1, 16 - NR, 17 - NR); sg = rng.choice(np.array([-1.0, 1.0]), c.shape)
    x = x + np.where(kind > 0, np.where(o < far, 0.515625, 0.5) * sg, 0.0)
    return pack(x, r, rng.integers(0, V, (N, 8, K)))
def setup_inputs_crowd(rng):
    kd, b, x, r, w = parts(rng, (0.0, 0.1, 0.2, 0.3)); r[:, :, 1] = b[:, :, 1][..., kd]
    for q in range(N):
        for g in range(8):
            k = (g + q) % 8; v = int(rng.integers(0, V)); mem = np.flatnonzero(kd == kd[v])
            if k < 4: w[q, g] = v
            if k == 2: w[q, g, K - 1] = mem[int(rng.integers(0, len(mem)))]
            if k == 3: w[q, g, 0] = mem[int(rng.integers(0, len(mem)))]
            if k == 4 or k == 5: w[q, g] = mem[rng.integers(0, len(mem), K)]
            if k == 6: w[q, g] = rng.choice(np.array([v, (v + 1) % V, V - 1]), K)
    return pack(x, r, w)
def check_ranges(d):
    bad = []
    for k in ("rec", "w0"):
        if np.min(d[k]) < 0 or np.max(d[k]) > V - 1: bad.append("range of " + k)
    a = np.abs(np.asarray(d["x"]).astype(np.float32))
    if not np.all((a == 0) | ((a >= 2.0 ** -19) & (a <= 4.0))): bad.append("range of x")
    return bad
def likeness(R, c, w):
    rc = np.take_along_axis(R, c.reshape(8, 1, 16 * K), 2).reshape(8, 16, 16, K)
    rw = np.take_along_axis(R, w[:, None, :], 2)[:, :, None, :]
    return np.add.reduce(np.abs(rc - rw) <= 2, axis=1, dtype=np.int32)
def reference(x, rec, w0):
    X = np.asarray(x).astype(np.float32).reshape(N, 8, 16, V); R = rec.astype(np.int32).reshape(N, 8, 16, V)
    w = np.stack([gentries(a) for a in w0]).astype(np.int32); ys = []
    for t in range(1, RO + 1):
        new = R.copy(); S = []; nxt = []
        for a in range(N):
            c = np.take_along_axis(R[a], w[a][:, None, :], 2)
            ok = likeness(R[a], c, w[a]) >= TH
            for b in range(A):
                q = (a + 1 + ((t - 1) * A + b) % (N - 1)) % N
                ok = ok & (likeness(R[q][(np.arange(8) + t + b) % 8], c, w[a]) >= TH)
            o = ok[:, (t + np.arange(16)) % 16]; has = np.any(o, axis=1); k = (t + np.argmax(o, axis=1)) % 16
            j = np.where(has, np.take_along_axis(c, k[:, None, :], 1)[:, 0], w[a])
            z = ((j + 1) % V).astype(np.int32); n = (c + 1) % V
            xn = np.take_along_axis(X[a], n.reshape(8, 1, 16 * K), 2).reshape(8, 16, 16, K)
            xz = np.take_along_axis(X[a], z[:, None, :], 2)[:, :, None, :]
            S.append(np.add.reduce(np.exp(-np.abs(xn.astype(np.float64) - xz.astype(np.float64))), axis=2))
            if t < RO:
                put = np.add.reduce(np.abs(xn - xz) <= np.float32(EPS), axis=1, dtype=np.int32) >= NR
                for g in range(8):
                    at = np.flatnonzero(has[g])
                    u, first = np.unique(z[g, at], return_index=True); lw = at[first]
                    new[a, g][:, u] = np.where(put[g][:, lw], n[g][:, lw], R[a, g][:, u])
            nxt.append(z)
        R = new; w = np.stack(nxt); ys.append(np.stack(S))
    return {"y": np.concatenate(ys, axis=3).reshape(N, 128, RO * K).astype(np.float32)}

def check_inputs(d):
    bad = list(check_ranges(d))
    if not bad:
        for name, y in reference(**d).items():
            for q in range(N):
                v = np.abs(np.asarray(y[q], np.float64)); s = np.sqrt(np.mean(v * v))
                if v.max() > 4 * s or s < 2.0 ** 1: bad.append('%s of rank %d is uneven or too small' % (name, q))
    return bad

@@ -1,0 +1,527 @@
+from concourse.bass import DstId, RemoteDMATransfer
+from concourse.mybir import AluOpType as ALU, ActivationFunctionType as AF
+
+V, K, RO, TH, NR = 3840, 256, 5, 11, 9
+SH = 17
+RW = 3880
+XW = 16 + 2 * V
+JD = 2
+B2 = 1.5 * 2.0 ** 25
+BH = 1.5 * 2.0 ** 23
+NCH = 4
+
+HEAD = ("xgX0 xgX1 oX0 oX1 oX2 eoX02 oX3 oY0 eoX21 gX0 gX1 gX2 egX02 gX3 egX21 egX31 rX xgY0 xgY1 preX0 preX1 preX2 preX3 "
+        "gY0 gY1 gY2 egY02 preY0 gY3 egY21 egY31 rY eoX31 oY1 chX0 eoY01 chX1 preY1 eoY11 chX2 poX0 poX1 poX2 poX3 ")
+SEQ = HEAD + "abX0 abX1 abX2 sgX02 abX3 sgX22 oY2 oY3 eoY21 eoY31"
+SEQL = HEAD + "abX0 abX1 abX3 abX2 oY2 oY3 eoY21 eoY31"
+SEQ2 = ("lX clX0 chY0 clX1 clX4 chY1 preY2 preY3 clX2 clX3 chY2 poY2 poY0 poY3 poY1 ctX01 ctX10 ctX20 ctX32 abY2 abY3 sgY2 sgY3 "
+        "lY fX0 clY4 fX1 nrY0 ctY01 clY0 fX2 nrY1 clY1 clX5 clY2 clX6 clY3 ctY10 ctY20 ctY32 abY0 abY1 "
+        "puX7 puX6 puX5 puX4 puX3 puX2 puX1 puX0 clY5 clY6 puY7 puY6 puY5 puY4 puY3 puY2 puY1 puY0")
+SEQ3 = ("teX0 teX1 chY0 chY1 preY2 preY3 taX0 chY2 poY3 poY0 poY1 poY2 teX2 taX1 teX3 daY3 abY0 abY1 taX2 taX3 stX "
+        "teY0 abY2 teY3 taY0 teY1 taY3 teY2 taY1 taY2 stY")
+
+SCRATCH = {
+    "recs": ("sbuf", [128, V], "int32"), "Rt": ("sbuf", [128, RW], "float32"), "xe": ("sbuf", [128, XW], "bfloat16"),
+    "w0s": ("sbuf", [128, 16], "int32"),
+    "g1": ("sbuf", [128, 512], "float32"), "tr": ("sbuf", [128, 512], "float32"),
+    "O": ("sbuf", [128, RO * 256], "uint16"), "Oin": ("sbuf", [128, RO * 256], "uint16"), "Og": ("sbuf", [128, RO * 256], "uint16"),
+    "WL": ("sbuf", [128, RO * 96], "uint16"), "Win": ("sbuf", [128, RO * 64], "uint16"), "Wg": ("sbuf", [128, RO * 64], "uint16"),
+    "Rw": ("sbuf", [128, 1024], "float32"), "Rwg": ("sbuf", [128, 1024], "float32"),
+    "do": ("sbuf", [128, 4096], "bfloat16"), "dg": ("sbuf", [128, 4096], "bfloat16"),
+    "xn": ("sbuf", [128, 4096], "bfloat16"), "ad": ("sbuf", [128, 4096], "float32"), "ex": ("sbuf", [128, 4096], "float32"),
+    "nr": ("sbuf", [128, 4096], "bfloat16"),
+    "rep": ("sbuf", [128, RO * 256], "bfloat16"), "repin": ("sbuf", [128, RO * 256], "bfloat16"),
+    "rr": ("sbuf", [128, 256], "bfloat16"), "n17": ("sbuf", [128, 256], "float32"), "ok": ("sbuf", [128, 256], "bfloat16"),
+    "tm": ("sbuf", [128, 256], "float32"), "sc": ("sbuf", [128, 256], "float32"), "sB": ("sbuf", [128, 256], "float32"),
+    "eq": ("sbuf", [128, 256], "float32"), "sc2": ("sbuf", [128, 256], "float32"), "Ed": ("sbuf", [128, 256], "float32"),
+    "pr": ("sbuf", [128, 256], "float32"), "xz": ("sbuf", [128, 256], "bfloat16"),
+    "mm": ("sbuf", [128, 16], "float32"), "mu": ("sbuf", [128, 16], "uint16"), "hh": ("sbuf", [128, 16], "float32"),
+    "zz": ("sbuf", [128, 16], "float32"), "ee": ("sbuf", [128, 16], "float32"), "F0": ("sbuf", [128, 16], "float32"),
+    "F": ("sbuf", [128, 16], "float32"), "vv": ("sbuf", [128, 16], "float32"), "tg": ("sbuf", [128, 32], "uint16"),
+    "acc": ("sbuf", [128, 256], "float32"),
+    "fl": ("sbuf", [128, (RO - 1) * 256], "float32"), "yl": ("sbuf", [128, (RO - 1) * 256], "float32"),
+    "pi": ("sbuf", [128, 8], "int32"), "pa": ("sbuf", [128, 8], "int32"), "pb": ("sbuf", [128, 4], "int32"),
+    "pos": ("sbuf", [128, 8], "float32"), "pbf": ("sbuf", [128, 4], "float32"), "lin": ("sbuf", [128, 8], "float32"),
+    "col": ("sbuf", [128, 8], "float32"),
+    "c16": ("sbuf", [128, 16], "float32"), "c3": ("sbuf", [128, 8], "float32"),
+    "ck": ("sbuf", [128, 144], "bfloat16"), "q": ("sbuf", [128, 256], "bfloat16"), "q16": ("sbuf", [128, 128], "bfloat16"),
+    "L3": ("sbuf", [128, 8], "uint16"), "LL": ("sbuf", [128, 6], "uint16"), "LD": ("sbuf", [128, 8], "uint16"),
+    "band": ("sbuf", [128, 256], "bfloat16"), "I": ("sbuf", [128, 128], "bfloat16"), "blk": ("sbuf", [128, 128], "bfloat16"),
+    "In": ("sbuf", [128, 128], "bfloat16"), "I16": ("sbuf", [128, 128], "bfloat16"), "blk2": ("sbuf", [128, 128], "bfloat16"),
+    "Iv": ("sbuf", [128, 128], "bfloat16"), "If": ("sbuf", [128, 128], "float32"), "bn": ("sbuf", [128, 128], "float32"),
+    "bt": ("sbuf", [128, RO * 128], "bfloat16"), "Bt": ("sbuf", [128, RO * 128], "bfloat16"), "Lt": ("sbuf", [128, RO * 128], "bfloat16"),
+    "M1": ("sbuf", [128, 128], "bfloat16"), "M2": ("sbuf", [128, 128], "bfloat16"), "I2": ("sbuf", [128, 128], "bfloat16"),
+    "RS": ("sbuf", [128, 128], "float32"), "RS2": ("sbuf", [128, 128], "float32"),
+    "ps": ("psum", [128, 4096], "float32"),
+}
+SEMAPHORES = (["cv", "ca", "cp", "cg", "sent", "lw", "lx0", "lx1", "ys"] + ["lr%d" % i for i in range(NCH)]
+              + ["%s%d" % (n, t) for n in ("aw", "aox", "aoy", "arx", "ary", "rw", "rox", "roy", "af", "ay", "sf") for t in range(1, RO + 1)])
+
+
+def helpers(T, topo):
+    out = {}
+    for c in T.cores:
+        for h in topo.cores_of(c):
+            if T.rank_of(h) is None and h not in out.values() and topo.die(h) == topo.die(c):
+                out[c] = h
+                break
+    return out
+
+
+def mask_of(engs):
+    m = 0
+    for e in engs:
+        m |= 1 << e
+    return m
+
+
+def rank_program(g, core, T, topo):
+    hp = helpers(T, topo)
+    rank = T.rank_of(core)
+    if rank is None:
+        for c in T.cores:
+            if hp[c] == core:
+                helper_program(g, core, c, T, topo)
+        return
+    group_program(g, core, rank, hp[core], T, topo)
+
+
+def helper_program(g, core, c, T, topo):
+    rid, pid, _ = topo.addr(c)
+    en = topo.engines(core, c)[0::2]
+    nf = len(topo.engines(c, core)[1::2])
+    for t in range(1, RO):
+        g.wait_ge(T.sem["af%d" % t], nf)
+        s = slice((t - 1) * 256, t * 256)
+        g.remote_dma(T.yl[:, s], T.fl[:, s], T.sem["ay%d" % t], T.sem.sent, pid, rid, mask_of(en))
+    g.wait_ge(T.sem.sent, len(en) * (RO - 1))
+
+
+def group_program(g, core, rank, helper, T, topo):
+    N = len(T.cores)
+    Q = {"v": g.vector, "a": g.scalar, "p": g.tensor, "g": g, "s": g.sync}
+    CS = {"v": "cv", "a": "ca", "p": "cp", "g": "cg"}
+    ops, lastw, readers, bankacc, totals = [], {}, {}, {}, {}
+
+    def op(q, fn, r=(), w=(), banks=(), ext=(), tok=None, inc=None):
+        me = len(ops)
+        who = q if tok is None else "dma%d" % me
+        deps = set()
+        for x in r:
+            if x in lastw:
+                deps.add(lastw[x])
+        for x in w:
+            deps.update(readers.get(x, []) + ([lastw[x]] if x in lastw else []))
+        for b in banks:
+            for e, d in bankacc.setdefault(b, {}).items():
+                if e != who:
+                    deps.add(d)
+            bankacc[b][who] = me
+        if q == "p":
+            deps = set(d for d in deps if ops[d]["who"] != "p")
+        for x in r:
+            readers.setdefault(x, []).append(me)
+        for x in w:
+            lastw[x] = me
+            readers[x] = []
+        ops.append({"q": q, "who": who, "fn": fn, "deps": deps, "ext": list(ext), "tok": tok, "inc": inc})
+
+    def emit():
+        need = set()
+        for o in ops:
+            top = {}
+            for d in o["deps"]:
+                top[ops[d]["who"]] = max(top.get(ops[d]["who"], -1), d)
+            o["deps"] = set(top.values())
+            need |= o["deps"]
+        cnt = {}
+        for i, o in enumerate(ops):
+            if o["tok"] is None and i in need:
+                cnt[o["q"]] = cnt.get(o["q"], 0) + 1
+                o["tok"] = (CS[o["q"]], cnt[o["q"]])
+                o["inc"] = 1
+        seen = {}
+        for o in ops:
+            want = {}
+            for s, n in [ops[d]["tok"] for d in o["deps"]] + o["ext"]:
+                want[s] = max(want.get(s, 0), n)
+            for s in sorted(want):
+                if seen.get((o["q"], s), 0) < want[s]:
+                    Q[o["q"]].wait_ge(T.sem[s], want[s])
+                    seen[(o["q"], s)] = want[s]
+            ins = o["fn"]()
+            if o["inc"]:
+                ins.then_inc(T.sem[o["tok"][0]], o["inc"])
+            if o["tok"] is not None:
+                totals[o["tok"][0]] = max(totals.get(o["tok"][0], 0), o["tok"][1])
+        for s in sorted(totals):
+            if max([n for (q, s2), n in seen.items() if s2 == s] + [0]) < totals[s]:
+                g.wait_ge(T.sem[s], totals[s])
+
+    v, a, pe = g.vector, g.scalar, g.tensor
+
+    def ts(out, in0, s1, op0, s2=None, op1=None, r=(), w=(), banks=()):
+        if op1 is None:
+            op("v", lambda: v.tensor_scalar(out, in0, s1, None, op0), r, w, banks)
+        else:
+            op("v", lambda: v.tensor_scalar(out, in0, s1, s2, op0, op1), r, w, banks)
+
+    def tt(out, in0, in1, o, r=(), w=(), banks=()):
+        op("v", lambda: v.tensor_tensor(out, in0, in1, o), r, w, banks)
+
+    def cp(out, in_, r=(), w=(), banks=()):
+        op("v", lambda: v.tensor_copy(out, in_), r, w, banks)
+
+    def scan(out, d0, d1, o1, r, w, banks=()):
+        op("v", lambda: v.tensor_tensor_scan(out, d0, d1, 0.0, ALU.mult, o1), r, w, banks)
+
+    def act(out, in_, f, bias=0.0, scale=1.0, r=(), w=(), banks=()):
+        op("a", lambda: a.activation(out, in_, f, bias=bias, scale=scale), r, w, banks)
+
+    def mm(out, lhsT, rhs, start, stop, r, w, bank, ext=()):
+        op("p", lambda: pe.matmul(out, lhsT, rhs, start, stop), r, w, [bank], ext)
+
+    def dma(q, out, in_, sem, n, r=(), w=(), ext=()):
+        op(q, lambda: Q[q].dma_start(out, in_), r, w, (), ext, tok=(sem, n), inc=16)
+
+    nsent = [0]
+
+    def send(dst, out, in_, sem, r):
+        rid, pid, _ = topo.addr(dst)
+        en = topo.engines(core, dst)[0::2]
+        nsent[0] += len(en)
+        op("g", lambda: g.remote_dma(out, in_, T.sem[sem], T.sem.sent, pid, rid, mask_of(en)), r, (), tok=("sent", nsent[0]))
+
+    def ps(b, lo=0, hi=512):
+        return T.ps[:, b * 512 + lo:b * 512 + hi]
+
+    def s256(t):
+        return slice((t - 1) * 256, t * 256)
+
+    def hs(h, n=128, base=0):
+        return slice(base + h * n, base + (h + 1) * n)
+
+    def guest(t):
+        return T.cores[(rank + 1 + (t - 1) % (N - 1)) % N]
+
+    def asker(t):
+        return T.cores[(rank - 1 - (t - 1) % (N - 1)) % N]
+
+    def narr(src):
+        return len(topo.engines(src, core)[0::2])
+
+    def turn(out, in_, lo, hi, t, arr, sem, name):
+        s = 16 * (t % 8)
+        dma("s", out[s:128, lo:hi], in_[0:128 - s, lo:hi], sem, 32, (), [name + "a"], [(arr, narr(asker(t)))])
+        dma("s", out[0:s, lo:hi], in_[128 - s:128, lo:hi], sem, 32, (), [name + "b"])
+
+    cw = V // NCH
+    dma("s", T.w0s[:], T.w0[:], "lw", 16, w=["w0s"])
+    for i in range(NCH):
+        dma("s" if i % 2 == 0 else "a", T.recs[:, i * cw:(i + 1) * cw], T.rec[:, i * cw:(i + 1) * cw], "lr%d" % i, 16, w=["recs%d" % i])
+
+    def iota(out, pat, base, cm, name, flag=True):
+        if flag:
+            op("g", lambda: g.iota(out, pat, base, cm, allow_small_or_imprecise_dtypes=True), (), [name])
+        else:
+            op("g", lambda: g.iota(out, pat, base, cm), (), [name])
+    iota(T.pi[:], [[-1, 8]], 16, 1, "pi", False)
+    iota(T.c16[:], [[1, 16]], 0, 0, "c16")
+    iota(T.c3[:], [[2, 8]], 16, 0, "c3")
+    iota(T.q[:], [[0, 2], [1, 128]], 0, 0, "q")
+    iota(T.q16[:], [[16, 8], [0, 16]], 0, 0, "q16")
+    iota(T.ck[:], [[0, 9], [1, 16]], 0, 0, "ck")
+    op("v", lambda: v.memset(T.Rt[:, 0:SH], 0.0), (), ["Rta"])
+    op("v", lambda: v.memset(T.Rt[:, SH + V:RW], 0.0), (), ["Rtb"])
+    op("v", lambda: v.memset(T.xe[:, 0:16], 0.0), (), ["xe0"])
+    op("v", lambda: v.memset(T.RS[:], 1.0), (), ["RS"])
+    op("v", lambda: v.memset(T.RS2[:], 1.0), (), ["RS2"])
+    op("v", lambda: v.memset(T.RS[:, 0::16], 0.0), (), ["RS"])
+    op("v", lambda: v.memset(T.RS2[:, 0::16], 0.0), (), ["RS2"])
+    op("v", lambda: v.memset(T.RS2[:, 15::16], 8192.0), (), ["RS2"])
+    RT = ["Rt", "Rta", "Rtb"] + ["Rt%d" % i for i in range(NCH)]
+    pk, C = T.pos[:, 0:1], T.col
+    ts(T.pa[:], T.pi[:], 15, ALU.bitwise_and, r=["pi"], w=["pa"])
+    ts(T.pb[:, 0:1], T.pi[:, 0:1], 16, ALU.bitwise_and, r=["pi"], w=["pb0"])
+    ts(T.pb[:, 2:3], T.pi[:, 0:1], 7, ALU.bitwise_and, r=["pi"], w=["pb2"])
+    ts(C[:, 0:1], T.pi[:, 0:1], -16.0, ALU.add, r=["pi"], w=["c0"])
+    cp(T.pos[:], T.pa[:], ["pa"], ["pos"])
+    ts(T.pb[:, 1:2], T.pa[:, 0:1], 1, ALU.logical_shift_right, r=["pa"], w=["pb1"])
+    ts(T.pb[:, 3:4], T.pa[:, 0:1], 3, ALU.logical_shift_right, r=["pa"], w=["pb3"])
+    ts(T.LD[:], T.c16[:, 0:8], 16.0, ALU.mult, 15.0, ALU.add, r=["c16"], w=["LD"])
+    cp(T.pbf[:], T.pb[:], ["pb0", "pb1", "pb2", "pb3"], ["pbf"])
+    tt(C[:, 1:2], C[:, 0:1], pk, ALU.subtract, ["c0", "pos"], ["c1"])
+    ts(T.LL[:, 0:2], T.c16[:, 0:2], 0.0, ALU.mult, T.pbf[:, 2:3], ALU.add, r=["c16", "pbf"], w=["LLa"])
+    ts(T.LL[:, 2:4], T.c16[:, 8:10], 8.0, ALU.min, T.pbf[:, 2:3], ALU.add, r=["c16", "pbf"], w=["LLb"])
+    ts(T.LL[:, 4:6], T.c16[:, 0:2], 8.0, ALU.mult, T.pbf[:, 1:2], ALU.add, r=["c16", "pbf"], w=["LLc"])
+    ts(C[:, 2:3], T.pbf[:, 2:3], 32.0, ALU.mult, T.pbf[:, 3:4], ALU.add, r=["pbf"], w=["c2"])
+    for h in range(2):
+        ts(T.zz[:, hs(h, 8)], T.w0s[:, hs(1 - h, 8)], -1.0, ALU.mult, float(8192 - SH), ALU.add, r=["w0s"], w=["zz%d" % h])
+
+    def lists(t, h):
+        o = (t - 1) * 96
+        if h == 0:
+            ts(T.WL[:, o:o + 32], T.zz[:, 0:8].indirect(T.LL[:, 0:2]), -1.0, ALU.mult, 8192.0, ALU.add, r=["zz0", "LLa"], w=["WL%d0" % t])
+        else:
+            ts(T.WL[:, o + 32:o + 96], T.zz[:].indirect(T.LL[:, 2:6]), -1.0, ALU.mult, 8192.0, ALU.add,
+               r=["zz0", "zz1", "LLb", "LLc"], w=["WL%d1" % t])
+            send(guest(t), T.Win[:, (t - 1) * 64:t * 64], T.WL[:, o:o + 64], "aw%d" % t, ["WL%d0" % t, "WL%d1" % t])
+            turn(T.Wg, T.Win, (t - 1) * 64, t * 64, t, "aw%d" % t, "rw%d" % t, "Wg%d" % t)
+
+    def fall(i):
+        if i == 0:
+            ts(T.ee[:], T.zz[:], float(8192 - SH - V + 1), ALU.is_equal, float(V), ALU.mult, r=["zz0", "zz1"], w=["ee"])
+        elif i == 1:
+            tt(T.F0[:], T.ee[:], T.zz[:], ALU.add, ["ee", "zz0", "zz1"], ["F0"])
+        else:
+            ts(T.F[:], T.F0[:], float(-V - 1), ALU.add, r=["F0"], w=["F"])
+
+    lists(1, 0)
+    lists(1, 1)
+    tt(C[:, 3:4], C[:, 2:3], T.pbf[:, 0:1], ALU.subtract, ["c2", "pbf"], ["c3c"])
+    ts(C[:, 4:5], pk, float(SH + V), ALU.add, r=["pos"], w=["c4"])
+    ts(C[:, 5:6], pk, float(4 * JD), ALU.is_lt, float(NR - (2 * NR - 16)), ALU.mult, r=["pos"], w=["c5"])
+    ts(T.lin[:], T.pos[:], -14.0, ALU.add, 8192.0, ALU.mult, r=["pos"], w=["lin"])
+    fall(0)
+    ts(T.I[:], T.q[:, 0:128], C[:, 0:1], ALU.is_equal, r=["q", "c0"], w=["I"])
+    ts(T.L3[:], T.c3[:], C[:, 3:4], ALU.add, r=["c3", "c3c"], w=["L3"])
+    ts(C[:, 6:7], C[:, 5:6], float(2 * NR - 16), ALU.add, r=["c5"], w=["c6"])
+    fall(1)
+    ts(T.band[:], T.q[:], C[:, 1:2], ALU.is_equal, r=["q", "c1"], w=["band"])
+    ts(T.blk[:], T.q16[:], C[:, 1:2], ALU.is_equal, r=["q16", "c1"], w=["blk"])
+    fall(2)
+    for nm, src, sc in (("In", "I", -1.0), ("I16", "I", 16.0), ("Iv", "I", float(-V)), ("If", "I", 1.0), ("bn", "blk", -1.0)):
+        act(T[nm][:], T[src][:], AF.Identity, scale=sc, r=[src], w=[nm])
+    for t in range(1, RO + 1):
+        act(T.Lt[:, hs(t - 1)], T.blk[:], AF.Identity, scale=T.lin[:, t:t + 1], r=["blk", "lin"], w=["Lt%d" % t])
+    dma("a", T.xe[:, 16:16 + V], T.x[:], "lx0", 16, r=["recs%d" % (NCH - 1)], w=["xe1"])
+    dma("a", T.xe[:, 16 + V:XW], T.x[:], "lx1", 16, w=["xe2"])
+    XE = ["xe0", "xe1", "xe2"]
+    ts(T.M1[:], T.ck[:, 0:128], pk, ALU.not_equal, -16384.0, ALU.mult, r=["ck", "pos"], w=["M1"])
+    ts(T.M2[:], T.ck[:, 0:128], pk, ALU.is_gt, -16384.0, ALU.mult, r=["ck", "pos"], w=["M2"])
+    for t in range(1, RO + 1):
+        ts(T.bt[:, hs(t - 1)], T.ck[:, 16 - t:144 - t], T.pos[:, t:t + 1], ALU.is_ge, -8192.0, ALU.mult, r=["ck", "pos"], w=["bt%d" % t])
+
+    def order():
+        op("g", lambda: g.affine_select(T.Bt[:], T.bt[:], [[0, RO], [-16, 8], [0, 16]], ALU.is_ge, 0.0, 0, 1),
+           ["bt%d" % t for t in range(1, RO + 1)], ["Bt"])
+        op("g", lambda: g.affine_select(T.Bt[:], T.Bt[:], [[0, RO], [16, 8], [0, 16]], ALU.is_ge, 0.0, 15, -1), ["Bt"], ["Bt"])
+        op("g", lambda: g.affine_select(T.Bt[:], T.Bt[:], [[0, RO], [-1, 128]], ALU.not_equal, 8192.0, 0, 1), ["Bt"], ["Bt"])
+    for i in range(NCH):
+        ts(T.Rt[:, SH + i * cw:SH + (i + 1) * cw], T.recs[:, i * cw:(i + 1) * cw], float(SH), ALU.add, r=["recs%d" % i], w=["Rt%d" % i])
+
+    CB, GB, NB, ZB = [4, 5], [6, 7], 3, [4, 2]
+    DB = [[0, 1, 2, 3], [6, 7, 0, 1]]
+
+    EB = [[4, 3, 4, 3], DB[1]]
+
+    def cs(h, c, n=1):
+        return slice(2048 * h + 512 * c, 2048 * h + 512 * (c + n))
+
+    def gd(t, own, h, c):
+        o = (t - 1) * 256 + 128 * h + 32 * c
+        rd = ["O%d%d" % (t, h), "Rw%d" % h] if own else ["Og%d%da" % (t, h), "Og%d%db" % (t, h), "Rwg"]
+        tt((T.do if own else T.dg)[:, cs(h, c)], T.Rt[:].indirect((T.O if own else T.Og)[:, o:o + 32]),
+           (T.Rw if own else T.Rwg)[:, hs(h, 512)], ALU.subtract, RT + rd, ["d%d%d%d" % (own, h, c)])
+
+    def eqc(t, own, h, c, n):
+        d = T.do if own else T.dg
+        nm = ["d%d%d%d" % (own, h, c + i) for i in range(n)]
+        ts(d[:, cs(h, c, n)], d[:, cs(h, c, n)], B2, ALU.add, B2, ALU.is_equal, r=nm, w=nm)
+        b = CB[h] if own else GB[h]
+        for k in range(4 * c, 4 * (c + n)):
+            s = ((0 if own else 16 * t) - k) % 128
+            if own and k == 15:
+                mm(ps(b, 0, 128), T.I16[:], T.repin[:, hs(h, 128, (t - 1) * 256)], False, False, ["I16"], ["L1%d" % h], b,
+                   [("ar%s%d" % ("xy"[h], t), narr(guest(t)))])
+            mm(ps(b, 0, 128), T.band[:, s:s + 128], d[:, hs(k, 128, 2048 * h)], k == 0, k == 15,
+               [nm[k // 4 - c], "band"], ["L%d%d" % (own, h)], b)
+
+    def reply(t, h):
+        s = hs(h, 128, (t - 1) * 256)
+        act(T.rep[:, s], ps(GB[h], 0, 128), AF.Sign, bias=0.5 - TH, r=["L0%d" % h], w=["rep%d%d" % (t, h)], banks=[GB[h]])
+        send(asker(t), T.repin[:, s], T.rep[:, s], "ar%s%d" % ("xy"[h], t), ["rep%d%d" % (t, h)])
+
+    def xg(t, h, c):
+        o = (t - 1) * 256 + 128 * h + 64 * c
+        act(T.xn[:, cs(h, 2 * c, 2)], T.xe[:].indirect(T.O[:, o:o + 64]), AF.Identity, r=XE + ["O%d%d" % (t, h)], w=["xn%d%d" % (h, c)])
+
+    def pre(h, j):
+        mm(ps(DB[h][j]), T.I[:], T.xn[:, cs(h, j)], True, False, ["I", "xn%d%d" % (h, j // 2)], ["df%d%d" % (h, j)], DB[h][j])
+
+    def post(h, j):
+        for i in range(4):
+            mm(ps(DB[h][j], 128 * i, 128 * i + 128), T.In[:], T.xz[:, hs(h)], False, i == 3, ["In", "xz%d" % h], ["df%d%d" % (h, j)], DB[h][j])
+
+    def absd(h, j):
+        act(T.ad[:, cs(h, j)], ps(DB[h][j]), AF.Abs, r=["df%d%d" % (h, j)], w=["ad%d%d" % (h, j)], banks=[DB[h][j]])
+
+    def count(h, j, first, last):
+        for i in range(4):
+            k = 4 * j + i
+            s = (-k) % 128
+            mm(ps(CB[h], 0, 128), T.band[:, s:s + 128], T.nr[:, hs(k, 128, 2048 * h)], first and i == 0, last and i == 3,
+               ["nr%d%d" % (h, j), "band"], ["NC%d" % h], CB[h])
+
+    def near(h, j):
+        ts(T.nr[:, cs(h, j)], ps(DB[h][j]), BH, ALU.add, BH, ALU.is_equal, r=["df%d%d" % (h, j)], w=["nr%d%d" % (h, j)], banks=[DB[h][j]])
+
+    def sgn(h, j, n=1):
+        act(T.nr[:, cs(h, j, n)], T.ad[:, cs(h, j, n)], AF.Sign, bias=0.5 + 2.0 ** -21, scale=-1.0,
+            r=["ad%d%d" % (h, j + i) for i in range(n)], w=["nr%d%d" % (h, j + i) for i in range(n)])
+
+    def expo(h):
+        act(T.ex[:, hs(h, 2048)], T.ad[:, hs(h, 2048)], AF.Exp, scale=-1.0, r=["ad%d%d" % (h, j) for j in range(4)], w=["ex%d" % h])
+
+    def fold(t):
+        rid, pid, _ = topo.addr(helper)
+        en = topo.engines(core, helper)[1::2]
+        n = len(en) // 2
+        trs = [RemoteDMATransfer(dst_ids=[DstId(rid=rid, pnc=pid)], dma_engine_mask=mask_of(en[h * n:(h + 1) * n]),
+                                 remote_sem=T.sem["af%d" % t], srcs=[T.ex[:, hs(k, 128, 2048 * h)] for k in range(16)],
+                                 dsts=[T.fl[:, hs(1 - h, 128, (t - 1) * 256)]], alu_op=1) for h in range(2)]
+        op("g", lambda: g.remote_dma_fused(trs, local_sem=T.sem["sf%d" % t]), ["ex0", "ex1"], (), tok=("sf%d" % t, len(en)))
+
+    nys = [0]
+
+    def ystore(t):
+        nys[0] += 16
+        dma("s", T.y[:, s256(t)], T.yl[:, s256(t)], "ys", nys[0], ext=[("ay%d" % t, narr(helper))])
+
+    def chain(t, h, i):
+        b, z, H = CB[h], ZB[h], "%d" % h
+        e8 = hs(h, 8)
+        if i == 0:
+            ts(T.ok[:, hs(h)], ps(b, 0, 128), float(16 + TH), ALU.is_ge, r=["L1" + H], w=["ok" + H], banks=[b])
+            mm(ps(b, 128, 256), T.Bt[:, hs(t - 1)], T.ok[:, hs(h)], True, True, ["Bt", "ok" + H], ["val" + H], b)
+        if i == 1:
+            if z == b:
+                tt(T.tm[:, hs(h)], ps(b, 128, 256), T.n17[:, hs(h)], ALU.min, ["val" + H, "n17"], ["tm" + H], [b])
+            mm(ps(z, 256, 384), T.I[:], T.M1[:], True, False, ["I", "M1"], ["Z" + H], z)
+            mm(ps(z, 256, 384), T.I[:], T.M2[:], False, False, ["I", "M2"], ["Z" + H], z)
+            mm(ps(z, 256, 384), T.Lt[:, hs(t - 1)], T.ok[:, hs(h)], False, False, ["Lt%d" % t, "ok" + H], ["Z" + H], z)
+            if z != b:
+                tt(T.tm[:, hs(h)], ps(b, 128, 256), T.n17[:, hs(h)], ALU.min, ["val" + H, "n17"], ["tm" + H], [b])
+            mm(ps(z, 256, 384), T.bn[:], T.tm[:, hs(h)], False, True, ["bn", "tm" + H], ["Z" + H], z)
+        if i == 2:
+            scan(T.sc[:, hs(h)], T.RS[:], ps(z, 256, 384), ALU.max, ["RS", "Z" + H], ["sc" + H], [z])
+            if t < RO:
+                act(T.sB[:, hs(h)], ps(z, 256, 384), AF.Identity, bias=16384.0, r=["Z" + H], w=["sB" + H], banks=[z])
+            tt(T.mm[:, e8], T.sc[:, 128 * h + 15:128 * h + 128:16], T.F[:, e8], ALU.max, ["sc" + H, "F"], ["mm" + H])
+            ts(T.mu[:, e8], T.mm[:, e8], -1.0, ALU.mult, 8191.0, ALU.add, r=["mm" + H], w=["mu" + H])
+            if t < RO:
+                ts(T.hh[:, e8], T.mm[:, e8], float(8192 - SH - V + 1), ALU.is_lt, float(V), ALU.mult, r=["mm" + H], w=["hh" + H])
+            cp(T.xz[:, hs(h)], T.xe[:].indirect(T.mu[:, e8]), XE + ["mu" + H], ["xz" + H])
+            if t < RO:
+                tt(T.zz[:, e8], T.mm[:, e8], T.hh[:, e8], ALU.add, ["mm" + H, "hh" + H], ["zz" + H])
+
+    def claim(t, h, i):
+        H, e8, b = "%d" % h, hs(h, 8), CB[h]
+        if i == 0:
+            tt(T.eq[:, hs(h)], T.sc[:, hs(h)].indirect(T.LD[:]), T.sB[:, hs(h)], ALU.is_equal, ["sc" + H, "LD", "sB" + H], ["eq" + H])
+        if i == 1:
+            scan(T.sc2[:, hs(h)], T.RS2[:], T.eq[:, hs(h)], ALU.add, ["RS2", "eq" + H], ["sc2" + H])
+        if i == 2:
+            s = slice(128 * h + 15, 128 * h + 128, 16)
+            tt(T.vv[:, e8], T.sc2[:, s], T.sc[:, s], ALU.subtract, ["sc2" + H, "sc" + H], ["vv" + H])
+        if i == 3:
+            ts(T.tg[:, 16 * h:16 * h + 16:2], T.vv[:, e8], 8192.0, ALU.add, C[:, 4:5], ALU.min, r=["vv" + H, "c4"], w=["tg" + H])
+        if i == 4:
+            o = t * 96 + 32 * h
+            tt(T.Ed[:, hs(h)], T.Rt[:].indirect(T.WL[:, o:o + 8]), T.n17[:, hs(h)], ALU.subtract, RT + ["WL%d%d" % (t + 1, h), "n17"], ["Ed" + H])
+        if i == 5:
+            ts(ps(b, 384, 512), ps(b, 0, 128), C[:, 6:7] if h else float(2 * NR - 16), ALU.is_lt, r=["NC" + H, "c6"], w=["np" + H], banks=[b])
+        if i == 6:
+            tt(T.pr[:, hs(h)], T.Ed[:, hs(h)], ps(b, 384, 512), ALU.mult, ["Ed" + H, "np" + H], ["pr" + H], [b])
+
+    def put(h, b):
+        s = hs(8 * h + b, 16)
+        tt(T.Rt[:].indirect(T.tg[:, 16 * h + 2 * b:16 * h + 2 * b + 1]), T.pr[:, s], T.n17[:, s], ALU.add,
+           ["tg%d" % h, "pr%d" % h, "n17"], ["Rt"])
+
+    def tail_exp(h, j):
+        act(ps(EB[h][j]), T.ad[:, cs(h, j)], AF.Exp, scale=-1.0, r=["ad%d%d" % (h, j)],
+            w=["e%d%d" % (h, j)] + ["df%d%d" % (h, i) for i in range(4) if DB[h][i] == EB[h][j]], banks=[EB[h][j]])
+
+    def tail_add(h, j):
+        s = T.acc[:, hs(1 - h)]
+        for i in range(4):
+            e = ps(EB[h][j], 128 * i, 128 * i + 128)
+            if j == 0 and i == 0:
+                cp(s, e, ["e%d0" % h], ["acc%d" % h], [EB[h][j]])
+            else:
+                tt(s, s, e, ALU.add, ["acc%d" % h, "e%d%d" % (h, j)], ["acc%d" % h], [EB[h][j]])
+
+    def tail_store(h):
+        nys[0] += 16
+        dma("s", T.y[:, hs(1 - h, 128, (RO - 1) * 256)], T.acc[:, hs(1 - h)], "ys", nys[0], r=["acc%d" % h])
+
+    def offsets(t, h):
+        s, n = hs(h, 128, (t - 1) * 256), "%s%d" % ("xy"[h], t)
+        op("v", lambda: v.transpose(T.tr[:, hs(h, 256)], T.g1[:, hs(h, 256)]), ["g1%d" % h], ["tr%d" % h])
+        cp(T.O[:, s], T.tr[:, hs(h, 256)].indirect(T.L3[:]), ["tr%d" % h, "L3"], ["O%d%d" % (t, h)])
+        send(guest(t), T.Oin[:, s], T.O[:, s], "ao" + n, ["O%d%d" % (t, h)])
+        turn(T.Og, T.Oin, s.start, s.stop, t, "ao" + n, "ro" + n, "Og%d%d" % (t, h))
+
+    def tail_abs(t, h, j):
+        s = T.ex[:, cs(h, j)]
+        ts(s, ps(DB[h][j]), -1.0, ALU.mult, r=["df%d%d" % (h, j)], w=["ex%d" % h], banks=[DB[h][j]])
+        tt(T.ad[:, cs(h, j)], s, ps(DB[h][j]), ALU.max, ["ex%d" % h, "df%d%d" % (h, j)], ["ad%d%d" % (h, j)], [DB[h][j]])
+
+    def run(t, w):
+        n = len(w.rstrip("0123456789"))
+        c, h, p = w[:n - 1], "XY".index(w[n - 1]), [int(z) for z in w[n:]]
+        if c in ("o", "g"):
+            gd(t, int(c == "o"), h, p[0])
+        elif c in ("eo", "eg"):
+            eqc(t, int(c == "eo"), h, p[0], p[1])
+        elif c == "ct":
+            count(h, p[0], p[1] == 1, p[1] == 2)
+        elif c in ("ch", "cl", "xg", "da"):
+            {"ch": chain, "cl": claim, "xg": xg, "da": tail_abs}[c](t, h, p[0])
+        elif c == "r":
+            reply(t, h)
+        elif c == "l":
+            lists(t + 1, h)
+        elif c == "f":
+            fall(p[0])
+        elif c == "st":
+            tail_store(h)
+        else:
+            {"pre": pre, "po": post, "ab": absd, "sg": sgn, "nr": near, "pu": put, "te": tail_exp, "ta": tail_add}[c](h, *p)
+
+    X, Y = 0, 1
+    for t in range(1, RO + 1):
+        last = t == RO
+        wl = (t - 1) * 96
+        WL = ["WL%d0" % t, "WL%d1" % t]
+        act(T.g1[:, 256:512], T.Rt[:].indirect(T.WL[:, wl + 80:wl + 96]), AF.Identity, r=RT + WL, w=["g11"])
+        for h in range(2):
+            act(T.Rw[:, hs(h, 512)], T.Rt[:].indirect(T.WL[:, wl + 32 * h:wl + 32 * h + 32]), AF.Identity, r=RT + WL, w=["Rw%d" % h])
+        cp(T.g1[:, 0:256], T.Rt[:].indirect(T.WL[:, wl + 64:wl + 80]), RT + WL, ["g10"])
+        for h in range(2):
+            offsets(t, h)
+        if t == 1:
+            order()
+        if t > 2:
+            ystore(t - 2)
+        act(T.Rwg[:], T.Rt[:].indirect(T.Wg[:, (t - 1) * 64:t * 64]), AF.Identity, r=RT + ["Wg%da" % t, "Wg%db" % t], w=["Rwg"])
+        act(T.rr[:], T.Rw[:, 384:640], AF.Relu, bias=float(-(SH + V - 2)), r=["Rw0", "Rw1"], w=["rr"])
+        mm(ps(NB, 0, 256), T.If[:], T.Rw[:, 384:640], True, False, ["If", "Rw0", "Rw1"], ["n7"], NB)
+        mm(ps(NB, 0, 256), T.Iv[:], T.rr[:], False, True, ["Iv", "rr"], ["n7"], NB)
+        if t > 1:
+            expo(X)
+        act(T.n17[:], ps(NB, 0, 256), AF.Identity, bias=1.0, r=["n7"], w=["n17"], banks=[NB])
+        if t > 1:
+            expo(Y)
+            fold(t - 1)
+        for w in (SEQL if last else SEQ).split():
+            run(t, w)
+        if last:
+            break
+        for w in SEQ2.split():
+            run(t, w)
+    ystore(RO - 1)
+    for w in SEQ3.split():
+        run(RO, w)
+    emit()

@@ -2,60 +2,84 @@ from concourse.bass import DstId, RemoteDMATransfer
 from concourse.mybir import AluOpType as ALU, ActivationFunctionType as AF
 
 V, K, RO, TH, NR = 3840, 256, 5, 11, 9
-SH = 17
-RW = 3880
+C0 = V // 2
+RW = V + 16
+XO = 15
 XW = 16 + 2 * V
-JD = 2
+MW = 272
 B2 = 1.5 * 2.0 ** 25
 BH = 1.5 * 2.0 ** 23
 NCH = 4
+POOL = [0, 1, 2, 3, 4, 5]
+REG = {"sh": (6, 0), "Lg": (6, 0), "Z": (6, 0), "ws": (6, 256), "LT": (6, 256), "val": (6, 256), "NC": (6, 256), "S": (6, 256),
+       "L": (7, 0), "put": (7, 0), "nP": (7, 256)}
+WEAVE = 24
+LONG = ("Ro", "Rg", "xn", "Rt", "do", "dg", "dx", "ad", "ng", "ac", "yt")
+TAG = [""]
 
-HEAD = ("xgX0 xgX1 oX0 oX1 oX2 eoX02 oX3 oY0 eoX21 gX0 gX1 gX2 egX02 gX3 egX21 egX31 rX xgY0 xgY1 preX0 preX1 preX2 preX3 "
-        "gY0 gY1 gY2 egY02 preY0 gY3 egY21 egY31 rY eoX31 oY1 chX0 eoY01 chX1 preY1 eoY11 chX2 poX0 poX1 poX2 poX3 ")
-SEQ = HEAD + "abX0 abX1 abX2 sgX02 abX3 sgX22 oY2 oY3 eoY21 eoY31"
-SEQL = HEAD + "abX0 abX1 abX3 abX2 oY2 oY3 eoY21 eoY31"
-SEQ2 = ("lX clX0 chY0 clX1 clX4 chY1 preY2 preY3 clX2 clX3 chY2 poY2 poY0 poY3 poY1 ctX01 ctX10 ctX20 ctX32 abY2 abY3 sgY2 sgY3 "
-        "lY fX0 clY4 fX1 nrY0 ctY01 clY0 fX2 nrY1 clY1 clX5 clY2 clX6 clY3 ctY10 ctY20 ctY32 abY0 abY1 "
-        "puX7 puX6 puX5 puX4 puX3 puX2 puX1 puX0 clY5 clY6 puY7 puY6 puY5 puY4 puY3 puY2 puY1 puY0")
-SEQ3 = ("teX0 teX1 chY0 chY1 preY2 preY3 taX0 chY2 poY3 poY0 poY1 poY2 teX2 taX1 teX3 daY3 abY0 abY1 taX2 taX3 stX "
-        "teY0 abY2 teY3 taY0 teY1 taY3 teY2 taY1 taY2 stY")
+HEAD = ""
+SEQ = ("ch2v ol2 np2 go3a -ex004 os Po122 go2v re Do12 cg2a gg3a Po102 Do10 Pg102 ys-- to12 gg2v Dg10 Pg122 hg0a go0a to10 Dg12 Pg002 "
+       "No12 No10 tg10 Ng10 tg12 Ng12 go1v Dg00 rp1v Po002 -fo Pg022 tg00 Dg02 Do00 lc1a Po022 tg02 Do02 Ng02 Ng00 hx1a to00 No00 Px122 "
+       "rp0a to02 c01 No02 c11 Px102 lc0v c21 hx0a c00 c10 c31 c20 c30 fl xz1a Dx10 zr2a Dx12 od2a tx10 Px002 xz0v Dx00 k12 ab12 Px022 "
+       "sg122 tx00 ab10 ex104 Dx02 Nx00 tx02 ab02 Nx12 Nx10 k02 Nx02 k22 tw k32 ab00 pu1 pu0")
+SEQL = ("ch2v np2 ol2 -ex004 os go1a go3v cg2a go2v Po102 Do10 Pg122 gg2v Po122 Do12 to10 gg3a Dg12 to12 Pg102 Dg10 Pg002 tg12 Ng12 -fo "
+        "hg0a Dg00 tg10 Ng10 rp1v Pg022 No12 No10 tg00 Dg02 Po022 go0a Do02 lc1v tg02 c01 c11 hx1a Ng00 c21 xz1v Px102 Ng02 rp0v hx0a "
+        "Po002 Do00 Dx10 to02 Px122 Dx12 ab10 No02 to00 No00 Px001 Px031 lc0v ab12 c00 c10 Px021 c20 ex122 Px011 xz0v Dx00 ex102 ab00 "
+        "Dx02 Dx03 Dx01 te00 ab01 ts12 ts10 da02 da03 ts11 te02 te01 te03 ts13 st1a ys-- ta01")
+SEQ = ("ch2v ol2 np2 go3a -ex004 os cg2a go2v go0v -fo Po122 Do12 Po102 Do10 gg3a to12 Pg122 hg0a Pg102 gg2v No12 to10 Dg10 Dg12 No10 "
+       "Pg002 tg10 go1a Po002 Dg00 lc1v Ng10 tg12 Ng12 Pg022 tg00 Dg02 rp1v Po022 tg02 Do00 Ng00 to00 Ng02 hx1a rp0a Do02 to02 hx0a Px102 "
+       "No00 c01 c11 No02 Px122 lc0v c21 c00 xz1a Dx12 c10 Dx10 c31 c20 Px002 c30 xz0v Dx00 ab12 sg122 Px022 tx10 tx00 Nx10 ab10 Dx02 "
+       "zr2a Nx00 tx02 Nx12 Nx02 od2a fl k02 ex104 ys-- k22 ab00 k12 ab02 k32 pu1 pu0 tw")
+SEQL = ("ch2v Po102 ol2 Po122 go2a -ex004 np2 os -fo cg2a go3v Do12 to12 Do10 Pg102 gg3a Pg122 gg2v Dg10 Dg12 to10 No12 tg10 hg0a tg12 "
+        "Pg022 go0v Ng10 Po002 Pg002 go1a Dg02 tg02 Ng12 rp1a hx1a Dg00 Do00 hx0a No10 Po022 Do02 tg00 lc1v Ng02 Ng00 to00 rp0v c01 c11 "
+        "c21 Px102 xz1v Dx10 Px122 ab10 ex102 No00 to02 No02 Dx12 ab12 ex122 lc0v c00 Px021 c10 Px031 c20 Px011 Px001 ys-- xz0v Dx00 ab00 Dx03 "
+        "Dx02 Dx01 te00 da02 da03 ts13 ab01 ts12 te01 ts11 te03 te02 ys- ts10 st1a ta01")
+SEQ = ("ch2v ol2 go3a Po102 -ex004 Po122 os -fo Po002 go2v cg2a Do12 np2 to12 Do10 to10 gg3a gg2v hg0a Pg122 Pg102 Dg12 No12 Dg10 tg12 No10 "
+       "tg10 Ng12 go1v Pg002 Dg00 Ng10 Pg022 go0a Dg02 Do00 tg00 rp1a Po022 lc1a Ng00 hx1a tg02 to00 Ng02 Do02 rp0a c01 Px122 c11 No00 "
+       "Px102 to02 c21 xz1v hx0a No02 lc0a Dx12 c00 Dx10 c10 ab12 Px002 sg122 tx10 c20 c32 xz0v ab10 od2v zr2a Px022 Nx10 Nx12 k02 Dx02 "
+       "Dx00 k21 k12 tx00 Nx00 k31 pu1 ab02 sg022 Nx02 k20 ab00 fl ex104 k30 tw pu0 ys--")
+SEQ = ("ch2v ol2 np2 go3a -ex004 os -fo cg2a go2v go0v Po122 Do12 Po102 Do10 gg3a to12 Pg122 hg0a Pg102 gg2v No12 to10 Dg10 Dg12 No10 "
+       "Pg002 tg10 go1a Po002 Dg00 lc1v Ng10 tg12 Ng12 Pg022 tg00 Dg02 rp1v Po022 tg02 Do00 Ng00 to00 Ng02 hx1a rp0a Do02 to02 hx0a Px102 "
+       "No00 c01 c11 No02 Px122 lc0v c21 c00 xz1a Dx12 c10 Dx10 c20 Px002 xz0v c32 Dx00 ab12 sg122 Px022 tx10 tx00 Nx10 ab10 Dx02 "
+       "zr1a zr0a Nx00 tx02 Nx12 Nx02 od2a k02 ex104 ys-- k11 k22 ab00 k32 pu1 k10 fl ab02 pu0 tw")
+SEQ1 = ("ch2v Po122 Po102 os re ol2 go2a go3v Po022 Do12 gx1a go0a go1v cg2a Do10 to12 No12 Po002 Do00 to10 No10 np2 gg3a Pg102 gg2v Do02 "
+        "to00 Dg10 Pg122 hg0a Dg12 No00 tg10 Pg022 tg12 Ng10 Ng12 Dg02 Pg002 lc1a rp1a to02 tg02 gx0a Dg00 No02 Ng02 Px002 hx1a tg00 Ng00 "
+        "rp0v c01 c11 Px102 c21 xz1v lc0v Dx10 c00 ab10 c31 c10 c20 c30 Px122 Dx12 xz0v Dx00 zr2v k12 sg102 od2a tx12 Px022 Nx10 Dx02 tx02 "
+        "ab00 fl Nx12 sg002 ab12 Nx00 k02 Nx02 ex104 k22 tw k32 pu1 ab02 pu0")
 
 SCRATCH = {
     "recs": ("sbuf", [128, V], "int32"), "Rt": ("sbuf", [128, RW], "float32"), "xe": ("sbuf", [128, XW], "bfloat16"),
-    "w0s": ("sbuf", [128, 16], "int32"),
-    "g1": ("sbuf", [128, 512], "float32"), "tr": ("sbuf", [128, 512], "float32"),
-    "O": ("sbuf", [128, RO * 256], "uint16"), "Oin": ("sbuf", [128, RO * 256], "uint16"), "Og": ("sbuf", [128, RO * 256], "uint16"),
-    "WL": ("sbuf", [128, RO * 96], "uint16"), "Win": ("sbuf", [128, RO * 64], "uint16"), "Wg": ("sbuf", [128, RO * 64], "uint16"),
-    "Rw": ("sbuf", [128, 1024], "float32"), "Rwg": ("sbuf", [128, 1024], "float32"),
-    "do": ("sbuf", [128, 4096], "bfloat16"), "dg": ("sbuf", [128, 4096], "bfloat16"),
-    "xn": ("sbuf", [128, 4096], "bfloat16"), "ad": ("sbuf", [128, 4096], "float32"), "ex": ("sbuf", [128, 4096], "float32"),
-    "nr": ("sbuf", [128, 4096], "bfloat16"),
+    "w0s": ("sbuf", [128, 16], "int32"), "WL": ("sbuf", [128, RO * 16], "uint16"),
+    "O": ("sbuf", [128, 256], "uint16"), "Os": ("sbuf", [128, RO * MW], "uint16"), "Oin": ("sbuf", [128, RO * MW], "uint16"),
+    "ch": ("sbuf", [128, 256], "float16"), "cg": ("sbuf", [128, 256], "float16"), "rr": ("sbuf", [128, 256], "float16"),
+    "Ro": ("sbuf", [128, 4096], "float16"), "Rg": ("sbuf", [128, 4096], "float16"), "xn": ("sbuf", [128, 4096], "bfloat16"),
+    "do": ("sbuf", [128, 4096], "bfloat16"), "dg": ("sbuf", [128, 4096], "bfloat16"), "dx": ("sbuf", [128, 4096], "bfloat16"),
+    "ad": ("sbuf", [128, 4096], "float32"), "ex": ("sbuf", [128, 32, 256], "float32"),
     "rep": ("sbuf", [128, RO * 256], "bfloat16"), "repin": ("sbuf", [128, RO * 256], "bfloat16"),
-    "rr": ("sbuf", [128, 256], "bfloat16"), "n17": ("sbuf", [128, 256], "float32"), "ok": ("sbuf", [128, 256], "bfloat16"),
-    "tm": ("sbuf", [128, 256], "float32"), "sc": ("sbuf", [128, 256], "float32"), "sB": ("sbuf", [128, 256], "float32"),
-    "eq": ("sbuf", [128, 256], "float32"), "sc2": ("sbuf", [128, 256], "float32"), "Ed": ("sbuf", [128, 256], "float32"),
+    "Ls": ("sbuf", [128, 256], "bfloat16"), "fT": ("sbuf", [128, 256], "bfloat16"),
+    "ok": ("sbuf", [128, 256], "bfloat16"), "fs": ("sbuf", [128, 256], "bfloat16"), "tm": ("sbuf", [128, 256], "float16"),
+    "sc": ("sbuf", [128, 256], "float32"), "zr": ("sbuf", [128, 256], "float32"), "eq": ("sbuf", [128, 256], "float32"),
+    "sc2": ("sbuf", [128, 256], "float32"), "old": ("sbuf", [128, 256], "float32"), "Ed": ("sbuf", [128, 256], "float32"),
     "pr": ("sbuf", [128, 256], "float32"), "xz": ("sbuf", [128, 256], "bfloat16"),
     "mm": ("sbuf", [128, 16], "float32"), "mu": ("sbuf", [128, 16], "uint16"), "hh": ("sbuf", [128, 16], "float32"),
     "zz": ("sbuf", [128, 16], "float32"), "ee": ("sbuf", [128, 16], "float32"), "F0": ("sbuf", [128, 16], "float32"),
     "F": ("sbuf", [128, 16], "float32"), "vv": ("sbuf", [128, 16], "float32"), "tg": ("sbuf", [128, 32], "uint16"),
-    "acc": ("sbuf", [128, 256], "float32"),
-    "fl": ("sbuf", [128, (RO - 1) * 256], "float32"), "yl": ("sbuf", [128, (RO - 1) * 256], "float32"),
-    "pi": ("sbuf", [128, 8], "int32"), "pa": ("sbuf", [128, 8], "int32"), "pb": ("sbuf", [128, 4], "int32"),
-    "pos": ("sbuf", [128, 8], "float32"), "pbf": ("sbuf", [128, 4], "float32"), "lin": ("sbuf", [128, 8], "float32"),
-    "col": ("sbuf", [128, 8], "float32"),
-    "c16": ("sbuf", [128, 16], "float32"), "c3": ("sbuf", [128, 8], "float32"),
-    "ck": ("sbuf", [128, 144], "bfloat16"), "q": ("sbuf", [128, 256], "bfloat16"), "q16": ("sbuf", [128, 128], "bfloat16"),
-    "L3": ("sbuf", [128, 8], "uint16"), "LL": ("sbuf", [128, 6], "uint16"), "LD": ("sbuf", [128, 8], "uint16"),
-    "band": ("sbuf", [128, 256], "bfloat16"), "I": ("sbuf", [128, 128], "bfloat16"), "blk": ("sbuf", [128, 128], "bfloat16"),
-    "In": ("sbuf", [128, 128], "bfloat16"), "I16": ("sbuf", [128, 128], "bfloat16"), "blk2": ("sbuf", [128, 128], "bfloat16"),
-    "Iv": ("sbuf", [128, 128], "bfloat16"), "If": ("sbuf", [128, 128], "float32"), "bn": ("sbuf", [128, 128], "float32"),
-    "bt": ("sbuf", [128, RO * 128], "bfloat16"), "Bt": ("sbuf", [128, RO * 128], "bfloat16"), "Lt": ("sbuf", [128, RO * 128], "bfloat16"),
-    "M1": ("sbuf", [128, 128], "bfloat16"), "M2": ("sbuf", [128, 128], "bfloat16"), "I2": ("sbuf", [128, 128], "bfloat16"),
-    "RS": ("sbuf", [128, 128], "float32"), "RS2": ("sbuf", [128, 128], "float32"),
+    "ng": ("sbuf", [128, 1024], "float32"), "acc": ("sbuf", [128, 1024], "float32"), "yt": ("sbuf", [128, 256], "float32"),
+    "fl": ("sbuf", [128, RO, 256], "float32"), "yl": ("sbuf", [128, RO, 256], "float32"), "y2": ("sbuf", [128, 256], "float32"),
+    "pi": ("sbuf", [128, 8], "int32"), "pa": ("sbuf", [128, 8], "int32"), "pos": ("sbuf", [128, 8], "float32"),
+    "neg": ("sbuf", [128, 8], "float32"), "col": ("sbuf", [128, 8], "float32"), "c16": ("sbuf", [128, 16], "float32"),
+    "ck": ("sbuf", [128, 256], "bfloat16"), "q": ("sbuf", [128, 256], "bfloat16"), "q16": ("sbuf", [128, 128], "bfloat16"),
+    "LD": ("sbuf", [128, 16], "uint16"), "one": ("sbuf", [128, 128], "bfloat16"), "G": ("sbuf", [128, 24], "bfloat16"),
+    "I": ("sbuf", [128, 256], "bfloat16"), "blk": ("sbuf", [128, 128], "bfloat16"), "Ifn": ("sbuf", [128, 256], "float32"),
+    "In": ("sbuf", [128, 128], "bfloat16"), "I32": ("sbuf", [128, 128], "bfloat16"), "IV": ("sbuf", [128, 128], "bfloat16"),
+    "bn": ("sbuf", [128, 128], "bfloat16"), "bV": ("sbuf", [128, 128], "bfloat16"),
+    "bt": ("sbuf", [128, RO * 128], "bfloat16"), "Bt": ("sbuf", [128, RO * 128], "bfloat16"),
+    "M1": ("sbuf", [128, 256], "bfloat16"), "M2": ("sbuf", [128, 256], "bfloat16"),
+    "RS": ("sbuf", [128, 256], "float32"), "RS2": ("sbuf", [128, 256], "float32"),
     "ps": ("psum", [128, 4096], "float32"),
 }
-SEMAPHORES = (["cv", "ca", "cp", "cg", "sent", "lw", "lx0", "lx1", "ys"] + ["lr%d" % i for i in range(NCH)]
-              + ["%s%d" % (n, t) for n in ("aw", "aox", "aoy", "arx", "ary", "rw", "rox", "roy", "af", "ay", "sf") for t in range(1, RO + 1)])
+SEMAPHORES = (["cv", "ca", "cp", "cg", "sent", "lw", "lx0", "lx1", "lx2", "ys"] + ["lr%d" % i for i in range(NCH)]
+              + ["%s%d" % (n, t) for n in ("ao", "ar0", "ar1", "ar2", "af", "ay", "sf") for t in range(1, RO + 1)])
 
 
 def helpers(T, topo):
@@ -75,6 +99,10 @@ def mask_of(engs):
     return m
 
 
+def rows_folded(t):
+    return 1
+
+
 def rank_program(g, core, T, topo):
     hp = helpers(T, topo)
     rank = T.rank_of(core)
@@ -92,8 +120,8 @@ def helper_program(g, core, c, T, topo):
     nf = len(topo.engines(c, core)[1::2])
     for t in range(1, RO):
         g.wait_ge(T.sem["af%d" % t], nf)
-        s = slice((t - 1) * 256, t * 256)
-        g.remote_dma(T.yl[:, s], T.fl[:, s], T.sem["ay%d" % t], T.sem.sent, pid, rid, mask_of(en))
+        s = slice(t - 1, t - 1 + rows_folded(t))
+        g.remote_dma(T.yl[:, s, :], T.fl[:, s, :], T.sem["ay%d" % t], T.sem.sent, pid, rid, mask_of(en))
     g.wait_ge(T.sem.sent, len(en) * (RO - 1))
 
 
@@ -124,9 +152,34 @@ def group_program(g, core, rank, helper, T, topo):
         for x in w:
             lastw[x] = me
             readers[x] = []
-        ops.append({"q": q, "who": who, "fn": fn, "deps": deps, "ext": list(ext), "tok": tok, "inc": inc})
+        ops.append({"q": q, "who": who, "fn": fn, "deps": deps, "ext": list(ext), "tok": tok, "inc": inc, "tag": TAG[0],
+                    "short": not any(x[:2] in LONG and x != "Rt" for x in w)})
+
+    def weave():
+        order, line_, done, seen = [i for i, o in enumerate(ops) if o["who"] == "v"], [], set(), {}
+        while order:
+            pick = order[0]
+            if line_ and line_[-1] in ops[pick]["deps"]:
+                for j in order[1:WEAVE]:
+                    o = ops[j]
+                    if o["short"] and not o["ext"] and all(d in done and d != line_[-1] if ops[d]["who"] == "v" else d <= seen.get(ops[d]["who"], -1)
+                                                           for d in o["deps"]):
+                        pick = j
+                        break
+            order.remove(pick)
+            line_.append(pick)
+            done.add(pick)
+            for d in ops[pick]["deps"]:
+                seen[ops[d]["who"]] = max(seen.get(ops[d]["who"], -1), d)
+        place = dict(zip(line_, sorted(line_)))
+        new = [None] * len(ops)
+        for i, o in enumerate(ops):
+            o["deps"] = set(place.get(d, d) for d in o["deps"])
+            new[place.get(i, i)] = o
+        ops[:] = new
 
     def emit():
+        weave()
         need = set()
         for o in ops:
             top = {}
@@ -149,6 +202,7 @@ def group_program(g, core, rank, helper, T, topo):
                 if seen.get((o["q"], s), 0) < want[s]:
                     Q[o["q"]].wait_ge(T.sem[s], want[s])
                     seen[(o["q"], s)] = want[s]
+            TAG[0] = o["tag"]
             ins = o["fn"]()
             if o["inc"]:
                 ins.then_inc(T.sem[o["tok"][0]], o["inc"])
@@ -169,20 +223,35 @@ def group_program(g, core, rank, helper, T, topo):
     def tt(out, in0, in1, o, r=(), w=(), banks=()):
         op("v", lambda: v.tensor_tensor(out, in0, in1, o), r, w, banks)
 
-    def cp(out, in_, r=(), w=(), banks=()):
-        op("v", lambda: v.tensor_copy(out, in_), r, w, banks)
-
     def scan(out, d0, d1, o1, r, w, banks=()):
         op("v", lambda: v.tensor_tensor_scan(out, d0, d1, 0.0, ALU.mult, o1), r, w, banks)
 
     def act(out, in_, f, bias=0.0, scale=1.0, r=(), w=(), banks=()):
         op("a", lambda: a.activation(out, in_, f, bias=bias, scale=scale), r, w, banks)
 
+    def copy(e, out, in_, r, w, banks=(), ext=()):
+        if e == "v":
+            op("v", lambda: v.tensor_copy(out, in_), r, w, banks, ext)
+        else:
+            op("a", lambda: a.activation(out, in_, AF.Identity), r, w, banks, ext)
+
+    def line(e, out, in_, scale, bias, r, w, banks=()):
+        if e == "v":
+            ts(out, in_, scale, ALU.mult, bias, ALU.add, r, w, banks)
+        else:
+            act(out, in_, AF.Identity, bias, scale, r, w, banks)
+
     def mm(out, lhsT, rhs, start, stop, r, w, bank, ext=()):
         op("p", lambda: pe.matmul(out, lhsT, rhs, start, stop), r, w, [bank], ext)
 
     def dma(q, out, in_, sem, n, r=(), w=(), ext=()):
         op(q, lambda: Q[q].dma_start(out, in_), r, w, (), ext, tok=(sem, n), inc=16)
+
+    def iota(out, pat, base, cm, name):
+        op("g", lambda: g.iota(out, pat, base, cm, allow_small_or_imprecise_dtypes=True), (), [name])
+
+    def select(out, in_, pat, cmp, fill, base, cm, r, w):
+        op("g", lambda: g.affine_select(out, in_, pat, cmp, fill, base, cm), r, w)
 
     nsent = [0]
 
@@ -191,9 +260,6 @@ def group_program(g, core, rank, helper, T, topo):
         en = topo.engines(core, dst)[0::2]
         nsent[0] += len(en)
         op("g", lambda: g.remote_dma(out, in_, T.sem[sem], T.sem.sent, pid, rid, mask_of(en)), r, (), tok=("sent", nsent[0]))
-
-    def ps(b, lo=0, hi=512):
-        return T.ps[:, b * 512 + lo:b * 512 + hi]
 
     def s256(t):
         return slice((t - 1) * 256, t * 256)
@@ -210,318 +276,341 @@ def group_program(g, core, rank, helper, T, topo):
     def narr(src):
         return len(topo.engines(src, core)[0::2])
 
-    def turn(out, in_, lo, hi, t, arr, sem, name):
-        s = 16 * (t % 8)
-        dma("s", out[s:128, lo:hi], in_[0:128 - s, lo:hi], sem, 32, (), [name + "a"], [(arr, narr(asker(t)))])
-        dma("s", out[0:s, lo:hi], in_[128 - s:128, lo:hi], sem, 32, (), [name + "b"])
+    def part(h, n=128, base=0):
+        return slice(base, base + 2 * n) if h == 2 else hs(h, n, base)
+
+    def halves(h):
+        return (0, 1) if h == 2 else (h,)
+
+    def nm(h, *names):
+        return ["#%d%d%d" % (REG[x] + (i,)) if x in REG else "%s%d" % (x, i) for x in names for i in halves(h)]
+
+    def reg(x, h, n=128):
+        s = part(h, 128, 512 * REG[x][0] + REG[x][1])
+        return T.ps[:, s.start:s.start + n * len(halves(h))]
+
+    def bk(*x):
+        return [REG[i][0] for i in x]
+
+    def turn(m, t):
+        s = (-16 * t) % 128
+        return m[:, s:s + 128]
+
+    Id = T.I[:, 0:128]
 
     cw = V // NCH
-    dma("s", T.w0s[:], T.w0[:], "lw", 16, w=["w0s"])
     for i in range(NCH):
-        dma("s" if i % 2 == 0 else "a", T.recs[:, i * cw:(i + 1) * cw], T.rec[:, i * cw:(i + 1) * cw], "lr%d" % i, 16, w=["recs%d" % i])
-
-    def iota(out, pat, base, cm, name, flag=True):
-        if flag:
-            op("g", lambda: g.iota(out, pat, base, cm, allow_small_or_imprecise_dtypes=True), (), [name])
-        else:
-            op("g", lambda: g.iota(out, pat, base, cm), (), [name])
-    iota(T.pi[:], [[-1, 8]], 16, 1, "pi", False)
-    iota(T.c16[:], [[1, 16]], 0, 0, "c16")
-    iota(T.c3[:], [[2, 8]], 16, 0, "c3")
-    iota(T.q[:], [[0, 2], [1, 128]], 0, 0, "q")
+        if i == 1:
+            dma("a", T.w0s[:], T.w0[:], "lw", 16, w=["w0s"])
+        dma("sa"[i % 2], T.recs[:, hs(i, cw)], T.rec[:, hs(i, cw)], "lr%d" % i, 16, w=["recs%d" % i])
+    op("g", lambda: g.iota(T.pi[:], [[-1, 8]], 16, 1), (), ["pi"])
     iota(T.q16[:], [[16, 8], [0, 16]], 0, 0, "q16")
-    iota(T.ck[:], [[0, 9], [1, 16]], 0, 0, "ck")
-    op("v", lambda: v.memset(T.Rt[:, 0:SH], 0.0), (), ["Rta"])
-    op("v", lambda: v.memset(T.Rt[:, SH + V:RW], 0.0), (), ["Rtb"])
-    op("v", lambda: v.memset(T.xe[:, 0:16], 0.0), (), ["xe0"])
-    op("v", lambda: v.memset(T.RS[:], 1.0), (), ["RS"])
-    op("v", lambda: v.memset(T.RS2[:], 1.0), (), ["RS2"])
-    op("v", lambda: v.memset(T.RS[:, 0::16], 0.0), (), ["RS"])
-    op("v", lambda: v.memset(T.RS2[:, 0::16], 0.0), (), ["RS2"])
-    op("v", lambda: v.memset(T.RS2[:, 15::16], 8192.0), (), ["RS2"])
-    RT = ["Rt", "Rta", "Rtb"] + ["Rt%d" % i for i in range(NCH)]
+    iota(T.q[:], [[0, 2], [1, 128]], 0, 0, "q")
+    iota(T.c16[:], [[16, 16]], 15, 0, "c16")
+    iota(T.ck[:], [[0, 16], [1, 16]], 0, 0, "ck")
+    iota(T.Rt[:, V:RW], [[0, RW - V]], 0, 0, "Rtb")
+    iota(T.xe[:, 0:16], [[0, 16]], 0, 0, "xe0")
+    dma("s", T.xe[:, XO:XO + V], T.x[:], "lx0", 16, r=["recs%d" % (NCH - 1)], w=["xe0", "xe1"])
+    dma("s", T.xe[:, XO + V:XO + V + 2], T.x[:, 0:2], "lx1", 16, w=["xe2"])
+    RT = ["Rt", "Rtb"] + ["Rt%d" % i for i in range(NCH)]
     pk, C = T.pos[:, 0:1], T.col
     ts(T.pa[:], T.pi[:], 15, ALU.bitwise_and, r=["pi"], w=["pa"])
-    ts(T.pb[:, 0:1], T.pi[:, 0:1], 16, ALU.bitwise_and, r=["pi"], w=["pb0"])
-    ts(T.pb[:, 2:3], T.pi[:, 0:1], 7, ALU.bitwise_and, r=["pi"], w=["pb2"])
     ts(C[:, 0:1], T.pi[:, 0:1], -16.0, ALU.add, r=["pi"], w=["c0"])
-    cp(T.pos[:], T.pa[:], ["pa"], ["pos"])
-    ts(T.pb[:, 1:2], T.pa[:, 0:1], 1, ALU.logical_shift_right, r=["pa"], w=["pb1"])
-    ts(T.pb[:, 3:4], T.pa[:, 0:1], 3, ALU.logical_shift_right, r=["pa"], w=["pb3"])
-    ts(T.LD[:], T.c16[:, 0:8], 16.0, ALU.mult, 15.0, ALU.add, r=["c16"], w=["LD"])
-    cp(T.pbf[:], T.pb[:], ["pb0", "pb1", "pb2", "pb3"], ["pbf"])
+    copy("v", T.pos[:], T.pa[:], ["pa"], ["pos"])
     tt(C[:, 1:2], C[:, 0:1], pk, ALU.subtract, ["c0", "pos"], ["c1"])
-    ts(T.LL[:, 0:2], T.c16[:, 0:2], 0.0, ALU.mult, T.pbf[:, 2:3], ALU.add, r=["c16", "pbf"], w=["LLa"])
-    ts(T.LL[:, 2:4], T.c16[:, 8:10], 8.0, ALU.min, T.pbf[:, 2:3], ALU.add, r=["c16", "pbf"], w=["LLb"])
-    ts(T.LL[:, 4:6], T.c16[:, 0:2], 8.0, ALU.mult, T.pbf[:, 1:2], ALU.add, r=["c16", "pbf"], w=["LLc"])
-    ts(C[:, 2:3], T.pbf[:, 2:3], 32.0, ALU.mult, T.pbf[:, 3:4], ALU.add, r=["pbf"], w=["c2"])
-    for h in range(2):
-        ts(T.zz[:, hs(h, 8)], T.w0s[:, hs(1 - h, 8)], -1.0, ALU.mult, float(8192 - SH), ALU.add, r=["w0s"], w=["zz%d" % h])
+    ts(T.blk[:], T.q16[:], C[:, 1:2], ALU.is_equal, r=["q16", "c1"], w=["blk"])
+    ts(T.I[:], T.q[:], C[:, 0:1], ALU.is_equal, r=["q", "c0"], w=["I"])
+    copy("v", T.LD[:], T.c16[:], ["c16"], ["LD"])
+    line("v", T.zz[:], T.w0s[:], -1.0, float(2 * V), ["w0s"], ["zz0", "zz1"])
+    act(T.one[:], T.q16[:, 0:128], AF.Exp, scale=0.0, r=["q16"], w=["one"])
+    line("v", C[:, 4:5], pk, 1.0, float(V), ["pos"], ["c4"])
+    line("v", T.neg[:], T.pos[:], -1.0, 1.0, ["pos"], ["neg"])
+
+    def scaled(*xs):
+        for x, src, sc in xs:
+            line("a", T[x][:], T[src][:, 0:T[x].shape[1]], sc, 0.0, [src], [x])
+
+    scaled(("Ifn", "I", -1.0), ("IV", "I", float(2 * V - C0)), ("In", "I", -1.0))
 
     def lists(t, h):
-        o = (t - 1) * 96
-        if h == 0:
-            ts(T.WL[:, o:o + 32], T.zz[:, 0:8].indirect(T.LL[:, 0:2]), -1.0, ALU.mult, 8192.0, ALU.add, r=["zz0", "LLa"], w=["WL%d0" % t])
-        else:
-            ts(T.WL[:, o + 32:o + 96], T.zz[:].indirect(T.LL[:, 2:6]), -1.0, ALU.mult, 8192.0, ALU.add,
-               r=["zz0", "zz1", "LLb", "LLc"], w=["WL%d1" % t])
-            send(guest(t), T.Win[:, (t - 1) * 64:t * 64], T.WL[:, o:o + 64], "aw%d" % t, ["WL%d0" % t, "WL%d1" % t])
-            turn(T.Wg, T.Win, (t - 1) * 64, t * 64, t, "aw%d" % t, "rw%d" % t, "Wg%d" % t)
+        line("v", T.WL[:, part(h, 8, 16 * (t - 1))], T.zz[:, part(h, 8)], -1.0, float(2 * V), nm(h, "zz"), nm(h, "WL%d" % t))
 
-    def fall(i):
-        if i == 0:
-            ts(T.ee[:], T.zz[:], float(8192 - SH - V + 1), ALU.is_equal, float(V), ALU.mult, r=["zz0", "zz1"], w=["ee"])
-        elif i == 1:
-            tt(T.F0[:], T.ee[:], T.zz[:], ALU.add, ["ee", "zz0", "zz1"], ["F0"])
-        else:
-            ts(T.F[:], T.F0[:], float(-V - 1), ALU.add, r=["F0"], w=["F"])
+    def turned(t):
+        mm(reg("ws", 0, 16), turn(T.Ifn, t), T.zz[:], True, False, ["Ifn"] + nm(2, "zz"), nm(0, "ws"), *bk("ws"))
+        mm(reg("ws", 0, 16), T.IV[:], T.one[:, 0:16], False, True, ["IV", "one"], nm(0, "ws"), *bk("ws"))
 
-    lists(1, 0)
-    lists(1, 1)
-    tt(C[:, 3:4], C[:, 2:3], T.pbf[:, 0:1], ALU.subtract, ["c2", "pbf"], ["c3c"])
-    ts(C[:, 4:5], pk, float(SH + V), ALU.add, r=["pos"], w=["c4"])
-    ts(C[:, 5:6], pk, float(4 * JD), ALU.is_lt, float(NR - (2 * NR - 16)), ALU.mult, r=["pos"], w=["c5"])
-    ts(T.lin[:], T.pos[:], -14.0, ALU.add, 8192.0, ALU.mult, r=["pos"], w=["lin"])
-    fall(0)
-    ts(T.I[:], T.q[:, 0:128], C[:, 0:1], ALU.is_equal, r=["q", "c0"], w=["I"])
-    ts(T.L3[:], T.c3[:], C[:, 3:4], ALU.add, r=["c3", "c3c"], w=["L3"])
-    ts(C[:, 6:7], C[:, 5:6], float(2 * NR - 16), ALU.add, r=["c5"], w=["c6"])
-    fall(1)
-    ts(T.band[:], T.q[:], C[:, 1:2], ALU.is_equal, r=["q", "c1"], w=["band"])
-    ts(T.blk[:], T.q16[:], C[:, 1:2], ALU.is_equal, r=["q16", "c1"], w=["blk"])
-    fall(2)
-    for nm, src, sc in (("In", "I", -1.0), ("I16", "I", 16.0), ("Iv", "I", float(-V)), ("If", "I", 1.0), ("bn", "blk", -1.0)):
-        act(T[nm][:], T[src][:], AF.Identity, scale=sc, r=[src], w=[nm])
-    for t in range(1, RO + 1):
-        act(T.Lt[:, hs(t - 1)], T.blk[:], AF.Identity, scale=T.lin[:, t:t + 1], r=["blk", "lin"], w=["Lt%d" % t])
-    dma("a", T.xe[:, 16:16 + V], T.x[:], "lx0", 16, r=["recs%d" % (NCH - 1)], w=["xe1"])
-    dma("a", T.xe[:, 16 + V:XW], T.x[:], "lx1", 16, w=["xe2"])
-    XE = ["xe0", "xe1", "xe2"]
-    ts(T.M1[:], T.ck[:, 0:128], pk, ALU.not_equal, -16384.0, ALU.mult, r=["ck", "pos"], w=["M1"])
-    ts(T.M2[:], T.ck[:, 0:128], pk, ALU.is_gt, -16384.0, ALU.mult, r=["ck", "pos"], w=["M2"])
-    for t in range(1, RO + 1):
-        ts(T.bt[:, hs(t - 1)], T.ck[:, 16 - t:144 - t], T.pos[:, t:t + 1], ALU.is_ge, -8192.0, ALU.mult, r=["ck", "pos"], w=["bt%d" % t])
+    def fall():
+        ts(T.ee[:], T.zz[:], float(V + 1), ALU.is_equal, float(V), ALU.mult, r=["zz0", "zz1"], w=["ee"])
+        tt(T.F0[:], T.ee[:], T.zz[:], ALU.add, ["ee", "zz0", "zz1"], ["F0"])
+        ts(T.F[:], T.F0[:], float(-V - 1), ALU.add, r=["F0"], w=["F"])
 
-    def order():
-        op("g", lambda: g.affine_select(T.Bt[:], T.bt[:], [[0, RO], [-16, 8], [0, 16]], ALU.is_ge, 0.0, 0, 1),
-           ["bt%d" % t for t in range(1, RO + 1)], ["Bt"])
-        op("g", lambda: g.affine_select(T.Bt[:], T.Bt[:], [[0, RO], [16, 8], [0, 16]], ALU.is_ge, 0.0, 15, -1), ["Bt"], ["Bt"])
-        op("g", lambda: g.affine_select(T.Bt[:], T.Bt[:], [[0, RO], [-1, 128]], ALU.not_equal, 8192.0, 0, 1), ["Bt"], ["Bt"])
+    lists(1, 2)
+    turned(1)
     for i in range(NCH):
-        ts(T.Rt[:, SH + i * cw:SH + (i + 1) * cw], T.recs[:, i * cw:(i + 1) * cw], float(SH), ALU.add, r=["recs%d" % i], w=["Rt%d" % i])
+        line("v", T.Rt[:, hs(i, cw)], T.recs[:, hs(i, cw)], 1.0, float(-C0), ["recs%d" % i], ["Rt%d" % i])
+    for i, sc in enumerate((1.0, 1.0, NR / (2.0 * NR - 16))):
+        line("a", T.G[:, hs(i, 8)], T.blk[:, 0::16], sc, 0.0, ["blk"], ["G"])
+    for t in range(1, RO + 1):
+        act(T.bt[:, hs(t - 1)], T.ck[:, 16 - t:144 - t], AF.Relu, bias=T.neg[:, t:t + 1], r=["ck", "neg"], w=["bt%d" % t])
+    act(T.RS[:], T.ck[:], AF.Sign, r=["ck"], w=["RS"])
 
-    CB, GB, NB, ZB = [4, 5], [6, 7], 3, [4, 2]
-    DB = [[0, 1, 2, 3], [6, 7, 0, 1]]
+    def rest():
+        scaled(("I32", "I", 32.0), ("bn", "blk", -1.0), ("bV", "blk", float(2 * V - C0)))
+        select(T.Bt[:], T.bt[:], [[0, RO], [-16, 8], [0, 16]], ALU.is_ge, 0.0, 0, 1, ["bt%d" % t for t in range(1, RO + 1)], ["Bt"])
+        select(T.Bt[:], T.Bt[:], [[0, RO], [16, 8], [0, 16]], ALU.is_ge, 0.0, 15, -1, ["Bt"], ["Bt"])
+        select(T.Bt[:], T.Bt[:], [[0, RO], [-1, 128]], ALU.not_equal, -1.0, 0, 1, ["Bt"], ["Bt"])
+        select(T.RS2[:], T.RS[:], [[0, 16], [1, 16]], ALU.not_equal, 8192.0, -15, 0, ["RS"], ["RS2"])
+        ts(T.M1[:], T.ck[:], pk, ALU.not_equal, -16384.0, ALU.mult, r=["ck", "pos"], w=["M1"])
+        ts(T.M2[:], T.ck[:], pk, ALU.is_gt, -16384.0, ALU.mult, r=["ck", "pos"], w=["M2"])
+        fall()
+        dma("s", T.xe[:, XO + V + 2:XO + 2 * V], T.x[:, 2:V], "lx2", 16, r=["Os1"], w=["xe3"])
 
-    EB = [[4, 3, 4, 3], DB[1]]
+    def arrived(t):
+        return [("ao%d" % t, narr(asker(t)))]
 
-    def cs(h, c, n=1):
-        return slice(2048 * h + 512 * c, 2048 * h + 512 * (c + n))
+    def names(t, h, e):
+        copy(e, T.ch[:, part(h)], T.Rt[:].indirect(T.WL[:, part(h, 8, 16 * (t - 1))]), RT + nm(h, "WL%d" % t), nm(h, "ch"))
+        mm(reg("sh", h), turn(T.I, t), T.ch[:, part(h)], True, True, ["I"] + nm(h, "ch"), nm(h, "sh"), *bk("sh"))
 
-    def gd(t, own, h, c):
-        o = (t - 1) * 256 + 128 * h + 32 * c
-        rd = ["O%d%d" % (t, h), "Rw%d" % h] if own else ["Og%d%da" % (t, h), "Og%d%db" % (t, h), "Rwg"]
-        tt((T.do if own else T.dg)[:, cs(h, c)], T.Rt[:].indirect((T.O if own else T.Og)[:, o:o + 32]),
-           (T.Rw if own else T.Rwg)[:, hs(h, 512)], ALU.subtract, RT + rd, ["d%d%d%d" % (own, h, c)])
+    def ask(t):
+        s = hs(t - 1, MW)
+        ts(T.Os[:, s], reg("sh", 0, MW), float(C0), ALU.add, r=nm(2, "sh") + nm(0, "ws"), w=["Os%d" % t], banks=bk("sh"))
+        send(guest(t), T.Oin[:, s], T.Os[:, s], "ao%d" % t, ["Os%d" % t])
 
-    def eqc(t, own, h, c, n):
-        d = T.do if own else T.dg
-        nm = ["d%d%d%d" % (own, h, c + i) for i in range(n)]
-        ts(d[:, cs(h, c, n)], d[:, cs(h, c, n)], B2, ALU.add, B2, ALU.is_equal, r=nm, w=nm)
-        b = CB[h] if own else GB[h]
-        for k in range(4 * c, 4 * (c + n)):
-            s = ((0 if own else 16 * t) - k) % 128
-            if own and k == 15:
-                mm(ps(b, 0, 128), T.I16[:], T.repin[:, hs(h, 128, (t - 1) * 256)], False, False, ["I16"], ["L1%d" % h], b,
-                   [("ar%s%d" % ("xy"[h], t), narr(guest(t)))])
-            mm(ps(b, 0, 128), T.band[:, s:s + 128], d[:, hs(k, 128, 2048 * h)], k == 0, k == 15,
-               [nm[k // 4 - c], "band"], ["L%d%d" % (own, h)], b)
+    def after(h):
+        ts(T.rr[:, part(h)], T.ch[:, part(h)], float(C0 - 1), ALU.is_ge, float(-V), ALU.mult, r=nm(h, "ch"), w=nm(h, "rr"))
+        mm(reg("nP", h), Id, T.ch[:, part(h)], True, False, ["I"] + nm(h, "ch"), nm(h, "nP"), *bk("nP"))
+        for x in halves(h):
+            mm(reg("nP", x), Id, T.one[:], False, False, ["I", "one"], nm(h, "nP"), *bk("nP"))
+        mm(reg("nP", h), Id, T.rr[:, part(h)], False, True, ["I"] + nm(h, "rr"), nm(h, "nP"), *bk("nP"))
 
-    def reply(t, h):
-        s = hs(h, 128, (t - 1) * 256)
-        act(T.rep[:, s], ps(GB[h], 0, 128), AF.Sign, bias=0.5 - TH, r=["L0%d" % h], w=["rep%d%d" % (t, h)], banks=[GB[h]])
-        send(asker(t), T.repin[:, s], T.rep[:, s], "ar%s%d" % ("xy"[h], t), ["rep%d%d" % (t, h)])
+    def big(t, p, qu, n, e):
+        s, w = hs(0, 1024 * n, 1024 * qu), ["%s%d" % ({"o": "Ro", "g": "Rg", "x": "xn"}[p], qu + i) for i in range(n)]
+        if p == "o":
+            copy(e, T.Ro[:, s], T.Rt[:].indirect(T.O[:, hs(0, 64 * n, 64 * qu)]), RT + ["O%d" % (qu // 2)], w)
+        elif p == "g":
+            copy(e, T.Rg[:, s], T.Rt[:].indirect(T.Oin[:, hs(0, 64 * n, (t - 1) * MW + 64 * qu)]), RT, w, (), arrived(t))
+        else:
+            copy(e, T.xn[:, s], T.xe[:, 16:16 + V].indirect(T.O[:, hs(0, 64 * n, 64 * qu)]), ["xe1", "xe2", "O%d" % (qu // 2)], w)
 
-    def xg(t, h, c):
-        o = (t - 1) * 256 + 128 * h + 64 * c
-        act(T.xn[:, cs(h, 2 * c, 2)], T.xe[:].indirect(T.O[:, o:o + 64]), AF.Identity, r=XE + ["O%d%d" % (t, h)], w=["xn%d%d" % (h, c)])
+    free, bank, due = set(POOL), {}, {}
 
-    def pre(h, j):
-        mm(ps(DB[h][j]), T.I[:], T.xn[:, cs(h, j)], True, False, ["I", "xn%d%d" % (h, j // 2)], ["df%d%d" % (h, j)], DB[h][j])
+    def piece(u):
+        return T.ps[:, 512 * bank[u][0]:512 * (bank[u][-1] + 1)], ["pb%d" % b for b in bank[u]], bank[u]
 
-    def post(h, j):
-        for i in range(4):
-            mm(ps(DB[h][j], 128 * i, 128 * i + 128), T.In[:], T.xz[:, hs(h)], False, i == 3, ["In", "xz%d" % h], ["df%d%d" % (h, j)], DB[h][j])
+    def cols(h, j, n=1):
+        return hs(0, 512 * n, 512 * (4 * h + j))
+
+    def sub(x, h, j, n):
+        return ["%s%d%d" % (x, h, j + i) for i in range(n)]
+
+    def diff(u, n=0):
+        if n:
+            b = min(b for b in free if free >= set(range(b, b + n)))
+            bank[u] = list(range(b, b + n))
+            free.difference_update(bank[u])
+        p, h, j = u
+        wide, small = {"o": ("Ro", "ch"), "g": ("Rg", "cg"), "x": ("xn", "xz")}[p]
+        for i in range(4 * len(bank[u])):
+            b = bank[u][i // 4]
+            if (p == "x") == (n > 0):
+                l, r, rd = Id, T[wide][:, 2048 * h + 4 * j + i:2048 * (h + 1):16], ["%s%d" % (wide, 2 * h), "%s%d" % (wide, 2 * h + 1)]
+            else:
+                l, r, rd = T.In[:], T[small][:, hs(h)], nm(h, small)
+            mm(T.ps[:, hs(i % 4, 128, 512 * b)], l, r, n > 0 and i % 4 == 0, n == 0 and i % 4 == 3, ["I", "In"] + rd, ["pb%d" % b], b)
+
+    def test(t, p, h, j):
+        d, rd, bs = piece((p, h, j))
+        c = BH if p == "x" else B2
+        ts(T["d" + p][:, cols(h, j, len(bs))], d, c, ALU.add, c, ALU.is_equal, r=rd, w=sub("d" + p, h, j, len(bs)), banks=bs)
+        due[p, h, j] = (len(bs), t % 8 if p == "g" else 0)
+
+    def sgn(h, j, n):
+        act(T.dx[:, cols(h, j, n)], T.ad[:, cols(h, j, n)], AF.Sign, bias=0.5 + 2.0 ** -21, scale=-1.0, r=sub("ad", h, j, n), w=sub("dx", h, j, n))
+        due["x", h, j] = (n, 16)
+
+    def count(p, h, j):
+        x = {"o": "LT", "g": "Lg", "x": "NC"}[p]
+        (n, s), o = due.pop((p, h, j)), 512 * REG[x][0] + REG[x][1] + 128 * h
+        for k in range(4 * j, 4 * (j + n)):
+            mm(T.ps[:, o + k:o + 128:16], T["d" + p][:, hs(k, 128, 2048 * h)], T.G[:, s:s + 8], True, True,
+               ["d%s%d%d" % (p, h, k // 4), "G"], nm(h, x), *bk(x))
+
+    def likes(h, e):
+        copy(e, T.Ls[:, part(h)], reg("LT", h), nm(h, "LT"), nm(h, "Ls"), bk("LT"))
+
+    answer = {}
+
+    def reply(t, h, e):
+        s = part(h, 128, (t - 1) * 256)
+        if e == "v":
+            ts(T.rep[:, s], reg("Lg", h), float(TH), ALU.is_ge, r=nm(h, "Lg"), w=nm(h, "rep%d" % t), banks=bk("Lg"))
+        else:
+            act(T.rep[:, s], reg("Lg", h), AF.Sign, bias=0.5 - TH, r=nm(h, "Lg"), w=nm(h, "rep%d" % t), banks=bk("Lg"))
+        send(asker(t), T.repin[:, s], T.rep[:, s], "ar%d%d" % (h, t), nm(h, "rep%d" % t))
+        answer.update({i: h for i in halves(h)})
+
+    def chain(t, h, i):
+        s, e8 = part(h), part(h, 8)
+        if i == 0:
+            for x in halves(h):
+                mm(reg("L", x), T.Ls[:, hs(x)], Id, True, False, ["I"] + nm(x, "Ls"), nm(x, "L"), *bk("L"))
+                mm(reg("L", x), T.repin[:, hs(x, 128, (t - 1) * 256)], T.I32[:], False, True, ["I32"], nm(x, "L"), *bk("L"),
+                   [("ar%d%d" % (answer[x], t), narr(guest(t)))])
+            ts(T.ok[:, s], reg("L", h), float(32 + TH), ALU.is_ge, r=nm(h, "L"), w=nm(h, "ok"), banks=bk("L"))
+            mm(reg("val", h), T.Bt[:, hs(t - 1)], T.ok[:, s], True, True, ["Bt"] + nm(h, "ok"), nm(h, "val"), *bk("val"))
+        if i == 1:
+            ts(T.fs[:, s], reg("val", h), -1.0, ALU.is_le, r=nm(h, "val"), w=nm(h, "fs"), banks=bk("val"))
+            tt(T.tm[:, s], T.fs[:, s], reg("nP", h), ALU.mult, nm(h, "fs", "nP"), nm(h, "tm"), bk("nP"))
+            for j, (l, r, rd) in enumerate(((Id, T.M1, ["I", "M1"]), (Id, T.M2, ["I", "M2"]), (T.bV[:], T.fs, ["bV"] + nm(h, "fs")),
+                                            (T.bn[:], T.tm, ["bn"] + nm(h, "tm")))):
+                mm(reg("Z", h), l, r[:, s], j == 0, j == 3, rd, nm(h, "Z"), *bk("Z"))
+        if i == 2:
+            scan(T.sc[:, s], T.RS[:, s], reg("Z", h), ALU.max, ["RS"] + nm(h, "Z"), nm(h, "sc"), bk("Z"))
+            tt(T.mm[:, e8], T.sc[:, s.start + 15:s.stop:16], T.F[:, e8], ALU.max, nm(h, "sc") + ["F"], nm(h, "mm"))
+            line("v", T.mu[:, e8], T.mm[:, e8], -1.0, float(2 * V + XO), nm(h, "mm"), nm(h, "mu"))
+        if i == 3:
+            ts(T.hh[:, e8], T.mm[:, e8], float(V), ALU.is_le, float(V), ALU.mult, r=nm(h, "mm"), w=nm(h, "hh"))
+            tt(T.zz[:, e8], T.mm[:, e8], T.hh[:, e8], ALU.add, nm(h, "mm", "hh"), nm(h, "zz"))
+            lists(t + 1, h)
+
+    def state(h, e):
+        copy(e, T.xz[:, part(h)], T.xe[:, 0:XO + 2 * V].indirect(T.mu[:, part(h, 8)]), ["xe0", "xe1", "xe2", "xe3"] + nm(h, "mu"), nm(h, "xz"))
+
+    def older(t, h, e):
+        copy(e, T.old[:, part(h)], T.Rt[:].indirect(T.WL[:, part(h, 8, 16 * t)]), RT + nm(h, "WL%d" % (t + 1)), nm(h, "old"))
+
+    def spread(h, e):
+        line(e, T.zr[:, part(h)], T.sc[:, part(h)].indirect(T.LD[:, 0:8 * len(halves(h))]), 1.0, -16384.0, nm(h, "sc") + ["LD"], nm(h, "zr"))
+
+    def claim(h, i):
+        s, e8 = part(h), part(h, 8)
+        if i == 0:
+            tt(T.Ed[:, s], T.old[:, s], reg("nP", h), ALU.subtract, nm(h, "old", "nP"), nm(h, "Ed"), bk("nP"))
+        if i == 1:
+            tt(T.eq[:, s], T.zr[:, s], reg("Z", h), ALU.is_equal, nm(h, "zr", "Z"), nm(h, "eq"), bk("Z"))
+            scan(T.sc2[:, s], T.RS2[:, s], T.eq[:, s], ALU.add, ["RS2"] + nm(h, "eq"), nm(h, "sc2"))
+            e = slice(s.start + 15, s.stop, 16)
+            tt(T.vv[:, e8], T.sc2[:, e], T.sc[:, e], ALU.subtract, nm(h, "sc2", "sc"), nm(h, "vv"))
+            ts(T.tg[:, 2 * e8.start:2 * e8.stop:2], T.vv[:, e8], float(2 * V), ALU.add, C[:, 4:5], ALU.min, r=nm(h, "vv") + ["c4"], w=nm(h, "tg"))
+        if i == 2:
+            ts(T.fT[:, s], reg("NC", h), float(NR), ALU.is_ge, r=nm(h, "NC"), w=nm(h, "fT"), banks=bk("NC"))
+            for x in halves(h):
+                mm(reg("put", x), T.fT[:, hs(x)], Id, True, True, ["I"] + nm(x, "fT"), nm(x, "put"), *bk("put"))
+        if i == 3:
+            tt(T.pr[:, s], T.Ed[:, s], reg("put", h), ALU.mult, nm(h, "Ed", "put"), nm(h, "pr"), bk("put"))
+
+    def put(h):
+        for b in range(8 * h + 7, 8 * h - 1, -1):
+            tt(T.Rt[:].indirect(T.tg[:, 2 * b:2 * b + 1]), T.old[:, hs(b, 16)], T.pr[:, hs(b, 16)], ALU.subtract, nm(h, "tg", "pr", "old"), ["Rt"])
 
     def absd(h, j):
-        act(T.ad[:, cs(h, j)], ps(DB[h][j]), AF.Abs, r=["df%d%d" % (h, j)], w=["ad%d%d" % (h, j)], banks=[DB[h][j]])
+        d, rd, bs = piece(("x", h, j))
+        act(T.ad[:, cols(h, j, len(bs))], d, AF.Abs, r=rd, w=sub("ad", h, j, len(bs)), banks=bs)
 
-    def count(h, j, first, last):
-        for i in range(4):
-            k = 4 * j + i
-            s = (-k) % 128
-            mm(ps(CB[h], 0, 128), T.band[:, s:s + 128], T.nr[:, hs(k, 128, 2048 * h)], first and i == 0, last and i == 3,
-               ["nr%d%d" % (h, j), "band"], ["NC%d" % h], CB[h])
-
-    def near(h, j):
-        ts(T.nr[:, cs(h, j)], ps(DB[h][j]), BH, ALU.add, BH, ALU.is_equal, r=["df%d%d" % (h, j)], w=["nr%d%d" % (h, j)], banks=[DB[h][j]])
-
-    def sgn(h, j, n=1):
-        act(T.nr[:, cs(h, j, n)], T.ad[:, cs(h, j, n)], AF.Sign, bias=0.5 + 2.0 ** -21, scale=-1.0,
-            r=["ad%d%d" % (h, j + i) for i in range(n)], w=["nr%d%d" % (h, j + i) for i in range(n)])
-
-    def expo(h):
-        act(T.ex[:, hs(h, 2048)], T.ad[:, hs(h, 2048)], AF.Exp, scale=-1.0, r=["ad%d%d" % (h, j) for j in range(4)], w=["ex%d" % h])
+    def expo(t, h, j, n):
+        act(T.ex[:, hs(0, 4 * n, 16 * (t % 2) + 4 * j), hs(h)], T.ad[:, cols(h, j, n)], AF.Exp, scale=-1.0,
+            r=sub("ad", h, j, n), w=sub("ex%d" % (t % 2), h, j, n))
 
     def fold(t):
         rid, pid, _ = topo.addr(helper)
-        en = topo.engines(core, helper)[1::2]
-        n = len(en) // 2
-        trs = [RemoteDMATransfer(dst_ids=[DstId(rid=rid, pnc=pid)], dma_engine_mask=mask_of(en[h * n:(h + 1) * n]),
-                                 remote_sem=T.sem["af%d" % t], srcs=[T.ex[:, hs(k, 128, 2048 * h)] for k in range(16)],
-                                 dsts=[T.fl[:, hs(1 - h, 128, (t - 1) * 256)]], alu_op=1) for h in range(2)]
-        op("g", lambda: g.remote_dma_fused(trs, local_sem=T.sem["sf%d" % t]), ["ex0", "ex1"], (), tok=("sf%d" % t, len(en)))
+        en, n = topo.engines(core, helper)[1::2], rows_folded(t)
+        trs = [RemoteDMATransfer(dst_ids=[DstId(rid=rid, pnc=pid)], dma_engine_mask=mask_of(en), remote_sem=T.sem["af%d" % t],
+                                 srcs=[T.ex[:, hs(k, n, 16 * (t % 2)), :] for k in range(16 // n)], dsts=[T.fl[:, hs(0, n, t - 1), :]],
+                                 alu_op=1)]
+        op("g", lambda: g.remote_dma_fused(trs, local_sem=T.sem["sf%d" % t]), sub("ex%d" % (t % 2), 0, 0, 4) + sub("ex%d" % (t % 2), 1, 0, 4),
+           (), tok=("sf%d" % t, len(en)))
 
     nys = [0]
 
-    def ystore(t):
+    def store(cs, src, r=(), ext=()):
         nys[0] += 16
-        dma("s", T.y[:, s256(t)], T.yl[:, s256(t)], "ys", nys[0], ext=[("ay%d" % t, narr(helper))])
+        dma("s", T.y[:, cs], src, "ys", nys[0], r=r, ext=ext)
 
-    def chain(t, h, i):
-        b, z, H = CB[h], ZB[h], "%d" % h
-        e8 = hs(h, 8)
-        if i == 0:
-            ts(T.ok[:, hs(h)], ps(b, 0, 128), float(16 + TH), ALU.is_ge, r=["L1" + H], w=["ok" + H], banks=[b])
-            mm(ps(b, 128, 256), T.Bt[:, hs(t - 1)], T.ok[:, hs(h)], True, True, ["Bt", "ok" + H], ["val" + H], b)
-        if i == 1:
-            if z == b:
-                tt(T.tm[:, hs(h)], ps(b, 128, 256), T.n17[:, hs(h)], ALU.min, ["val" + H, "n17"], ["tm" + H], [b])
-            mm(ps(z, 256, 384), T.I[:], T.M1[:], True, False, ["I", "M1"], ["Z" + H], z)
-            mm(ps(z, 256, 384), T.I[:], T.M2[:], False, False, ["I", "M2"], ["Z" + H], z)
-            mm(ps(z, 256, 384), T.Lt[:, hs(t - 1)], T.ok[:, hs(h)], False, False, ["Lt%d" % t, "ok" + H], ["Z" + H], z)
-            if z != b:
-                tt(T.tm[:, hs(h)], ps(b, 128, 256), T.n17[:, hs(h)], ALU.min, ["val" + H, "n17"], ["tm" + H], [b])
-            mm(ps(z, 256, 384), T.bn[:], T.tm[:, hs(h)], False, True, ["bn", "tm" + H], ["Z" + H], z)
-        if i == 2:
-            scan(T.sc[:, hs(h)], T.RS[:], ps(z, 256, 384), ALU.max, ["RS", "Z" + H], ["sc" + H], [z])
-            if t < RO:
-                act(T.sB[:, hs(h)], ps(z, 256, 384), AF.Identity, bias=16384.0, r=["Z" + H], w=["sB" + H], banks=[z])
-            tt(T.mm[:, e8], T.sc[:, 128 * h + 15:128 * h + 128:16], T.F[:, e8], ALU.max, ["sc" + H, "F"], ["mm" + H])
-            ts(T.mu[:, e8], T.mm[:, e8], -1.0, ALU.mult, 8191.0, ALU.add, r=["mm" + H], w=["mu" + H])
-            if t < RO:
-                ts(T.hh[:, e8], T.mm[:, e8], float(8192 - SH - V + 1), ALU.is_lt, float(V), ALU.mult, r=["mm" + H], w=["hh" + H])
-            cp(T.xz[:, hs(h)], T.xe[:].indirect(T.mu[:, e8]), XE + ["mu" + H], ["xz" + H])
-            if t < RO:
-                tt(T.zz[:, e8], T.mm[:, e8], T.hh[:, e8], ALU.add, ["mm" + H, "hh" + H], ["zz" + H])
+    def ystore(t):
+        back = [("ay%d" % t, narr(helper))]
+        if rows_folded(t) == 1:
+            store(s256(t), T.yl[:, t - 1, :], ext=back)
+        else:
+            op("v", lambda: v.tensor_tensor(T.y2[:], T.yl[:, t - 1, :], T.yl[:, t, :], ALU.add), (), ["y2"], (), back)
+            store(s256(t), T.y2[:], ["y2"])
 
-    def claim(t, h, i):
-        H, e8, b = "%d" % h, hs(h, 8), CB[h]
-        if i == 0:
-            tt(T.eq[:, hs(h)], T.sc[:, hs(h)].indirect(T.LD[:]), T.sB[:, hs(h)], ALU.is_equal, ["sc" + H, "LD", "sB" + H], ["eq" + H])
-        if i == 1:
-            scan(T.sc2[:, hs(h)], T.RS2[:], T.eq[:, hs(h)], ALU.add, ["RS2", "eq" + H], ["sc2" + H])
-        if i == 2:
-            s = slice(128 * h + 15, 128 * h + 128, 16)
-            tt(T.vv[:, e8], T.sc2[:, s], T.sc[:, s], ALU.subtract, ["sc2" + H, "sc" + H], ["vv" + H])
-        if i == 3:
-            ts(T.tg[:, 16 * h:16 * h + 16:2], T.vv[:, e8], 8192.0, ALU.add, C[:, 4:5], ALU.min, r=["vv" + H, "c4"], w=["tg" + H])
-        if i == 4:
-            o = t * 96 + 32 * h
-            tt(T.Ed[:, hs(h)], T.Rt[:].indirect(T.WL[:, o:o + 8]), T.n17[:, hs(h)], ALU.subtract, RT + ["WL%d%d" % (t + 1, h), "n17"], ["Ed" + H])
-        if i == 5:
-            ts(ps(b, 384, 512), ps(b, 0, 128), C[:, 6:7] if h else float(2 * NR - 16), ALU.is_lt, r=["NC" + H, "c6"], w=["np" + H], banks=[b])
-        if i == 6:
-            tt(T.pr[:, hs(h)], T.Ed[:, hs(h)], ps(b, 384, 512), ALU.mult, ["Ed" + H, "np" + H], ["pr" + H], [b])
+    def tail_abs(h, j):
+        d, rd, bs = piece(("x", h, j))
+        line("v", T.ng[:, 0:512 * len(bs)], d, -1.0, 0.0, rd, ["ng"], bs)
+        tt(T.ad[:, cols(h, j, len(bs))], T.ng[:, 0:512 * len(bs)], d, ALU.max, ["ng"] + rd, sub("ad", h, j, len(bs)), bs)
 
-    def put(h, b):
-        s = hs(8 * h + b, 16)
-        tt(T.Rt[:].indirect(T.tg[:, 16 * h + 2 * b:16 * h + 2 * b + 1]), T.pr[:, s], T.n17[:, s], ALU.add,
-           ["tg%d" % h, "pr%d" % h, "n17"], ["Rt"])
+    added = [0]
+
+    def tail_sum(h, j):
+        for k in range(4 * j, 4 * j + 4):
+            added[0] += 1
+            mm(reg("S", h), T.Ifn[:, 0:128], T.ex[:, 16 * (RO % 2) + k, hs(h)], added[0] == 1, added[0] == 16,
+               ["Ifn", "ex%d%d%d" % (RO % 2, h, j), "tm0"], nm(h, "S"), *bk("S"))
+
+    def tail_store(h, e):
+        line(e, T.yt[:, hs(h)], reg("S", h), -1.0, 0.0, nm(h, "S"), nm(h, "yt"), bk("S"))
+        store(hs(h, 128, (RO - 1) * 256), T.yt[:, hs(h)], nm(h, "yt"))
 
     def tail_exp(h, j):
-        act(ps(EB[h][j]), T.ad[:, cs(h, j)], AF.Exp, scale=-1.0, r=["ad%d%d" % (h, j)],
-            w=["e%d%d" % (h, j)] + ["df%d%d" % (h, i) for i in range(4) if DB[h][i] == EB[h][j]], banks=[EB[h][j]])
+        d, rd, bs = piece(("x", h, j))
+        n = len(bs)
+        acc = T.acc[:, 0:512 * n]
+        if j == 0:
+            act(acc, T.ad[:, cols(h, 0, n)], AF.Exp, scale=-1.0, r=sub("ad", h, 0, n), w=["acc"])
+        else:
+            act(d, T.ad[:, cols(h, j, n)], AF.Exp, scale=-1.0, r=sub("ad", h, j, n), w=rd, banks=bs)
+            tt(acc, acc, d, ALU.add, ["acc"] + rd, ["acc"], bs)
 
-    def tail_add(h, j):
-        s = T.acc[:, hs(1 - h)]
-        for i in range(4):
-            e = ps(EB[h][j], 128 * i, 128 * i + 128)
-            if j == 0 and i == 0:
-                cp(s, e, ["e%d0" % h], ["acc%d" % h], [EB[h][j]])
-            else:
-                tt(s, s, e, ALU.add, ["acc%d" % h, "e%d%d" % (h, j)], ["acc%d" % h], [EB[h][j]])
+    def tail_add(h, n):
+        for m in (512, 256)[2 - n:]:
+            tt(T.acc[:, 0:m], T.acc[:, 0:m], T.acc[:, m:2 * m], ALU.add, ["acc"], ["acc"])
+        tt(T.yt[:, hs(h)], T.acc[:, 0:128], T.acc[:, 128:256], ALU.add, ["acc"], nm(h, "yt"))
+        store(hs(h, 128, (RO - 1) * 256), T.yt[:, hs(h)], nm(h, "yt"))
 
-    def tail_store(h):
-        nys[0] += 16
-        dma("s", T.y[:, hs(1 - h, 128, (RO - 1) * 256)], T.acc[:, hs(1 - h)], "ys", nys[0], r=["acc%d" % h])
-
-    def offsets(t, h):
-        s, n = hs(h, 128, (t - 1) * 256), "%s%d" % ("xy"[h], t)
-        op("v", lambda: v.transpose(T.tr[:, hs(h, 256)], T.g1[:, hs(h, 256)]), ["g1%d" % h], ["tr%d" % h])
-        cp(T.O[:, s], T.tr[:, hs(h, 256)].indirect(T.L3[:]), ["tr%d" % h, "L3"], ["O%d%d" % (t, h)])
-        send(guest(t), T.Oin[:, s], T.O[:, s], "ao" + n, ["O%d%d" % (t, h)])
-        turn(T.Og, T.Oin, s.start, s.stop, t, "ao" + n, "ro" + n, "Og%d%d" % (t, h))
-
-    def tail_abs(t, h, j):
-        s = T.ex[:, cs(h, j)]
-        ts(s, ps(DB[h][j]), -1.0, ALU.mult, r=["df%d%d" % (h, j)], w=["ex%d" % h], banks=[DB[h][j]])
-        tt(T.ad[:, cs(h, j)], s, ps(DB[h][j]), ALU.max, ["ex%d" % h, "df%d%d" % (h, j)], ["ad%d%d" % (h, j)], [DB[h][j]])
+    def unit(w):
+        if w[0] in "PD" or w[:2] in ("to", "tg", "tx"):
+            return (w[1], int(w[2]), int(w[3]))
+        if w[:2] in ("ab", "da", "te"):
+            return ("x", int(w[2]), int(w[3]))
+        return None
 
     def run(t, w):
-        n = len(w.rstrip("0123456789"))
-        c, h, p = w[:n - 1], "XY".index(w[n - 1]), [int(z) for z in w[n:]]
-        if c in ("o", "g"):
-            gd(t, int(c == "o"), h, p[0])
-        elif c in ("eo", "eg"):
-            eqc(t, int(c == "eo"), h, p[0], p[1])
-        elif c == "ct":
-            count(h, p[0], p[1] == 1, p[1] == 2)
-        elif c in ("ch", "cl", "xg", "da"):
-            {"ch": chain, "cl": claim, "xg": xg, "da": tail_abs}[c](t, h, p[0])
-        elif c == "r":
-            reply(t, h)
-        elif c == "l":
-            lists(t + 1, h)
-        elif c == "f":
-            fall(p[0])
-        elif c == "st":
-            tail_store(h)
+        c, p = w[:2], [int(z) if z.isdigit() else z for z in w[2:]]
+        if c[0] in "PD":
+            diff(unit(w), *p[2:])
+        elif c[0] == "N":
+            count(c[1], *p)
+        elif c in ("go", "gg", "gx"):
+            big(t, c[1], p[0], 1, p[1])
+        elif c in ("ho", "hg", "hx"):
+            big(t, c[1], 2 * p[0], 2, p[1])
+        elif c in ("to", "tg", "tx"):
+            test(t, c[1], *p)
+        elif c == "ol":
+            ts(T.O[:, part(*p)], T.ch[:, part(*p)], float(C0), ALU.add, r=nm(*p, "ch"), w=nm(*p, "O"))
+        elif c == "cg":
+            copy(p[1], T.cg[:, part(p[0])], T.Rt[:].indirect(T.Oin[:, part(p[0], 8, (t - 1) * MW + 256)]), RT, nm(p[0], "cg"), (), arrived(t))
+        elif c[0] == "c" and c[1].isdigit():
+            chain(t, p[0], int(c[1]))
+        elif c[0] == "k":
+            claim(p[0], int(c[1]))
+        elif c == "tw":
+            turned(t + 1)
+        elif c == "re":
+            if t == 1:
+                rest()
+        elif c in ("ch", "os", "rp", "od", "ex", "fo", "ys"):
+            {"ch": names, "os": ask, "rp": reply, "od": older, "ex": expo, "fo": fold, "ys": ystore}[c](t, *p)
         else:
-            {"pre": pre, "po": post, "ab": absd, "sg": sgn, "nr": near, "pu": put, "te": tail_exp, "ta": tail_add}[c](h, *p)
+            {"np": after, "zr": spread, "xz": state, "lc": likes, "fl": fall, "ab": absd, "sg": sgn, "pu": put, "da": tail_abs,
+             "ts": tail_sum, "st": tail_store, "te": tail_exp, "ta": tail_add}[c](*p)
 
-    X, Y = 0, 1
-    for t in range(1, RO + 1):
-        last = t == RO
-        wl = (t - 1) * 96
-        WL = ["WL%d0" % t, "WL%d1" % t]
-        act(T.g1[:, 256:512], T.Rt[:].indirect(T.WL[:, wl + 80:wl + 96]), AF.Identity, r=RT + WL, w=["g11"])
-        for h in range(2):
-            act(T.Rw[:, hs(h, 512)], T.Rt[:].indirect(T.WL[:, wl + 32 * h:wl + 32 * h + 32]), AF.Identity, r=RT + WL, w=["Rw%d" % h])
-        cp(T.g1[:, 0:256], T.Rt[:].indirect(T.WL[:, wl + 64:wl + 80]), RT + WL, ["g10"])
-        for h in range(2):
-            offsets(t, h)
-        if t == 1:
-            order()
-        if t > 2:
-            ystore(t - 2)
-        act(T.Rwg[:], T.Rt[:].indirect(T.Wg[:, (t - 1) * 64:t * 64]), AF.Identity, r=RT + ["Wg%da" % t, "Wg%db" % t], w=["Rwg"])
-        act(T.rr[:], T.Rw[:, 384:640], AF.Relu, bias=float(-(SH + V - 2)), r=["Rw0", "Rw1"], w=["rr"])
-        mm(ps(NB, 0, 256), T.If[:], T.Rw[:, 384:640], True, False, ["If", "Rw0", "Rw1"], ["n7"], NB)
-        mm(ps(NB, 0, 256), T.Iv[:], T.rr[:], False, True, ["Iv", "rr"], ["n7"], NB)
-        if t > 1:
-            expo(X)
-        act(T.n17[:], ps(NB, 0, 256), AF.Identity, bias=1.0, r=["n7"], w=["n17"], banks=[NB])
-        if t > 1:
-            expo(Y)
-            fold(t - 1)
-        for w in (SEQL if last else SEQ).split():
-            run(t, w)
-        if last:
-            break
-        for w in SEQ2.split():
-            run(t, w)
-    ystore(RO - 1)
-    for w in SEQ3.split():
-        run(RO, w)
+    seq = [(t - w.count("-"), w.strip("-")) for t in range(1, RO + 1) for w in {1: SEQ1, RO: SEQL}.get(t, SEQ).split() if t > w.count("-")]
+    for i, (t, w) in enumerate(seq):
+        TAG[0] = "%d%s" % (t, w)
+        run(t, w)
+        u = unit(w)
+        if u and (t, u) not in [(s, unit(x)) for s, x in seq[i + 1:i + 150]]:
+            free.update(bank.pop(u))
     emit()

@@ -5,78 +5,59 @@ V, K, RO, TH, NR = 3840, 256, 5, 11, 9
 C0 = V // 2
 RW = V + 16
 XO = 15
-XW = 16 + 2 * V
 MW = 272
 B2 = 1.5 * 2.0 ** 25
 BH = 1.5 * 2.0 ** 23
+BIG = 8192.0
 NCH = 4
 POOL = [0, 1, 2, 3, 4, 5]
-REG = {"sh": (6, 0), "Lg": (6, 0), "Z": (6, 0), "ws": (6, 256), "LT": (6, 256), "val": (6, 256), "NC": (6, 256), "S": (6, 256),
-       "L": (7, 0), "put": (7, 0), "nP": (7, 256)}
-WEAVE = 24
-LONG = ("Ro", "Rg", "xn", "Rt", "do", "dg", "dx", "ad", "ng", "ac", "yt")
+BW = 18
+REG = {"Lg": (0, 128, "A"), "dn": (0, 8 * BW, "AB"), "eq": (0, 128, "A"), "S": (0, 128, "A"), "NC": (128, 128, "B"),
+       "put": (128, 128, "B"), "LT": (272, 8 * BW, "D"), "nP": (272, 128, "D"), "Z": (416, 8, "E"), "tg": (424, 8, "F")}
+CYC, PCYC, GATH, SCAT, FIX, SEM, PLAT, HOP, FOLD = 0.83, 0.42, 1.4, 3.0, {"v": 60, "a": 120, "p": 10}, 100, 150, 2200, 16000
+IDLE = 1.0
+SPAN = [0]
 TAG = [""]
 
-HEAD = ""
-SEQ = ("ch2v ol2 np2 go3a -ex004 os Po122 go2v re Do12 cg2a gg3a Po102 Do10 Pg102 ys-- to12 gg2v Dg10 Pg122 hg0a go0a to10 Dg12 Pg002 "
-       "No12 No10 tg10 Ng10 tg12 Ng12 go1v Dg00 rp1v Po002 -fo Pg022 tg00 Dg02 Do00 lc1a Po022 tg02 Do02 Ng02 Ng00 hx1a to00 No00 Px122 "
-       "rp0a to02 c01 No02 c11 Px102 lc0v c21 hx0a c00 c10 c31 c20 c30 fl xz1a Dx10 zr2a Dx12 od2a tx10 Px002 xz0v Dx00 k12 ab12 Px022 "
-       "sg122 tx00 ab10 ex104 Dx02 Nx00 tx02 ab02 Nx12 Nx10 k02 Nx02 k22 tw k32 ab00 pu1 pu0")
-SEQL = ("ch2v np2 ol2 -ex004 os go1a go3v cg2a go2v Po102 Do10 Pg122 gg2v Po122 Do12 to10 gg3a Dg12 to12 Pg102 Dg10 Pg002 tg12 Ng12 -fo "
-        "hg0a Dg00 tg10 Ng10 rp1v Pg022 No12 No10 tg00 Dg02 Po022 go0a Do02 lc1v tg02 c01 c11 hx1a Ng00 c21 xz1v Px102 Ng02 rp0v hx0a "
-        "Po002 Do00 Dx10 to02 Px122 Dx12 ab10 No02 to00 No00 Px001 Px031 lc0v ab12 c00 c10 Px021 c20 ex122 Px011 xz0v Dx00 ex102 ab00 "
-        "Dx02 Dx03 Dx01 te00 ab01 ts12 ts10 da02 da03 ts11 te02 te01 te03 ts13 st1a ys-- ta01")
-SEQ = ("ch2v ol2 np2 go3a -ex004 os cg2a go2v go0v -fo Po122 Do12 Po102 Do10 gg3a to12 Pg122 hg0a Pg102 gg2v No12 to10 Dg10 Dg12 No10 "
-       "Pg002 tg10 go1a Po002 Dg00 lc1v Ng10 tg12 Ng12 Pg022 tg00 Dg02 rp1v Po022 tg02 Do00 Ng00 to00 Ng02 hx1a rp0a Do02 to02 hx0a Px102 "
-       "No00 c01 c11 No02 Px122 lc0v c21 c00 xz1a Dx12 c10 Dx10 c31 c20 Px002 c30 xz0v Dx00 ab12 sg122 Px022 tx10 tx00 Nx10 ab10 Dx02 "
-       "zr2a Nx00 tx02 Nx12 Nx02 od2a fl k02 ex104 ys-- k22 ab00 k12 ab02 k32 pu1 pu0 tw")
-SEQL = ("ch2v Po102 ol2 Po122 go2a -ex004 np2 os -fo cg2a go3v Do12 to12 Do10 Pg102 gg3a Pg122 gg2v Dg10 Dg12 to10 No12 tg10 hg0a tg12 "
-        "Pg022 go0v Ng10 Po002 Pg002 go1a Dg02 tg02 Ng12 rp1a hx1a Dg00 Do00 hx0a No10 Po022 Do02 tg00 lc1v Ng02 Ng00 to00 rp0v c01 c11 "
-        "c21 Px102 xz1v Dx10 Px122 ab10 ex102 No00 to02 No02 Dx12 ab12 ex122 lc0v c00 Px021 c10 Px031 c20 Px011 Px001 ys-- xz0v Dx00 ab00 Dx03 "
-        "Dx02 Dx01 te00 da02 da03 ts13 ab01 ts12 te01 ts11 te03 te02 ys- ts10 st1a ta01")
-SEQ = ("ch2v ol2 go3a Po102 -ex004 Po122 os -fo Po002 go2v cg2a Do12 np2 to12 Do10 to10 gg3a gg2v hg0a Pg122 Pg102 Dg12 No12 Dg10 tg12 No10 "
-       "tg10 Ng12 go1v Pg002 Dg00 Ng10 Pg022 go0a Dg02 Do00 tg00 rp1a Po022 lc1a Ng00 hx1a tg02 to00 Ng02 Do02 rp0a c01 Px122 c11 No00 "
-       "Px102 to02 c21 xz1v hx0a No02 lc0a Dx12 c00 Dx10 c10 ab12 Px002 sg122 tx10 c20 c32 xz0v ab10 od2v zr2a Px022 Nx10 Nx12 k02 Dx02 "
-       "Dx00 k21 k12 tx00 Nx00 k31 pu1 ab02 sg022 Nx02 k20 ab00 fl ex104 k30 tw pu0 ys--")
-SEQ = ("ch2v ol2 np2 go3a -ex004 os -fo cg2a go2v go0v Po122 Do12 Po102 Do10 gg3a to12 Pg122 hg0a Pg102 gg2v No12 to10 Dg10 Dg12 No10 "
-       "Pg002 tg10 go1a Po002 Dg00 lc1v Ng10 tg12 Ng12 Pg022 tg00 Dg02 rp1v Po022 tg02 Do00 Ng00 to00 Ng02 hx1a rp0a Do02 to02 hx0a Px102 "
-       "No00 c01 c11 No02 Px122 lc0v c21 c00 xz1a Dx12 c10 Dx10 c20 Px002 xz0v c32 Dx00 ab12 sg122 Px022 tx10 tx00 Nx10 ab10 Dx02 "
-       "zr1a zr0a Nx00 tx02 Nx12 Nx02 od2a k02 ex104 ys-- k11 k22 ab00 k32 pu1 k10 fl ab02 pu0 tw")
-SEQ1 = ("ch2v Po122 Po102 os re ol2 go2a go3v Po022 Do12 gx1a go0a go1v cg2a Do10 to12 No12 Po002 Do00 to10 No10 np2 gg3a Pg102 gg2v Do02 "
-        "to00 Dg10 Pg122 hg0a Dg12 No00 tg10 Pg022 tg12 Ng10 Ng12 Dg02 Pg002 lc1a rp1a to02 tg02 gx0a Dg00 No02 Ng02 Px002 hx1a tg00 Ng00 "
-        "rp0v c01 c11 Px102 c21 xz1v lc0v Dx10 c00 ab10 c31 c10 c20 c30 Px122 Dx12 xz0v Dx00 zr2v k12 sg102 od2a tx12 Px022 Nx10 Dx02 tx02 "
-        "ab00 fl Nx12 sg002 ab12 Nx00 k02 Nx02 ex104 k22 tw k32 pu1 ab02 pu0")
+HEAD = ("olv cha osv rr go3a go2v go1a Po122 Do12 cga gg3a gg2v gg0v gg1a to12 No12 Pg122 Dg12 tg12 Ng12 Pg102 Dg10 tg10 Ng10 th1v "
+        "Pg022 Dg02 tg02 Ng02 Pg002 Dg00 tg00 Ng00 th0v go0a gx3a gx2a -ex104 -ex004 -fo ys-- Po102 Do10 to10 No10 dn1 Px122 nk1 sc1 wl1v xz1v "
+        "gx1a gx0a cv Po022 Do02 to02 No02 ")
+SEQ = HEAD + ("Dx12 ab12 sg122 Nx12 Px102 Dx10 Po002 Do00 to00 No00 dn0 nk0 sc0 wl0v xz0v tx10 Nx10 ab10 Px022 Dx02 Px002 Dx00 fs2a od2a np2 ed2 "
+              "eq2 zc2a tx02 Nx02 ft1v pr1 tx00 Nx00 ft0v pr0 pu1 pu0 ab02 ab00")
+SEQ1 = SEQ
+SEQL = HEAD + ("Dx12 ab12 ex122 Px102 Dx10 Po002 Do00 to00 No00 dn0 nk0 sc0 wl0v xz0v ab10 ex102 Px001 Px011 Px021 Px031 ts12 ts13 ts10 ts11 "
+               "st1a Dx00 ab00 te00 Dx01 Dx02 Dx03 da02 da03 ab01 te01 te02 te03 ys- ta0")
+SEQ1 = 'cha osv gg2v olv -ex104 go2a cga go3v gg3a Pg122 Pg102 Po122 Dg12 gg0a Do12 -fo to12 gg1a tg12 Po102 gx0v Dg10 go1a tg10 Pg022 Ng12 Dg02 rr Do10 to10 Pg002 No12 gx1a tg02 No10 go0a Ng10 Po022 th1a Dg00 Do02 tg00 dn1 Ng02 Po002 gx3a Ng00 nk1 gx2a sc1 th0a wl1a xz1a to02 Px122 No02 Do00 dn0 ys-- to00 Px102 Dx10 No00 nk0 tx10 Dx12 sc0 wl0v ab12 Px002 Nx10 xz0v -ex004 Dx00 Px022 Dx02 fs2a np2 sg122 od2v Nx12 eq2 ed2 ft1v tx00 tx02 Nx02 ab00 Nx00 ab10 cv ft0v pr0 pr1 pu1 pu0 zc2v ab02'
+SEQ = 'chv ola go2a go3v Po102 osv Po122 Do12 go1a gg2v cga gx2a to12 gg3a Do10 gg1a Pg102 to10 Pg122 gg0a Po022 go0v rr Dg12 Dg10 Do02 tg12 No12 Ng12 tg10 Pg022 Ng10 th1v Dg02 Pg002 gx3a No10 dn1 nk1 Dg00 ys-- to02 Po002 tg02 tg00 Ng02 No02 sc1 wl1v gx0a Ng00 Px102 -ex104 Do00 xz1v to00 Px122 Dx12 -ex004 th0v Dx10 tx10 No00 gx1a ab12 dn0 nk0 sg122 sc0 fs2v wl0a Px002 xz0a Dx00 np2 Nx10 Nx12 tx00 Px022 od2a Dx02 Nx00 tx02 eq2 Nx02 ft1v ed2 ab00 ab10 -fo pr1 ab02 pu1 cv ft0a pr0 zc2v pu0'
+SEQL = 'cha olv -ex004 osv cga Pg022 gg0v gg1a Dg02 tg02 Po122 gg2a Pg102 Pg122 gg3a go2a go3v go0v Dg10 Dg12 Do12 -ex104 tg10 gx1a cv to12 Pg002 gx2a Ng10 gx3a Dg00 rr tg12 Ng12 th1v tg00 Po102 No12 Do10 Po022 to10 go1v Do02 Po002 Ng02 dn1 Ng00 No10 nk1 sc1 th0a Do00 to02 wl1a xz1a dn0 to00 ys-- No00 Px122 gx0a Dx12 No02 ab12 ex122 nk0 -fo sc0 Px102 wl0v Dx10 Px001 Px021 Px011 xz0v ab10 Dx01 Dx00 ys- ex102 Dx02 ts10 ab00 ts11 da02 Px031 ts12 ab01 te00 Dx03 ts13 da03 te01 st1a te02 te03 ta0'
 
 SCRATCH = {
-    "recs": ("sbuf", [128, V], "int32"), "Rt": ("sbuf", [128, RW], "float32"), "xe": ("sbuf", [128, XW], "bfloat16"),
-    "w0s": ("sbuf", [128, 16], "int32"), "WL": ("sbuf", [128, RO * 16], "uint16"),
+    "recs": ("sbuf", [128, V], "int32"), "Rt": ("sbuf", [128, RW], "float32"),
+    "xe": ("sbuf", [128, V + 32], "bfloat16"), "xa": ("sbuf", [128, V], "bfloat16"),
+    "w0s": ("sbuf", [128, 16], "int32"), "WL": ("sbuf", [128, (RO + 1) * 16], "uint16"),
     "O": ("sbuf", [128, 256], "uint16"), "Os": ("sbuf", [128, RO * MW], "uint16"), "Oin": ("sbuf", [128, RO * MW], "uint16"),
     "ch": ("sbuf", [128, 256], "float16"), "cg": ("sbuf", [128, 256], "float16"), "rr": ("sbuf", [128, 256], "float16"),
     "Ro": ("sbuf", [128, 4096], "float16"), "Rg": ("sbuf", [128, 4096], "float16"), "xn": ("sbuf", [128, 4096], "bfloat16"),
     "do": ("sbuf", [128, 4096], "bfloat16"), "dg": ("sbuf", [128, 4096], "bfloat16"), "dx": ("sbuf", [128, 4096], "bfloat16"),
     "ad": ("sbuf", [128, 4096], "float32"), "ex": ("sbuf", [128, 32, 256], "float32"),
-    "rep": ("sbuf", [128, RO * 256], "bfloat16"), "repin": ("sbuf", [128, RO * 256], "bfloat16"),
-    "Ls": ("sbuf", [128, 256], "bfloat16"), "fT": ("sbuf", [128, 256], "bfloat16"),
-    "ok": ("sbuf", [128, 256], "bfloat16"), "fs": ("sbuf", [128, 256], "bfloat16"), "tm": ("sbuf", [128, 256], "float16"),
-    "sc": ("sbuf", [128, 256], "float32"), "zr": ("sbuf", [128, 256], "float32"), "eq": ("sbuf", [128, 256], "float32"),
-    "sc2": ("sbuf", [128, 256], "float32"), "old": ("sbuf", [128, 256], "float32"), "Ed": ("sbuf", [128, 256], "float32"),
-    "pr": ("sbuf", [128, 256], "float32"), "xz": ("sbuf", [128, 256], "bfloat16"),
-    "mm": ("sbuf", [128, 16], "float32"), "mu": ("sbuf", [128, 16], "uint16"), "hh": ("sbuf", [128, 16], "float32"),
-    "zz": ("sbuf", [128, 16], "float32"), "ee": ("sbuf", [128, 16], "float32"), "F0": ("sbuf", [128, 16], "float32"),
-    "F": ("sbuf", [128, 16], "float32"), "vv": ("sbuf", [128, 16], "float32"), "tg": ("sbuf", [128, 32], "uint16"),
-    "ng": ("sbuf", [128, 1024], "float32"), "acc": ("sbuf", [128, 1024], "float32"), "yt": ("sbuf", [128, 256], "float32"),
-    "fl": ("sbuf", [128, RO, 256], "float32"), "yl": ("sbuf", [128, RO, 256], "float32"), "y2": ("sbuf", [128, 256], "float32"),
-    "pi": ("sbuf", [128, 8], "int32"), "pa": ("sbuf", [128, 8], "int32"), "pos": ("sbuf", [128, 8], "float32"),
-    "neg": ("sbuf", [128, 8], "float32"), "col": ("sbuf", [128, 8], "float32"), "c16": ("sbuf", [128, 16], "float32"),
+    "rep": ("sbuf", [128, RO * 16, BW], "bfloat16"), "repin": ("sbuf", [128, RO * 16 * BW], "bfloat16"),
+    "nk": ("sbuf", [128, 16 * BW], "bfloat16"), "e0": ("sbuf", [128, 16 * BW], "bfloat16"),
+    "U": ("sbuf", [128, 16 * BW], "float32"), "F": ("sbuf", [128, 16 * BW], "bfloat16"), "H": ("sbuf", [128, 256], "float16"),
+    "uf": ("sbuf", [128, 16], "float32"), "ub": ("sbuf", [128, 256], "float32"), "LU": ("sbuf", [128, 16], "uint16"),
+    "rw": ("sbuf", [128, 16], "float16"), "zc": ("sbuf", [128, 16], "float16"), "u0": ("sbuf", [128, 16], "float32"),
+    "wx": ("sbuf", [128, 256], "float16"), "eq": ("sbuf", [128, 256], "bfloat16"), "fT": ("sbuf", [128, 256], "bfloat16"),
+    "old": ("sbuf", [128, 256], "float32"), "Ed": ("sbuf", [128, 256], "float32"), "pr": ("sbuf", [128, 256], "float32"),
+    "xz": ("sbuf", [128, 256], "bfloat16"), "tg": ("sbuf", [128, 32], "uint16"),
+    "ng": ("sbuf", [128, 512], "float32"), "acc": ("sbuf", [128, 512], "float32"), "yt": ("sbuf", [128, 256], "float32"),
+    "fl": ("sbuf", [128, RO, 256], "float32"), "yl": ("sbuf", [128, RO, 256], "float32"),
+    "pi": ("sbuf", [128, 1], "int32"), "pa": ("sbuf", [128, 1], "int32"), "col": ("sbuf", [128, 8], "float32"),
+    "c16": ("sbuf", [128, 16], "float32"), "LD": ("sbuf", [128, 16], "uint16"),
     "ck": ("sbuf", [128, 256], "bfloat16"), "q": ("sbuf", [128, 256], "bfloat16"), "q16": ("sbuf", [128, 128], "bfloat16"),
-    "LD": ("sbuf", [128, 16], "uint16"), "one": ("sbuf", [128, 128], "bfloat16"), "G": ("sbuf", [128, 24], "bfloat16"),
-    "I": ("sbuf", [128, 256], "bfloat16"), "blk": ("sbuf", [128, 128], "bfloat16"), "Ifn": ("sbuf", [128, 256], "float32"),
-    "In": ("sbuf", [128, 128], "bfloat16"), "I32": ("sbuf", [128, 128], "bfloat16"), "IV": ("sbuf", [128, 128], "bfloat16"),
-    "bn": ("sbuf", [128, 128], "bfloat16"), "bV": ("sbuf", [128, 128], "bfloat16"),
-    "bt": ("sbuf", [128, RO * 128], "bfloat16"), "Bt": ("sbuf", [128, RO * 128], "bfloat16"),
-    "M1": ("sbuf", [128, 256], "bfloat16"), "M2": ("sbuf", [128, 256], "bfloat16"),
-    "RS": ("sbuf", [128, 256], "float32"), "RS2": ("sbuf", [128, 256], "float32"),
-    "ps": ("psum", [128, 4096], "float32"),
+    "one": ("sbuf", [128, 128], "bfloat16"), "G": ("sbuf", [128, 40], "bfloat16"), "I": ("sbuf", [128, 256], "bfloat16"),
+    "blk": ("sbuf", [128, 128], "bfloat16"), "If": ("sbuf", [128, 128], "float32"), "In": ("sbuf", [128, 128], "bfloat16"),
+    "Ih": ("sbuf", [128, 128], "bfloat16"),
+    "Mi": ("sbuf", [128, 256], "float32"), "Mk": ("sbuf", [128, 128], "bfloat16"), "Dt": ("sbuf", [128, RO, 8, BW], "bfloat16"),
+    "ps": ("psum", [128, 8, 512], "float32"),
 }
 SEMAPHORES = (["cv", "ca", "cp", "cg", "sent", "lw", "lx0", "lx1", "lx2", "ys"] + ["lr%d" % i for i in range(NCH)]
               + ["%s%d" % (n, t) for n in ("ao", "ar0", "ar1", "ar2", "af", "ay", "sf") for t in range(1, RO + 1)])
@@ -99,10 +80,6 @@ def mask_of(engs):
     return m
 
 
-def rows_folded(t):
-    return 1
-
-
 def rank_program(g, core, T, topo):
     hp = helpers(T, topo)
     rank = T.rank_of(core)
@@ -111,7 +88,8 @@ def rank_program(g, core, T, topo):
             if hp[c] == core:
                 helper_program(g, core, c, T, topo)
         return
-    group_program(g, core, rank, hp[core], T, topo)
+    plan = order(group_program(g, core, rank, hp[core], T, topo, None))
+    group_program(g, core, rank, hp[core], T, topo, plan)
 
 
 def helper_program(g, core, c, T, topo):
@@ -120,81 +98,166 @@ def helper_program(g, core, c, T, topo):
     nf = len(topo.engines(c, core)[1::2])
     for t in range(1, RO):
         g.wait_ge(T.sem["af%d" % t], nf)
-        s = slice(t - 1, t - 1 + rows_folded(t))
-        g.remote_dma(T.yl[:, s, :], T.fl[:, s, :], T.sem["ay%d" % t], T.sem.sent, pid, rid, mask_of(en))
+        g.remote_dma(T.yl[:, t - 1, :], T.fl[:, t - 1, :], T.sem["ay%d" % t], T.sem.sent, pid, rid, mask_of(en))
     g.wait_ge(T.sem.sent, len(en) * (RO - 1))
 
 
-def group_program(g, core, rank, helper, T, topo):
+def order(ops):
+    n = len(ops)
+    users = [[] for _ in ops]
+    for i, o in enumerate(ops):
+        for d in list(o["deps"]) + [d for d, _ in o["far"]]:
+            users[d].append(i)
+    rank = [0.0] * n
+    for i in range(n - 1, -1, -1):
+        o = ops[i]
+        rank[i] += o["cost"] + o["lat"]
+        for d in o["deps"]:
+            rank[d] = max(rank[d], rank[i])
+        for d, late in o["far"]:
+            rank[d] = max(rank[d], rank[i] + late)
+    left = [len(o["deps"]) + len(o["far"]) for o in ops]
+    ready, done, free, out = [i for i in range(n) if not left[i]], [0.0] * n, {}, []
+    bank, pool, given, uses = {b: ("", 0.0) for b in range(8)}, set(POOL), {}, {}
+    for o in ops:
+        if o["piece"]:
+            uses[o["piece"][0]] = uses.get(o["piece"][0], 0) + 1
+
+    def banks(o):
+        if not o["piece"]:
+            return o["banks"]
+        u, m, which = o["piece"]
+        if u not in given:
+            can = [b for b in pool if b % m == 0 and pool >= set(range(b, b + m))]
+            if not can:
+                return None
+            b = min(can, key=lambda b: (max(bank[b + x][1] for x in range(m)), b))
+            return [b + x for x in which]
+        return [given[u] + x for x in which]
+
+    def start(i):
+        o = ops[i]
+        s = [free.get(o["q"], 0.0)] + [done[d] + late for d, late in o["far"]]
+        s += [done[d] for d in o["deps"] if not (o["q"] == "p" == ops[d]["q"])]
+        return max(s + [bank[b][1] for b in banks(o) if bank[b][0] != o["q"]])
+
+    while ready:
+        can = [i for i in ready if banks(ops[i]) is not None]
+        st = {i: start(i) for i in can}
+        first = min(can, key=lambda i: st[i] + ops[i]["cost"])
+        mine = [j for j in can if ops[j]["q"] == ops[first]["q"]]
+        i = max((j for j in mine if st[j] < st[first] + ops[first]["cost"]), key=lambda j: (rank[j], -j))
+        for j in sorted(mine, key=lambda j: -rank[j]):
+            end = st[i] + ops[i]["cost"]
+            if rank[j] > rank[i] and st[j] < end and IDLE * (st[j] - st[i]) < min(end - st[j], rank[j] - rank[i]):
+                fit = [x for x in mine if st[x] + ops[x]["cost"] <= st[j]]
+                i = max(fit, key=lambda x: (rank[x], -x)) if fit else j
+                break
+        o = ops[i]
+        bs = banks(o)
+        if o["piece"]:
+            u, m, which = o["piece"]
+            if u not in given:
+                given[u] = bs[0] - which[0]
+                pool.difference_update(range(given[u], given[u] + m))
+            uses[u] -= 1
+            if not uses[u]:
+                pool.update(range(given[u], given[u] + m))
+        free[o["q"]] = st[i] + o["cost"]
+        done[i] = st[i] + o["cost"] + o["lat"]
+        for b in bs:
+            bank[b] = (o["q"], max(done[i], bank[b][1]))
+        out.append(i)
+        ready.remove(i)
+        for u in users[i]:
+            left[u] -= 1
+            if not left[u]:
+                ready.append(u)
+    return out, given
+
+
+def order(ops):
+    begin, done, busy, held, given, since, uses = [], [], {}, {b: [] for b in range(8)}, {}, {}, {}
+    left = {b: 0.0 for b in POOL}
+    for o in ops:
+        if o["piece"]:
+            uses[o["piece"][0]] = uses.get(o["piece"][0], 0) + 1
+    for o in ops:
+        s = max([0.0] + [done[d] + late for d, late in o["far"]]
+                + [begin[d] + ops[d]["cost"] if o["q"] == "p" == ops[d]["q"] else done[d] for d in o["deps"]])
+        bs = o["banks"]
+        if o["piece"]:
+            u, m, which = o["piece"]
+            if u not in given:
+                given[u] = min((b for b in left if b % m == 0 and all(b + x in left for x in range(m))),
+                               key=lambda b: (max([s] + [left[b + x] for x in range(m)]), b))
+                since[u] = max(left.pop(given[u] + x) for x in range(m))
+            s = max(s, since[u])
+            bs = [given[u] + x for x in which]
+        mine = busy.setdefault(o["q"], [])
+        while True:
+            hit = [e for b, e in mine if b < s + o["cost"] and e > s]
+            hit += [e for x in bs for b, e, q in held[x] if q != o["q"] and b < s + o["cost"] + o["lat"] and e > s]
+            if not hit:
+                break
+            s = min(hit)
+        begin.append(s)
+        done.append(s + o["cost"] + o["lat"])
+        mine.append((s, s + o["cost"]))
+        for x in bs:
+            held[x].append((s, done[-1], o["q"]))
+        if o["piece"]:
+            uses[u] -= 1
+            if not uses[u]:
+                left.update({given[u] + x: max(e for _, e, _ in held[given[u] + x]) for x in range(m)})
+    SPAN[:] = [max(done), begin]
+    return sorted(range(len(ops)), key=lambda i: (begin[i], i)), given
+
+
+def group_program(g, core, rank, helper, T, topo, plan):
     N = len(T.cores)
     Q = {"v": g.vector, "a": g.scalar, "p": g.tensor, "g": g, "s": g.sync}
     CS = {"v": "cv", "a": "ca", "p": "cp", "g": "cg"}
-    ops, lastw, readers, bankacc, totals = [], {}, {}, {}, {}
+    ops, lastw, readers, raised = [], {}, {}, {}
 
-    def op(q, fn, r=(), w=(), banks=(), ext=(), tok=None, inc=None):
+    def op(q, fn, cost, r=(), w=(), banks=(), ext=(), tok=None, inc=None, lat=SEM):
         me = len(ops)
-        who = q if tok is None else "dma%d" % me
-        deps = set()
-        for x in r:
-            if x in lastw:
-                deps.add(lastw[x])
+        deps = set(lastw[x] for x in r if x in lastw)
         for x in w:
             deps.update(readers.get(x, []) + ([lastw[x]] if x in lastw else []))
-        for b in banks:
-            for e, d in bankacc.setdefault(b, {}).items():
-                if e != who:
-                    deps.add(d)
-            bankacc[b][who] = me
-        if q == "p":
-            deps = set(d for d in deps if ops[d]["who"] != "p")
         for x in r:
             readers.setdefault(x, []).append(me)
         for x in w:
             lastw[x] = me
             readers[x] = []
-        ops.append({"q": q, "who": who, "fn": fn, "deps": deps, "ext": list(ext), "tok": tok, "inc": inc, "tag": TAG[0],
-                    "short": not any(x[:2] in LONG and x != "Rt" for x in w)})
-
-    def weave():
-        order, line_, done, seen = [i for i, o in enumerate(ops) if o["who"] == "v"], [], set(), {}
-        while order:
-            pick = order[0]
-            if line_ and line_[-1] in ops[pick]["deps"]:
-                for j in order[1:WEAVE]:
-                    o = ops[j]
-                    if o["short"] and not o["ext"] and all(d in done and d != line_[-1] if ops[d]["who"] == "v" else d <= seen.get(ops[d]["who"], -1)
-                                                           for d in o["deps"]):
-                        pick = j
-                        break
-            order.remove(pick)
-            line_.append(pick)
-            done.add(pick)
-            for d in ops[pick]["deps"]:
-                seen[ops[d]["who"]] = max(seen.get(ops[d]["who"], -1), d)
-        place = dict(zip(line_, sorted(line_)))
-        new = [None] * len(ops)
-        for i, o in enumerate(ops):
-            o["deps"] = set(place.get(d, d) for d in o["deps"])
-            new[place.get(i, i)] = o
-        ops[:] = new
+        deps.discard(me)
+        pc = banks if banks and isinstance(banks[0], str) else None
+        if pc:
+            banks = [plan[1][pc[0]] + x for x in pc[2]] if plan else []
+        ops.append({"q": q, "piece": pc, "who": q if tok is None else "dma%d" % me, "fn": fn, "deps": deps, "ext": list(ext), "tok": tok, "inc": inc,
+                    "tag": TAG[0], "cost": cost, "lat": lat, "banks": list(banks), "r": list(r), "w": list(w), "far": [raised[s] for s, _ in ext]})
 
     def emit():
-        weave()
-        need = set()
-        for o in ops:
+        seq, last, need = plan[0], {}, set()
+        place = {i: n for n, i in enumerate(seq)}
+        for i in seq:
+            o = ops[i]
+            for b in o["banks"]:
+                o["deps"].update(d for e, d in last.setdefault(b, {}).items() if e != o["q"])
+                last[b][o["q"]] = i
             top = {}
             for d in o["deps"]:
-                top[ops[d]["who"]] = max(top.get(ops[d]["who"], -1), d)
+                who = ops[d]["who"]
+                if not (who == "p" == o["q"]) and (who not in top or place[d] > place[top[who]]):
+                    top[who] = d
             o["deps"] = set(top.values())
             need |= o["deps"]
-        cnt = {}
-        for i, o in enumerate(ops):
+        cnt, seen, totals = {}, {}, {}
+        for i in seq:
+            o = ops[i]
             if o["tok"] is None and i in need:
                 cnt[o["q"]] = cnt.get(o["q"], 0) + 1
-                o["tok"] = (CS[o["q"]], cnt[o["q"]])
-                o["inc"] = 1
-        seen = {}
-        for o in ops:
+                o["tok"], o["inc"] = (CS[o["q"]], cnt[o["q"]]), 1
             want = {}
             for s, n in [ops[d]["tok"] for d in o["deps"]] + o["ext"]:
                 want[s] = max(want.get(s, 0), n)
@@ -214,26 +277,26 @@ def group_program(g, core, rank, helper, T, topo):
 
     v, a, pe = g.vector, g.scalar, g.tensor
 
-    def ts(out, in0, s1, op0, s2=None, op1=None, r=(), w=(), banks=()):
+    def size(ap):
+        n = 1
+        for s in ap.shape[1:]:
+            n *= s
+        return n
+
+    def cost(e, out, f=1.0):
+        return FIX[e] + size(out) * f * CYC
+
+    def ts(out, in0, s1, op0, s2=None, op1=None, r=(), w=(), banks=(), f=1.0):
         if op1 is None:
-            op("v", lambda: v.tensor_scalar(out, in0, s1, None, op0), r, w, banks)
+            op("v", lambda: v.tensor_scalar(out, in0, s1, None, op0), cost("v", out, f), r, w, banks)
         else:
-            op("v", lambda: v.tensor_scalar(out, in0, s1, s2, op0, op1), r, w, banks)
+            op("v", lambda: v.tensor_scalar(out, in0, s1, s2, op0, op1), cost("v", out, f), r, w, banks)
 
-    def tt(out, in0, in1, o, r=(), w=(), banks=()):
-        op("v", lambda: v.tensor_tensor(out, in0, in1, o), r, w, banks)
+    def tt(out, in0, in1, o, r=(), w=(), banks=(), ext=(), f=1.0):
+        op("v", lambda: v.tensor_tensor(out, in0, in1, o), cost("v", in1, f), r, w, banks, ext)
 
-    def scan(out, d0, d1, o1, r, w, banks=()):
-        op("v", lambda: v.tensor_tensor_scan(out, d0, d1, 0.0, ALU.mult, o1), r, w, banks)
-
-    def act(out, in_, f, bias=0.0, scale=1.0, r=(), w=(), banks=()):
-        op("a", lambda: a.activation(out, in_, f, bias=bias, scale=scale), r, w, banks)
-
-    def copy(e, out, in_, r, w, banks=(), ext=()):
-        if e == "v":
-            op("v", lambda: v.tensor_copy(out, in_), r, w, banks, ext)
-        else:
-            op("a", lambda: a.activation(out, in_, AF.Identity), r, w, banks, ext)
+    def act(out, in_, fn, bias=0.0, scale=1.0, r=(), w=(), banks=()):
+        op("a", lambda: a.activation(out, in_, fn, bias=bias, scale=scale), cost("a", out), r, w, banks)
 
     def line(e, out, in_, scale, bias, r, w, banks=()):
         if e == "v":
@@ -241,28 +304,39 @@ def group_program(g, core, rank, helper, T, topo):
         else:
             act(out, in_, AF.Identity, bias, scale, r, w, banks)
 
-    def mm(out, lhsT, rhs, start, stop, r, w, bank, ext=()):
-        op("p", lambda: pe.matmul(out, lhsT, rhs, start, stop), r, w, [bank], ext)
+    def gather(e, out, win, off, r, w, add=0.0, ext=()):
+        src = win.indirect(off)
+        if e == "a":
+            op("a", lambda: a.activation(out, src, AF.Identity, bias=add), cost("v", out, GATH), r, w, (), ext)
+        elif add:
+            op("v", lambda: v.tensor_scalar(out, src, add, None, ALU.add), cost("v", out, GATH), r, w, (), ext)
+        else:
+            op("v", lambda: v.tensor_copy(out, src), cost("v", out, GATH), r, w, (), ext)
 
-    def dma(q, out, in_, sem, n, r=(), w=(), ext=()):
-        op(q, lambda: Q[q].dma_start(out, in_), r, w, (), ext, tok=(sem, n), inc=16)
+    def mms(calls, r, w, banks, f=1, start=True, stop=True, each=False):
+        def fn():
+            for i, (o, l, x) in enumerate(calls):
+                ins = pe.matmul(o, l, x, each or (start and i == 0), each or (stop and i == len(calls) - 1))
+            return ins
+        op("p", fn, sum(FIX["p"] + max(64, size(x)) * f * PCYC for _, _, x in calls), r, w, banks, lat=SEM + PLAT)
 
-    def iota(out, pat, base, cm, name):
-        op("g", lambda: g.iota(out, pat, base, cm, allow_small_or_imprecise_dtypes=True), (), [name])
+    def dma(q, out, in_, sem, n, late, r=(), w=(), ext=()):
+        op(q, lambda: Q[q].dma_start(out, in_), 100, r, w, (), ext, (sem, n), 16, late)
 
-    def select(out, in_, pat, cmp, fill, base, cm, r, w):
-        op("g", lambda: g.affine_select(out, in_, pat, cmp, fill, base, cm), r, w)
+    def iota(out, pat, name):
+        op("g", lambda: g.iota(out, pat, 0, 0, allow_small_or_imprecise_dtypes=True), 130 + 2 * CYC * size(out), (), [name])
+
+    def select(out, pat, cmp, fill, base, cm, r, w):
+        op("g", lambda: g.affine_select(out, out, pat, cmp, fill, base, cm), 170 + 2 * CYC * size(out), r, w)
 
     nsent = [0]
 
     def send(dst, out, in_, sem, r):
         rid, pid, _ = topo.addr(dst)
         en = topo.engines(core, dst)[0::2]
+        raised[sem] = (len(ops), HOP + (2500 if not nsent[0] else 0))
         nsent[0] += len(en)
-        op("g", lambda: g.remote_dma(out, in_, T.sem[sem], T.sem.sent, pid, rid, mask_of(en)), r, (), tok=("sent", nsent[0]))
-
-    def s256(t):
-        return slice((t - 1) * 256, t * 256)
+        op("g", lambda: g.remote_dma(out, in_, T.sem[sem], T.sem.sent, pid, rid, mask_of(en)), 500, r, (), tok=("sent", nsent[0]), lat=0)
 
     def hs(h, n=128, base=0):
         return slice(base + h * n, base + (h + 1) * n)
@@ -283,120 +357,120 @@ def group_program(g, core, rank, helper, T, topo):
         return (0, 1) if h == 2 else (h,)
 
     def nm(h, *names):
-        return ["#%d%d%d" % (REG[x] + (i,)) if x in REG else "%s%d" % (x, i) for x in names for i in halves(h)]
+        return ["%s%d" % (x, i) for x in names for i in halves(h)]
 
-    def reg(x, h, n=128):
-        s = part(h, 128, 512 * REG[x][0] + REG[x][1])
-        return T.ps[:, s.start:s.start + n * len(halves(h))]
+    def slots(h, x):
+        return nm(h, *["#" + s for s in REG[x][2]])
 
-    def bk(*x):
-        return [REG[i][0] for i in x]
+    def reg(x, h):
+        s = slice(REG[x][0], REG[x][0] + REG[x][1])
+        return T.ps[:, 6:8, s] if h == 2 else T.ps[:, 6 + h, s]
 
-    def turn(m, t):
+    def bk(h):
+        return [6 + i for i in halves(h)]
+
+    def turn(t):
         s = (-16 * t) % 128
-        return m[:, s:s + 128]
+        return T.I[:, s:s + 128]
 
     Id = T.I[:, 0:128]
+    MARK, SIGNS, MORE, MISS = 0, 16, 24, 32
+
+    def marks(s):
+        return T.G[:, s:s + 8]
 
     cw = V // NCH
     for i in range(NCH):
         if i == 1:
-            dma("a", T.w0s[:], T.w0[:], "lw", 16, w=["w0s"])
-        dma("sa"[i % 2], T.recs[:, hs(i, cw)], T.rec[:, hs(i, cw)], "lr%d" % i, 16, w=["recs%d" % i])
-    op("g", lambda: g.iota(T.pi[:], [[-1, 8]], 16, 1), (), ["pi"])
-    iota(T.q16[:], [[16, 8], [0, 16]], 0, 0, "q16")
-    iota(T.q[:], [[0, 2], [1, 128]], 0, 0, "q")
-    iota(T.c16[:], [[16, 16]], 15, 0, "c16")
-    iota(T.ck[:], [[0, 16], [1, 16]], 0, 0, "ck")
-    iota(T.Rt[:, V:RW], [[0, RW - V]], 0, 0, "Rtb")
-    iota(T.xe[:, 0:16], [[0, 16]], 0, 0, "xe0")
-    dma("s", T.xe[:, XO:XO + V], T.x[:], "lx0", 16, r=["recs%d" % (NCH - 1)], w=["xe0", "xe1"])
-    dma("s", T.xe[:, XO + V:XO + V + 2], T.x[:, 0:2], "lx1", 16, w=["xe2"])
-    RT = ["Rt", "Rtb"] + ["Rt%d" % i for i in range(NCH)]
-    pk, C = T.pos[:, 0:1], T.col
+            dma("a", T.w0s[:], T.w0[:], "lw", 16, 2000, w=["w0s"])
+        dma("sa"[i % 2], T.recs[:, hs(i, cw)], T.rec[:, hs(i, cw)], "lr%d" % i, 16, 2500 + 1000 * i, w=["recs%d" % i])
+    RECS = ["recs%d" % i for i in range(NCH)]
+    dma("s", T.xe[:, XO:XO + V], T.x[:], "lx0", 16, 3000, r=RECS[-1:], w=["xe1"])
+    dma("s", T.xe[:, XO + V:XO + V + 2], T.x[:, 0:2], "lx1", 16, 2000, r=RECS[-1:], w=["xe2"])
+    dma("s", T.xa[:], T.x[:], "lx2", 16, 3000, r=["xe1"], w=["xa"])
+    op("g", lambda: g.iota(T.pi[:], [[0, 1]], 0, 1), 130, (), ["pi"])
+    iota(T.q[:], [[0, 2], [1, 128]], "q")
+    iota(T.q16[:], [[16, 8], [0, 16]], "q16")
+    iota(T.ck[:], [[0, 16], [1, 16]], "ck")
+    iota(T.c16[:], [[1, 16]], "c16")
+    iota(T.Rt[:, V:RW], [[0, RW - V]], "Rtb")
+    C = T.col
+    pk = C[:, 1:2]
     ts(T.pa[:], T.pi[:], 15, ALU.bitwise_and, r=["pi"], w=["pa"])
-    ts(C[:, 0:1], T.pi[:, 0:1], -16.0, ALU.add, r=["pi"], w=["c0"])
-    copy("v", T.pos[:], T.pa[:], ["pa"], ["pos"])
-    tt(C[:, 1:2], C[:, 0:1], pk, ALU.subtract, ["c0", "pos"], ["c1"])
-    ts(T.blk[:], T.q16[:], C[:, 1:2], ALU.is_equal, r=["q16", "c1"], w=["blk"])
+    line("v", C[:, 0:1], T.pi[:], 1.0, 0.0, ["pi"], ["c0"])
+    line("v", pk, T.pa[:], 1.0, 0.0, ["pa"], ["pk"])
+    line("v", C[:, 3:4], T.pa[:], 1.0, float(V), ["pa"], ["c3"])
+    tt(C[:, 4:5], C[:, 0:1], pk, ALU.subtract, ["c0", "pk"], ["c4"])
+    ts(T.blk[:], T.q16[:], C[:, 4:5], ALU.is_equal, r=["q16", "c4"], w=["blk"])
     ts(T.I[:], T.q[:], C[:, 0:1], ALU.is_equal, r=["q", "c0"], w=["I"])
-    copy("v", T.LD[:], T.c16[:], ["c16"], ["LD"])
-    line("v", T.zz[:], T.w0s[:], -1.0, float(2 * V), ["w0s"], ["zz0", "zz1"])
-    act(T.one[:], T.q16[:, 0:128], AF.Exp, scale=0.0, r=["q16"], w=["one"])
-    line("v", C[:, 4:5], pk, 1.0, float(V), ["pos"], ["c4"])
-    line("v", T.neg[:], T.pos[:], -1.0, 1.0, ["pos"], ["neg"])
+    act(T.one[:], T.q16[:], AF.Exp, scale=0.0, r=["q16"], w=["one"])
+    for x, src, sc in (("In", "I", -1.0), ("If", "I", 1.0), ("Ih", "I", 0.5)):
+        line("a", T[x][:], T[src][:, 0:128], sc, 0.0, [src], [x])
+    for i, sc in enumerate((1.0, 1.0, NR / (2.0 * NR - 16), BIG, 1.0 / (16.5 - TH))):
+        line("a", marks(8 * i), T.blk[:, 0::16], sc, 0.0, ["blk"], ["G%d" % i])
+    GS = ["G%d" % i for i in range(5)]
+    for x, ap, c in (("e0", T.e0[:], 0.0), ("e0", T.e0[:, 0::BW], BIG), ("Dt", T.Dt[:], 0.0), ("#D", T.ps[:, 6:8, 272:416], 0.0),
+                     ("rep", T.rep[:, :, 0], BIG), ("rep", T.rep[:, :, BW - 1], -BIG)):
+        op("v", lambda ap=ap, c=c: v.memset(ap, c), cost("v", ap, 0.5), (), nm(2, x), bk(2) if x == "#D" else ())
+    ts(T.Mi[:], T.ck[:], pk, ALU.is_equal, BIG, ALU.mult, r=["ck", "pk"], w=["Mi"])
+    ts(T.Mk[:], T.ck[:, 0:128], pk, ALU.is_lt, 0.5, ALU.mult, r=["ck", "pk"], w=["Mk"])
+    tt(T.Mk[:], T.Mk[:], T.Mi[:, 0:128], ALU.add, ["Mk", "Mi"], ["Mk"], f=2)
+    ts(T.Mi[:], T.ck[:], pk, ALU.is_equal, r=["ck", "pk"], w=["Mi"])
+    line("v", T.LU[:], T.c16[:], float(BW), float(BW - 1), ["c16"], ["LU"])
+    line("v", T.LD[:], T.c16[:], 1.0, 0.0, ["c16"], ["LD"])
+    line("v", T.WL[:, 0:16], T.w0s[:], 1.0, 0.0, ["w0s"], nm(2, "WL1"))
+    line("v", T.zc[:], T.w0s[:], 1.0, float(-C0), ["w0s"], nm(2, "zc"))
+    ts(T.u0[:], T.w0s[:], float(V - 1), ALU.is_ge, float(-V), ALU.mult, r=["w0s"], w=["u0"])
+    tt(T.u0[:], T.u0[:], T.zc[:], ALU.add, ["u0"] + nm(2, "zc"), ["u0"])
+    tt(T.wx[:], T.u0[:].indirect(T.LD[:]), T.Mi[:], ALU.mult, ["u0", "LD", "Mi"], ["wx"])
 
-    def scaled(*xs):
-        for x, src, sc in xs:
-            line("a", T[x][:], T[src][:, 0:T[x].shape[1]], sc, 0.0, [src], [x])
-
-    scaled(("Ifn", "I", -1.0), ("IV", "I", float(2 * V - C0)), ("In", "I", -1.0))
-
-    def lists(t, h):
-        line("v", T.WL[:, part(h, 8, 16 * (t - 1))], T.zz[:, part(h, 8)], -1.0, float(2 * V), nm(h, "zz"), nm(h, "WL%d" % t))
+    def differences():
+        for c, fill in ((1, -1.0), (2, 1.0)):
+            for m in (0, 1):
+                select(T.Dt[:, :, :, c:c + 16], [[-1, RO], [-16, 8], [1, 16]], ALU.not_equal, fill, -16 * m, 1, ["Os1"], nm(2, "Dt"))
+        select(T.Dt[:, :, :, 1:18], [[0, RO], [-16, 8], [0, 17]], ALU.is_ge, 0.0, 0, 1, (), nm(2, "Dt"))
+        select(T.Dt[:, :, :, 1:18], [[0, RO], [16, 8], [0, 17]], ALU.is_ge, 0.0, 15, -1, (), nm(2, "Dt"))
 
     def turned(t):
-        mm(reg("ws", 0, 16), turn(T.Ifn, t), T.zz[:], True, False, ["Ifn"] + nm(2, "zz"), nm(0, "ws"), *bk("ws"))
-        mm(reg("ws", 0, 16), T.IV[:], T.one[:, 0:16], False, True, ["IV", "one"], nm(0, "ws"), *bk("ws"))
+        mms([(T.ps[:, 6, 256:MW], turn(t), T.zc[:])], ["I"] + nm(2, "zc"), ["#C0"], [6])
 
-    def fall():
-        ts(T.ee[:], T.zz[:], float(V + 1), ALU.is_equal, float(V), ALU.mult, r=["zz0", "zz1"], w=["ee"])
-        tt(T.F0[:], T.ee[:], T.zz[:], ALU.add, ["ee", "zz0", "zz1"], ["F0"])
-        ts(T.F[:], T.F0[:], float(-V - 1), ALU.add, r=["F0"], w=["F"])
-
-    lists(1, 2)
     turned(1)
-    for i in range(NCH):
-        line("v", T.Rt[:, hs(i, cw)], T.recs[:, hs(i, cw)], 1.0, float(-C0), ["recs%d" % i], ["Rt%d" % i])
-    for i, sc in enumerate((1.0, 1.0, NR / (2.0 * NR - 16))):
-        line("a", T.G[:, hs(i, 8)], T.blk[:, 0::16], sc, 0.0, ["blk"], ["G"])
-    for t in range(1, RO + 1):
-        act(T.bt[:, hs(t - 1)], T.ck[:, 16 - t:144 - t], AF.Relu, bias=T.neg[:, t:t + 1], r=["ck", "neg"], w=["bt%d" % t])
-    act(T.RS[:], T.ck[:], AF.Sign, r=["ck"], w=["RS"])
 
-    def rest():
-        scaled(("I32", "I", 32.0), ("bn", "blk", -1.0), ("bV", "blk", float(2 * V - C0)))
-        select(T.Bt[:], T.bt[:], [[0, RO], [-16, 8], [0, 16]], ALU.is_ge, 0.0, 0, 1, ["bt%d" % t for t in range(1, RO + 1)], ["Bt"])
-        select(T.Bt[:], T.Bt[:], [[0, RO], [16, 8], [0, 16]], ALU.is_ge, 0.0, 15, -1, ["Bt"], ["Bt"])
-        select(T.Bt[:], T.Bt[:], [[0, RO], [-1, 128]], ALU.not_equal, -1.0, 0, 1, ["Bt"], ["Bt"])
-        select(T.RS2[:], T.RS[:], [[0, 16], [1, 16]], ALU.not_equal, 8192.0, -15, 0, ["RS"], ["RS2"])
-        ts(T.M1[:], T.ck[:], pk, ALU.not_equal, -16384.0, ALU.mult, r=["ck", "pos"], w=["M1"])
-        ts(T.M2[:], T.ck[:], pk, ALU.is_gt, -16384.0, ALU.mult, r=["ck", "pos"], w=["M2"])
-        fall()
-        dma("s", T.xe[:, XO + V + 2:XO + 2 * V], T.x[:, 2:V], "lx2", 16, r=["Os1"], w=["xe3"])
+    def lists(t, e, out, off, r, w, add=0.0, ext=()):
+        if t == 1:
+            gather(e, out, T.recs[:], off, RECS + r, w, add - C0, ext)
+        else:
+            gather(e, out, T.Rt[:, 0:V], off, ["Rt"] + r, w, add, ext)
+
+    def times(t, h):
+        return T.WL[:, part(h, 8, 16 * (t - 1))]
 
     def arrived(t):
         return [("ao%d" % t, narr(asker(t)))]
 
-    def names(t, h, e):
-        copy(e, T.ch[:, part(h)], T.Rt[:].indirect(T.WL[:, part(h, 8, 16 * (t - 1))]), RT + nm(h, "WL%d" % t), nm(h, "ch"))
-        mm(reg("sh", h), turn(T.I, t), T.ch[:, part(h)], True, True, ["I"] + nm(h, "ch"), nm(h, "sh"), *bk("sh"))
-
-    def ask(t):
+    def ask(t, e):
         s = hs(t - 1, MW)
-        ts(T.Os[:, s], reg("sh", 0, MW), float(C0), ALU.add, r=nm(2, "sh") + nm(0, "ws"), w=["Os%d" % t], banks=bk("sh"))
+        mms([(T.ps[:, 6, 0:256], turn(t), T.ch[:])], ["I", "ch"], ["#A0", "#B0"], [6])
+        line(e, T.Os[:, s], T.ps[:, 6, 0:MW], 1.0, float(C0), ["#A0", "#B0", "#C0"], ["Os%d" % t], [6])
         send(guest(t), T.Oin[:, s], T.Os[:, s], "ao%d" % t, ["Os%d" % t])
+        if t == 1:
+            differences()
 
-    def after(h):
-        ts(T.rr[:, part(h)], T.ch[:, part(h)], float(C0 - 1), ALU.is_ge, float(-V), ALU.mult, r=nm(h, "ch"), w=nm(h, "rr"))
-        mm(reg("nP", h), Id, T.ch[:, part(h)], True, False, ["I"] + nm(h, "ch"), nm(h, "nP"), *bk("nP"))
-        for x in halves(h):
-            mm(reg("nP", x), Id, T.one[:], False, False, ["I", "one"], nm(h, "nP"), *bk("nP"))
-        mm(reg("nP", h), Id, T.rr[:, part(h)], False, True, ["I"] + nm(h, "rr"), nm(h, "nP"), *bk("nP"))
-
-    def big(t, p, qu, n, e):
-        s, w = hs(0, 1024 * n, 1024 * qu), ["%s%d" % ({"o": "Ro", "g": "Rg", "x": "xn"}[p], qu + i) for i in range(n)]
+    def big(t, p, qu, e):
+        s = hs(qu, 1024)
         if p == "o":
-            copy(e, T.Ro[:, s], T.Rt[:].indirect(T.O[:, hs(0, 64 * n, 64 * qu)]), RT + ["O%d" % (qu // 2)], w)
+            lists(t, e, T.Ro[:, s], T.O[:, hs(qu, 64)], ["O"], ["Ro%d" % qu])
         elif p == "g":
-            copy(e, T.Rg[:, s], T.Rt[:].indirect(T.Oin[:, hs(0, 64 * n, (t - 1) * MW + 64 * qu)]), RT, w, (), arrived(t))
+            lists(t, e, T.Rg[:, s], T.Oin[:, hs(qu, 64, (t - 1) * MW)], [], ["Rg%d" % qu], 0.0, arrived(t))
         else:
-            copy(e, T.xn[:, s], T.xe[:, 16:16 + V].indirect(T.O[:, hs(0, 64 * n, 64 * qu)]), ["xe1", "xe2", "O%d" % (qu // 2)], w)
+            gather(e, T.xn[:, s], T.xe[:, 16:16 + V], T.O[:, hs(qu, 64)], ["xe1", "xe2", "O"], ["xn%d" % qu])
 
-    free, bank, due = set(POOL), {}, {}
+    bank, due = {}, {}
 
     def piece(u):
-        return T.ps[:, 512 * bank[u][0]:512 * (bank[u][-1] + 1)], ["pb%d" % b for b in bank[u]], bank[u]
+        key, n = bank[u]
+        b = plan[1][key] if plan else 0
+        return T.ps[:, b:b + n, :], ["%s.%d" % (key, i) for i in range(n)], (key, n, list(range(n)))
 
     def cols(h, j, n=1):
         return hs(0, 512 * n, 512 * (4 * h + j))
@@ -405,108 +479,114 @@ def group_program(g, core, rank, helper, T, topo):
         return ["%s%d%d" % (x, h, j + i) for i in range(n)]
 
     def diff(u, n=0):
-        if n:
-            b = min(b for b in free if free >= set(range(b, b + n)))
-            bank[u] = list(range(b, b + n))
-            free.difference_update(bank[u])
         p, h, j = u
+        if n:
+            bank[u] = (TAG[0], n)
+        key, m = bank[u]
         wide, small = {"o": ("Ro", "ch"), "g": ("Rg", "cg"), "x": ("xn", "xz")}[p]
-        for i in range(4 * len(bank[u])):
-            b = bank[u][i // 4]
+        for i in range(m):
             if (p == "x") == (n > 0):
-                l, r, rd = Id, T[wide][:, 2048 * h + 4 * j + i:2048 * (h + 1):16], ["%s%d" % (wide, 2 * h), "%s%d" % (wide, 2 * h + 1)]
+                calls = [(Id, T[wide][:, 2048 * h + 4 * (j + i) + k:2048 * (h + 1):16]) for k in range(4)]
+                rd = ["%s%d" % (wide, 2 * h), "%s%d" % (wide, 2 * h + 1)]
             else:
-                l, r, rd = T.In[:], T[small][:, hs(h)], nm(h, small)
-            mm(T.ps[:, hs(i % 4, 128, 512 * b)], l, r, n > 0 and i % 4 == 0, n == 0 and i % 4 == 3, ["I", "In"] + rd, ["pb%d" % b], b)
+                calls, rd = [(T.In[:], T[small][:, hs(h)])] * 4, ["xz%d" % h if p == "x" else small]
+            w = ["%s.%d" % (key, i)]
+            b = (plan[1][key] if plan else 0) + i
+            mms([(T.ps[:, b, hs(k)], l, x) for k, (l, x) in enumerate(calls)], ["I", "In"] + rd, w, (key, m, [i]), 1, n > 0, n == 0)
 
     def test(t, p, h, j):
         d, rd, bs = piece((p, h, j))
         c = BH if p == "x" else B2
-        ts(T["d" + p][:, cols(h, j, len(bs))], d, c, ALU.add, c, ALU.is_equal, r=rd, w=sub("d" + p, h, j, len(bs)), banks=bs)
-        due[p, h, j] = (len(bs), t % 8 if p == "g" else 0)
+        ts(T["d" + p][:, cols(h, j, bs[1])], d, c, ALU.add, c, ALU.not_equal if p == "o" else ALU.is_equal, r=rd,
+           w=sub("d" + p, h, j, bs[1]), banks=bs)
+        due[p, h, j] = (bs[1], {"g": t % 8, "o": MISS, "x": MARK}[p])
 
     def sgn(h, j, n):
         act(T.dx[:, cols(h, j, n)], T.ad[:, cols(h, j, n)], AF.Sign, bias=0.5 + 2.0 ** -21, scale=-1.0, r=sub("ad", h, j, n), w=sub("dx", h, j, n))
-        due["x", h, j] = (n, 16)
+        due["x", h, j] = (n, SIGNS)
 
-    def count(p, h, j):
+    def count(t, p, h, j):
         x = {"o": "LT", "g": "Lg", "x": "NC"}[p]
-        (n, s), o = due.pop((p, h, j)), 512 * REG[x][0] + REG[x][1] + 128 * h
-        for k in range(4 * j, 4 * (j + n)):
-            mm(T.ps[:, o + k:o + 128:16], T["d" + p][:, hs(k, 128, 2048 * h)], T.G[:, s:s + 8], True, True,
-               ["d%s%d%d" % (p, h, k // 4), "G"], nm(h, x), *bk(x))
-
-    def likes(h, e):
-        copy(e, T.Ls[:, part(h)], reg("LT", h), nm(h, "LT"), nm(h, "Ls"), bk("LT"))
+        (n, s), (o, wide, _) = due.pop((p, h, j)), REG[x]
+        mms([(T.ps[:, 6 + h, o + (k if p == "x" else (t - k - 1) % 16 + (p == "o")):o + wide:wide // 8], T["d" + p][:, hs(k, 128, 2048 * h)], marks(s))
+             for k in range(4 * j, 4 * (j + n))], GS + sub("d" + p, h, j, n), slots(h, x), bk(h), each=True)
 
     answer = {}
 
-    def reply(t, h, e):
-        s = part(h, 128, (t - 1) * 256)
+    def reaches(e, out, in_, bound, r, w, banks):
         if e == "v":
-            ts(T.rep[:, s], reg("Lg", h), float(TH), ALU.is_ge, r=nm(h, "Lg"), w=nm(h, "rep%d" % t), banks=bk("Lg"))
+            ts(out, in_, float(bound), ALU.is_ge, r=r, w=w, banks=banks)
         else:
-            act(T.rep[:, s], reg("Lg", h), AF.Sign, bias=0.5 - TH, r=nm(h, "Lg"), w=nm(h, "rep%d" % t), banks=bk("Lg"))
-        send(asker(t), T.repin[:, s], T.rep[:, s], "ar%d%d" % (h, t), nm(h, "rep%d" % t))
+            act(out, in_, AF.Sign, bias=0.5 - bound, r=r, w=w, banks=banks)
+
+    def reply(t, h, e):
+        s = part(h, 8, (t - 1) * 16)
+        reaches(e, T.rep[:, s, 1:17], reg("Lg", h), TH, slots(h, "Lg") + nm(h, "rep"), nm(h, "rep%d" % t), bk(h))
+        send(asker(t), T.repin[:, BW * s.start:BW * s.stop], T.rep[:, s, :], "ar%d%d" % (h, t), nm(h, "rep%d" % t))
         answer.update({i: h for i in halves(h)})
 
-    def chain(t, h, i):
-        s, e8 = part(h), part(h, 8)
-        if i == 0:
-            for x in halves(h):
-                mm(reg("L", x), T.Ls[:, hs(x)], Id, True, False, ["I"] + nm(x, "Ls"), nm(x, "L"), *bk("L"))
-                mm(reg("L", x), T.repin[:, hs(x, 128, (t - 1) * 256)], T.I32[:], False, True, ["I32"], nm(x, "L"), *bk("L"),
-                   [("ar%d%d" % (answer[x], t), narr(guest(t)))])
-            ts(T.ok[:, s], reg("L", h), float(32 + TH), ALU.is_ge, r=nm(h, "L"), w=nm(h, "ok"), banks=bk("L"))
-            mm(reg("val", h), T.Bt[:, hs(t - 1)], T.ok[:, s], True, True, ["Bt"] + nm(h, "ok"), nm(h, "val"), *bk("val"))
-        if i == 1:
-            ts(T.fs[:, s], reg("val", h), -1.0, ALU.is_le, r=nm(h, "val"), w=nm(h, "fs"), banks=bk("val"))
-            tt(T.tm[:, s], T.fs[:, s], reg("nP", h), ALU.mult, nm(h, "fs", "nP"), nm(h, "tm"), bk("nP"))
-            for j, (l, r, rd) in enumerate(((Id, T.M1, ["I", "M1"]), (Id, T.M2, ["I", "M2"]), (T.bV[:], T.fs, ["bV"] + nm(h, "fs")),
-                                            (T.bn[:], T.tm, ["bn"] + nm(h, "tm")))):
-                mm(reg("Z", h), l, r[:, s], j == 0, j == 3, rd, nm(h, "Z"), *bk("Z"))
-        if i == 2:
-            scan(T.sc[:, s], T.RS[:, s], reg("Z", h), ALU.max, ["RS"] + nm(h, "Z"), nm(h, "sc"), bk("Z"))
-            tt(T.mm[:, e8], T.sc[:, s.start + 15:s.stop:16], T.F[:, e8], ALU.max, nm(h, "sc") + ["F"], nm(h, "mm"))
-            line("v", T.mu[:, e8], T.mm[:, e8], -1.0, float(2 * V + XO), nm(h, "mm"), nm(h, "mu"))
-        if i == 3:
-            ts(T.hh[:, e8], T.mm[:, e8], float(V), ALU.is_le, float(V), ALU.mult, r=nm(h, "mm"), w=nm(h, "hh"))
-            tt(T.zz[:, e8], T.mm[:, e8], T.hh[:, e8], ALU.add, nm(h, "mm", "hh"), nm(h, "zz"))
-            lists(t + 1, h)
+    def chosen(buf, h):
+        s = part(h, 8 * BW)
+        return buf[:, s.start + BW - 1:s.stop:BW]
 
-    def state(h, e):
-        copy(e, T.xz[:, part(h)], T.xe[:, 0:XO + 2 * V].indirect(T.mu[:, part(h, 8)]), ["xe0", "xe1", "xe2", "xe3"] + nm(h, "mu"), nm(h, "xz"))
+    def steps(t, h):
+        o, e8 = reg("dn", h), hs(h, 8)
+        lead = T.ps[:, 6 + h, 1:8 * BW:BW]
+        calls = [(o, T.ch[:, hs(h)], T.Dt[:, t - 1]), (o, T.rr[:, hs(h)], T.Dt[:, t - 1])]
+        if t == 1:
+            calls.append((lead, T.wx[:, hs(h)], marks(MARK)))
+        else:
+            ts(T.rw[:, e8], chosen(T.U, h), float(V - 2 - C0), ALU.is_ge, float(-V), ALU.mult, r=nm(h, "U"), w=nm(h, "rw"))
+            calls += [(lead, T.If[:], chosen(T.U, h)), (lead, Id, T.rw[:, e8]), (lead, Id, T.one[:, 0:8])]
+        mms(calls, ["ch", "rr", "wx", "I", "If", "one"] + GS + nm(2, "Dt") + nm(h, "U", "rw"), slots(h, "dn"), bk(h))
 
-    def older(t, h, e):
-        copy(e, T.old[:, part(h)], T.Rt[:].indirect(T.WL[:, part(h, 8, 16 * t)]), RT + nm(h, "WL%d" % (t + 1)), nm(h, "old"))
+    def untwin(t, h):
+        ext = [("ar%d%d" % (x, t), narr(guest(t))) for x in sorted(set(answer[i] for i in halves(h)))]
+        tt(T.nk[:, part(h, 8 * BW)], reg("LT", h), T.repin[:, part(h, 8 * BW, (t - 1) * 16 * BW)], ALU.is_ge, slots(h, "LT"), nm(h, "nk"), bk(h), ext)
 
-    def spread(h, e):
-        line(e, T.zr[:, part(h)], T.sc[:, part(h)].indirect(T.LD[:, 0:8 * len(halves(h))]), 1.0, -16384.0, nm(h, "sc") + ["LD"], nm(h, "zr"))
+    def scan(out, d0, d1, o0, o1, r, w, banks, f):
+        op("v", lambda: v.tensor_tensor_scan(out, d0, d1, 0.0, o0, o1), cost("v", d1, f), r, w, banks)
 
-    def claim(h, i):
-        s, e8 = part(h), part(h, 8)
-        if i == 0:
-            tt(T.Ed[:, s], T.old[:, s], reg("nP", h), ALU.subtract, nm(h, "old", "nP"), nm(h, "Ed"), bk("nP"))
-        if i == 1:
-            tt(T.eq[:, s], T.zr[:, s], reg("Z", h), ALU.is_equal, nm(h, "zr", "Z"), nm(h, "eq"), bk("Z"))
-            scan(T.sc2[:, s], T.RS2[:, s], T.eq[:, s], ALU.add, ["RS2"] + nm(h, "eq"), nm(h, "sc2"))
-            e = slice(s.start + 15, s.stop, 16)
-            tt(T.vv[:, e8], T.sc2[:, e], T.sc[:, e], ALU.subtract, nm(h, "sc2", "sc"), nm(h, "vv"))
-            ts(T.tg[:, 2 * e8.start:2 * e8.stop:2], T.vv[:, e8], float(2 * V), ALU.add, C[:, 4:5], ALU.min, r=nm(h, "vv") + ["c4"], w=nm(h, "tg"))
-        if i == 2:
-            ts(T.fT[:, s], reg("NC", h), float(NR), ALU.is_ge, r=nm(h, "NC"), w=nm(h, "fT"), banks=bk("NC"))
-            for x in halves(h):
-                mm(reg("put", x), T.fT[:, hs(x)], Id, True, True, ["I"] + nm(x, "fT"), nm(x, "put"), *bk("put"))
-        if i == 3:
-            tt(T.pr[:, s], T.Ed[:, s], reg("put", h), ALU.mult, nm(h, "Ed", "put"), nm(h, "pr"), bk("put"))
+    def choose(h):
+        for x in halves(h):
+            scan(T.U[:, hs(x, 8 * BW)], reg("dn", x), T.nk[:, hs(x, 8 * BW)], ALU.add, ALU.mult, slots(x, "dn") + nm(x, "nk"), nm(x, "U"), bk(x), 1)
+        src = T.U[:, part(h, 8 * BW)].indirect(T.LU[:, 0:8 * len(halves(h))])
+        tt(T.H[:, part(h)], src, T.Mi[:, part(h)], ALU.mult, nm(h, "U") + ["LU", "Mi"], nm(h, "H"), f=GATH)
+        for x in halves(h):
+            mms([(reg("Z", x), T.H[:, hs(x)], marks(MARK))], GS + nm(x, "H"), slots(x, "Z"), bk(x))
+
+    def flag(h, e):
+        scan(T.F[:, part(h, 8 * BW)], T.nk[:, part(h, 8 * BW)], T.e0[:, part(h, 8 * BW)], ALU.mult, ALU.add, nm(h, "nk", "e0"), nm(h, "F"), (), 0.5)
+        tt(T.uf[:, part(h, 8)], chosen(T.U, h), chosen(T.F, h), ALU.add, nm(h, "U", "F"), nm(h, "uf"), f=2)
+        gather(e, T.ub[:, part(h)], T.uf[:, part(h, 8)], T.LD[:, 0:8 * len(halves(h))], nm(h, "uf") + ["LD"], nm(h, "ub"))
+
+    def claim(h):
+        for x in halves(h):
+            mms([(reg("eq", x), T.blk[:], T.H[:, hs(x)]), (reg("eq", x), Id, T.Mk[:])], ["blk", "I", "Mk"] + nm(x, "H"), slots(x, "eq"), bk(x))
+        tt(T.eq[:, part(h)], reg("eq", h), T.ub[:, part(h)], ALU.is_equal, slots(h, "eq") + nm(h, "ub"), nm(h, "eq"), bk(h))
+        for x in halves(h):
+            mms([(reg("tg", x), T.H[:, hs(x)], marks(MARK)), (reg("tg", x), T.eq[:, hs(x)], marks(MORE))], GS + nm(x, "H", "eq"), slots(x, "tg"), bk(x))
+        s = part(h, 16)
+        ts(T.tg[:, s.start:s.stop:2], reg("tg", h), float(C0 + 1), ALU.add, C[:, 3:4], ALU.min, r=slots(h, "tg") + ["c3"], w=nm(h, "tg"), banks=bk(h))
+
+    def after(h):
+        for x in halves(h):
+            mms([(reg("nP", x), Id, r) for r in (T.ch[:, hs(x)], T.rr[:, hs(x)], T.one[:])], ["I", "ch", "rr", "one"], slots(x, "nP"), bk(x))
+
+    def near(h, e):
+        reaches(e, T.fT[:, part(h)], reg("NC", h), NR, slots(h, "NC"), nm(h, "fT"), bk(h))
+        for x in halves(h):
+            calls = [(T.fT[:, hs(x)], Id)] if e == "v" else [(T.one[:], T.Ih[:]), (T.fT[:, hs(x)], T.Ih[:])]
+            mms([(reg("put", x), l, r) for l, r in calls], ["I", "Ih", "one"] + nm(x, "fT"), slots(x, "put"), bk(x))
 
     def put(h):
         for b in range(8 * h + 7, 8 * h - 1, -1):
-            tt(T.Rt[:].indirect(T.tg[:, 2 * b:2 * b + 1]), T.old[:, hs(b, 16)], T.pr[:, hs(b, 16)], ALU.subtract, nm(h, "tg", "pr", "old"), ["Rt"])
+            tt(T.Rt[:].indirect(T.tg[:, 2 * b:2 * b + 1]), T.old[:, hs(b, 16)], T.pr[:, hs(b, 16)], ALU.subtract,
+               nm(h, "tg", "pr", "old") + ["Rtb"] + ["Rt%d" % i for i in range(NCH)], ["Rt"], f=SCAT)
 
     def absd(h, j):
         d, rd, bs = piece(("x", h, j))
-        act(T.ad[:, cols(h, j, len(bs))], d, AF.Abs, r=rd, w=sub("ad", h, j, len(bs)), banks=bs)
+        act(T.ad[:, cols(h, j, bs[1])], d, AF.Abs, r=rd, w=sub("ad", h, j, bs[1]), banks=bs)
 
     def expo(t, h, j, n):
         act(T.ex[:, hs(0, 4 * n, 16 * (t % 2) + 4 * j), hs(h)], T.ad[:, cols(h, j, n)], AF.Exp, scale=-1.0,
@@ -514,58 +594,46 @@ def group_program(g, core, rank, helper, T, topo):
 
     def fold(t):
         rid, pid, _ = topo.addr(helper)
-        en, n = topo.engines(core, helper)[1::2], rows_folded(t)
+        en = topo.engines(core, helper)[1::2]
         trs = [RemoteDMATransfer(dst_ids=[DstId(rid=rid, pnc=pid)], dma_engine_mask=mask_of(en), remote_sem=T.sem["af%d" % t],
-                                 srcs=[T.ex[:, hs(k, n, 16 * (t % 2)), :] for k in range(16 // n)], dsts=[T.fl[:, hs(0, n, t - 1), :]],
-                                 alu_op=1)]
-        op("g", lambda: g.remote_dma_fused(trs, local_sem=T.sem["sf%d" % t]), sub("ex%d" % (t % 2), 0, 0, 4) + sub("ex%d" % (t % 2), 1, 0, 4),
-           (), tok=("sf%d" % t, len(en)))
+                                 srcs=[T.ex[:, 16 * (t % 2) + k, :] for k in range(16)], dsts=[T.fl[:, t - 1, :]], alu_op=1)]
+        raised["ay%d" % t] = (len(ops), 2 * HOP)
+        op("g", lambda: g.remote_dma_fused(trs, local_sem=T.sem["sf%d" % t]), 500, sub("ex%d" % (t % 2), 0, 0, 4) + sub("ex%d" % (t % 2), 1, 0, 4),
+           (), tok=("sf%d" % t, len(en)), lat=FOLD)
 
     nys = [0]
 
     def store(cs, src, r=(), ext=()):
         nys[0] += 16
-        dma("s", T.y[:, cs], src, "ys", nys[0], r=r, ext=ext)
-
-    def ystore(t):
-        back = [("ay%d" % t, narr(helper))]
-        if rows_folded(t) == 1:
-            store(s256(t), T.yl[:, t - 1, :], ext=back)
-        else:
-            op("v", lambda: v.tensor_tensor(T.y2[:], T.yl[:, t - 1, :], T.yl[:, t, :], ALU.add), (), ["y2"], (), back)
-            store(s256(t), T.y2[:], ["y2"])
+        dma("s", T.y[:, cs], src, "ys", nys[0], 2000, r=r, ext=ext)
 
     def tail_abs(h, j):
         d, rd, bs = piece(("x", h, j))
-        line("v", T.ng[:, 0:512 * len(bs)], d, -1.0, 0.0, rd, ["ng"], bs)
-        tt(T.ad[:, cols(h, j, len(bs))], T.ng[:, 0:512 * len(bs)], d, ALU.max, ["ng"] + rd, sub("ad", h, j, len(bs)), bs)
+        line("v", T.ng[:], d, -1.0, 0.0, rd, ["ng"], bs)
+        tt(T.ad[:, cols(h, j)], T.ng[:], d, ALU.max, ["ng"] + rd, sub("ad", h, j, 1), bs)
 
     added = [0]
 
     def tail_sum(h, j):
-        for k in range(4 * j, 4 * j + 4):
-            added[0] += 1
-            mm(reg("S", h), T.Ifn[:, 0:128], T.ex[:, 16 * (RO % 2) + k, hs(h)], added[0] == 1, added[0] == 16,
-               ["Ifn", "ex%d%d%d" % (RO % 2, h, j), "tm0"], nm(h, "S"), *bk("S"))
+        added[0] += 1
+        mms([(reg("S", h), T.If[:], T.ex[:, 16 * (RO % 2) + k, hs(h)]) for k in range(4 * j, 4 * j + 4)],
+            ["If", "ex%d%d%d" % (RO % 2, h, j)], slots(h, "S"), bk(h), 4, added[0] == 1, added[0] == 4)
 
     def tail_store(h, e):
-        line(e, T.yt[:, hs(h)], reg("S", h), -1.0, 0.0, nm(h, "S"), nm(h, "yt"), bk("S"))
+        line(e, T.yt[:, hs(h)], reg("S", h), 1.0, 0.0, slots(h, "S"), nm(h, "yt"), bk(h))
         store(hs(h, 128, (RO - 1) * 256), T.yt[:, hs(h)], nm(h, "yt"))
 
     def tail_exp(h, j):
         d, rd, bs = piece(("x", h, j))
-        n = len(bs)
-        acc = T.acc[:, 0:512 * n]
         if j == 0:
-            act(acc, T.ad[:, cols(h, 0, n)], AF.Exp, scale=-1.0, r=sub("ad", h, 0, n), w=["acc"])
+            act(T.acc[:], T.ad[:, cols(h, 0)], AF.Exp, scale=-1.0, r=sub("ad", h, 0, 1), w=["acc"])
         else:
-            act(d, T.ad[:, cols(h, j, n)], AF.Exp, scale=-1.0, r=sub("ad", h, j, n), w=rd, banks=bs)
-            tt(acc, acc, d, ALU.add, ["acc"] + rd, ["acc"], bs)
+            act(d, T.ad[:, cols(h, j)], AF.Exp, scale=-1.0, r=sub("ad", h, j, 1), w=rd, banks=bs)
+            tt(T.acc[:], T.acc[:], d, ALU.add, ["acc"] + rd, ["acc"], bs)
 
-    def tail_add(h, n):
-        for m in (512, 256)[2 - n:]:
-            tt(T.acc[:, 0:m], T.acc[:, 0:m], T.acc[:, m:2 * m], ALU.add, ["acc"], ["acc"])
-        tt(T.yt[:, hs(h)], T.acc[:, 0:128], T.acc[:, 128:256], ALU.add, ["acc"], nm(h, "yt"))
+    def tail_add(h):
+        tt(T.acc[:, 0:256], T.acc[:, 0:256], T.acc[:, 256:512], ALU.add, ["acc"], ["acc"], f=2)
+        tt(T.yt[:, hs(h)], T.acc[:, 0:128], T.acc[:, 128:256], ALU.add, ["acc"], nm(h, "yt"), f=2)
         store(hs(h, 128, (RO - 1) * 256), T.yt[:, hs(h)], nm(h, "yt"))
 
     def unit(w):
@@ -577,40 +645,54 @@ def group_program(g, core, rank, helper, T, topo):
 
     def run(t, w):
         c, p = w[:2], [int(z) if z.isdigit() else z for z in w[2:]]
+        h = p[0] if p else 2
         if c[0] in "PD":
             diff(unit(w), *p[2:])
         elif c[0] == "N":
-            count(c[1], *p)
+            count(t, c[1], *p)
         elif c in ("go", "gg", "gx"):
-            big(t, c[1], p[0], 1, p[1])
-        elif c in ("ho", "hg", "hx"):
-            big(t, c[1], 2 * p[0], 2, p[1])
+            big(t, c[1], *p)
         elif c in ("to", "tg", "tx"):
             test(t, c[1], *p)
         elif c == "ol":
-            ts(T.O[:, part(*p)], T.ch[:, part(*p)], float(C0), ALU.add, r=nm(*p, "ch"), w=nm(*p, "O"))
+            if h == "c":
+                ts(T.O[:], T.ch[:], float(C0), ALU.add, r=["ch"], w=["O"], f=0.5)
+            else:
+                lists(t, h, T.O[:], times(t, 2), nm(2, "WL%d" % t), ["O"], float(C0))
+        elif c == "ch":
+            lists(t, h, T.ch[:], times(t, 2), nm(2, "WL%d" % t), ["ch"])
+        elif c == "rr":
+            ts(T.rr[:], T.ch[:], float(C0 - 1), ALU.is_ge, float(-V), ALU.mult, r=["ch"], w=["rr"], f=0.5)
         elif c == "cg":
-            copy(p[1], T.cg[:, part(p[0])], T.Rt[:].indirect(T.Oin[:, part(p[0], 8, (t - 1) * MW + 256)]), RT, nm(p[0], "cg"), (), arrived(t))
-        elif c[0] == "c" and c[1].isdigit():
-            chain(t, p[0], int(c[1]))
-        elif c[0] == "k":
-            claim(p[0], int(c[1]))
-        elif c == "tw":
+            lists(t, h, T.cg[:], T.Oin[:, hs(0, 16, (t - 1) * MW + 256)], [], ["cg"], 0.0, arrived(t))
+        elif c == "cv":
+            for i in range(NCH if t == 1 else 0):
+                line("a", T.Rt[:, hs(i, cw)], T.recs[:, hs(i, cw)], 1.0, float(-C0), ["recs%d" % i], ["Rt%d" % i])
+        elif c == "wl":
+            line(p[1], times(t + 1, h), reg("Z", h), 1.0, float(C0 + 1), slots(h, "Z"), nm(h, "WL%d" % (t + 1)), bk(h))
+        elif c == "zc":
+            line(p[1], T.zc[:, part(h, 8)], reg("Z", h), 1.0, 1.0, slots(h, "Z"), nm(h, "zc"), bk(h))
             turned(t + 1)
-        elif c == "re":
-            if t == 1:
-                rest()
-        elif c in ("ch", "os", "rp", "od", "ex", "fo", "ys"):
-            {"ch": names, "os": ask, "rp": reply, "od": older, "ex": expo, "fo": fold, "ys": ystore}[c](t, *p)
+        elif c == "xz":
+            gather(p[1], T.xz[:, part(h)], T.xa[:], times(t + 1, h), ["xa"] + nm(h, "WL%d" % (t + 1)), nm(h, "xz"))
+        elif c == "od":
+            lists(t, p[1], T.old[:, part(h)], times(t + 1, h), nm(h, "WL%d" % (t + 1)), nm(h, "old"))
+        elif c == "ed":
+            tt(T.Ed[:, part(h)], T.old[:, part(h)], reg("nP", h), ALU.subtract, nm(h, "old") + slots(h, "nP"), nm(h, "Ed"), bk(h))
+        elif c == "pr":
+            tt(T.pr[:, part(h)], T.Ed[:, part(h)], reg("put", h), ALU.mult, nm(h, "Ed") + slots(h, "put"), nm(h, "pr"), bk(h))
+        elif c == "ys":
+            store(hs(t - 1, 256), T.yl[:, t - 1, :], ext=[("ay%d" % t, narr(helper))])
+        elif c in ("os", "th", "dn", "nk", "ex", "fo"):
+            {"os": ask, "th": reply, "dn": steps, "nk": untwin, "ex": expo, "fo": fold}[c](t, *p)
         else:
-            {"np": after, "zr": spread, "xz": state, "lc": likes, "fl": fall, "ab": absd, "sg": sgn, "pu": put, "da": tail_abs,
+            {"sc": choose, "fs": flag, "eq": claim, "np": after, "ft": near, "ab": absd, "sg": sgn, "pu": put, "da": tail_abs,
              "ts": tail_sum, "st": tail_store, "te": tail_exp, "ta": tail_add}[c](*p)
 
     seq = [(t - w.count("-"), w.strip("-")) for t in range(1, RO + 1) for w in {1: SEQ1, RO: SEQL}.get(t, SEQ).split() if t > w.count("-")]
     for i, (t, w) in enumerate(seq):
         TAG[0] = "%d%s" % (t, w)
         run(t, w)
-        u = unit(w)
-        if u and (t, u) not in [(s, unit(x)) for s, x in seq[i + 1:i + 150]]:
-            free.update(bank.pop(u))
-    emit()
+    if plan:
+        emit()
+    return ops

@@ -3,7 +3,8 @@ from concourse.mybir import AluOpType as ALU, ActivationFunctionType as AF
 
 V, K, RO, TH, NR = 3840, 256, 5, 11, 9
 C0 = V // 2
-RW = V + 16
+NB = 2
+RW = V + 16 * NB
 XO = 15
 MW = 272
 B2 = 1.5 * 2.0 ** 25
@@ -14,7 +15,7 @@ POOL = [0, 1, 2, 3, 4, 5]
 BW = 18
 REG = {"Lg": (0, 128, "A"), "dn": (0, 8 * BW, "AB"), "eq": (0, 128, "A"), "S": (0, 128, "A"), "NC": (128, 128, "B"),
        "put": (128, 128, "B"), "LT": (272, 8 * BW, "D"), "nP": (272, 128, "D"), "Z": (416, 8, "E"), "tg": (424, 8, "F")}
-CYC, PCYC, GATH, SCAT, FIX, SEM, PLAT, HOP, FOLD = 0.83, 0.42, 1.4, 3.0, {"v": 60, "a": 120, "p": 10}, 100, 150, 2200, 16000
+CYC, PCYC, GATH, SCAT, FIX, SEM, PLAT, HOP, FOLD = 0.83, 0.42, 1.5, 3.0, {"v": 60, "a": 120, "p": 3}, 100, 150, 2200, 16000
 IDLE = 1.0
 SPAN = [0]
 TAG = [""]
@@ -30,6 +31,10 @@ SEQL = HEAD + ("Dx12 ab12 ex122 Px102 Dx10 Po002 Do00 to00 No00 dn0 nk0 sc0 wl0v
 SEQ1 = 'cha osv gg2v olv -ex104 go2a cga go3v gg3a Pg122 Pg102 Po122 Dg12 gg0a Do12 -fo to12 gg1a tg12 Po102 gx0v Dg10 go1a tg10 Pg022 Ng12 Dg02 rr Do10 to10 Pg002 No12 gx1a tg02 No10 go0a Ng10 Po022 th1a Dg00 Do02 tg00 dn1 Ng02 Po002 gx3a Ng00 nk1 gx2a sc1 th0a wl1a xz1a to02 Px122 No02 Do00 dn0 ys-- to00 Px102 Dx10 No00 nk0 tx10 Dx12 sc0 wl0v ab12 Px002 Nx10 xz0v -ex004 Dx00 Px022 Dx02 fs2a np2 sg122 od2v Nx12 eq2 ed2 ft1v tx00 tx02 Nx02 ab00 Nx00 ab10 cv ft0v pr0 pr1 pu1 pu0 zc2v ab02'
 SEQ = 'chv ola go2a go3v Po102 osv Po122 Do12 go1a gg2v cga gx2a to12 gg3a Do10 gg1a Pg102 to10 Pg122 gg0a Po022 go0v rr Dg12 Dg10 Do02 tg12 No12 Ng12 tg10 Pg022 Ng10 th1v Dg02 Pg002 gx3a No10 dn1 nk1 Dg00 ys-- to02 Po002 tg02 tg00 Ng02 No02 sc1 wl1v gx0a Ng00 Px102 -ex104 Do00 xz1v to00 Px122 Dx12 -ex004 th0v Dx10 tx10 No00 gx1a ab12 dn0 nk0 sg122 sc0 fs2v wl0a Px002 xz0a Dx00 np2 Nx10 Nx12 tx00 Px022 od2a Dx02 Nx00 tx02 eq2 Nx02 ft1v ed2 ab00 ab10 -fo pr1 ab02 pu1 cv ft0a pr0 zc2v pu0'
 SEQL = 'cha olv -ex004 osv cga Pg022 gg0v gg1a Dg02 tg02 Po122 gg2a Pg102 Pg122 gg3a go2a go3v go0v Dg10 Dg12 Do12 -ex104 tg10 gx1a cv to12 Pg002 gx2a Ng10 gx3a Dg00 rr tg12 Ng12 th1v tg00 Po102 No12 Do10 Po022 to10 go1v Do02 Po002 Ng02 dn1 Ng00 No10 nk1 sc1 th0a Do00 to02 wl1a xz1a dn0 to00 ys-- No00 Px122 gx0a Dx12 No02 ab12 ex122 nk0 -fo sc0 Px102 wl0v Dx10 Px001 Px021 Px011 xz0v ab10 Dx01 Dx00 ys- ex102 Dx02 ts10 ab00 ts11 da02 Px031 ts12 ab01 te00 Dx03 ts13 da03 te01 st1a te02 te03 ta0'
+SEQ1 = 'cha olc go3a osv cga Pg102 Po122 Po102 gx0v go2a Do10 gg2v Do12 gg3a go1v gg0a gx3a gg1v to10 to12 Pg002 Pg122 Dg10 tg10 Dg12 Pg022 No12 Dg00 tg12 No10 Ng12 Po022 Ng10 tg00 Po002 go0a th1a Ng00 rr Dg02 tg02 Ng02 gx2a Do02 Do00 to02 th0a to00 Px102 nk1 dn1 No02 No00 sc1 dn0 gx1a nk0 sc0 wl0v fs2a wl1a xz1a Px122 Px022 od2v Dx12 ab12 eq20 Px002 xz0a Dx00 tx00 np2 Dx02 Dx10 tx10 cv Nx00 tx02 Nx02 ft0a eq21 ed2 ai1 sg122 ab10 pr0 Nx12 Nx10 ft1a pr1 ab02 pu1 zc2v ab00 ai0 pu0'
+SEQ = 'chv osv cga Pg122 gg2a gg1a Po102 olc go3v gg3v Dg12 -ex102 Po122 -ex022 go2a gg0a Do12 to12 tg12 Do10 Pg102 Pg022 Dg10 Ng12 go0a tg10 Ng10 go1v Pg002 th1v rr No12 Dg02 Dg00 to10 -ex122 dn1 No10 tg02 Po022 nk1 tg00 Ng00 Do02 sc1 gx2a Ng02 Po002 Do00 wl1a -ex002 gx3a th0v to02 xz1a No02 Px102 Dx10 to00 dn0 cv No00 tx10 -fo nk0 gx1a Px122 sc0 wl0v np2 fs2v Dx12 eq20 Nx10 gx0a ab12 xz0v eq21 Px022 od2a Dx02 Px002 tx02 Dx00 ed2 sg122 Nx02 tx00 Nx00 ft0a Nx12 ft1a ys-- ab02 pr0 ab10 ai0 ai1 ab00 pr1 pu1 pu0 zc2v'
+SEQL = '-ex122 chv osv -ex102 -ex022 -ex002 -fo cga Pg122 gg2a gg1a Po102 olc go3v gg3v Dg12 Po122 go2v gg0a Do12 to12 tg12 Do10 Pg102 Pg022 Dg10 Ng12 go0a tg10 Ng10 go1v Pg002 th1v rr No12 Dg02 Dg00 to10 dn1 No10 tg02 Po022 nk1 tg00 Ng00 Do02 sc1 gx2a Ng02 Po002 Do00 wl1a gx3a th0v to02 xz1a No02 Px102 Dx10 to00 dn0 No00 nk0 gx1a Px122 sc0 wl0v Dx12 ab12 ex122 xz0v ys-- gx0a ab10 ex102 Px001 Px021 Px011 Dx01 Dx00 ys- Dx02 ts10 ab00 ts11 da02 Px031 ts12 ab01 te00 Dx03 ts13 da03 te01 st1a te02 te03 ta0'
+SPLIT = False
 
 SCRATCH = {
     "recs": ("sbuf", [128, V], "int32"), "Rt": ("sbuf", [128, RW], "float32"),
@@ -45,16 +50,16 @@ SCRATCH = {
     "U": ("sbuf", [128, 16 * BW], "float32"), "F": ("sbuf", [128, 16 * BW], "bfloat16"), "H": ("sbuf", [128, 256], "float16"),
     "uf": ("sbuf", [128, 16], "float32"), "ub": ("sbuf", [128, 256], "float32"), "LU": ("sbuf", [128, 16], "uint16"),
     "rw": ("sbuf", [128, 16], "float16"), "zc": ("sbuf", [128, 16], "float16"), "u0": ("sbuf", [128, 16], "float32"),
-    "wx": ("sbuf", [128, 256], "float16"), "eq": ("sbuf", [128, 256], "bfloat16"), "fT": ("sbuf", [128, 256], "bfloat16"),
+    "wx": ("sbuf", [128, 256], "float16"), "eq": ("sbuf", [128, 256 * NB], "bfloat16"), "fT": ("sbuf", [128, 256], "bfloat16"),
     "old": ("sbuf", [128, 256], "float32"), "Ed": ("sbuf", [128, 256], "float32"), "pr": ("sbuf", [128, 256], "float32"),
-    "xz": ("sbuf", [128, 256], "bfloat16"), "tg": ("sbuf", [128, 32], "uint16"),
+    "xz": ("sbuf", [128, 256], "bfloat16"), "tg": ("sbuf", [128, 16], "uint16"), "GB": ("sbuf", [128, 8 * NB], "bfloat16"),
     "ng": ("sbuf", [128, 512], "float32"), "acc": ("sbuf", [128, 512], "float32"), "yt": ("sbuf", [128, 256], "float32"),
     "fl": ("sbuf", [128, RO, 256], "float32"), "yl": ("sbuf", [128, RO, 256], "float32"),
-    "pi": ("sbuf", [128, 1], "int32"), "pa": ("sbuf", [128, 1], "int32"), "col": ("sbuf", [128, 8], "float32"),
+    "pi": ("sbuf", [128, 1], "int32"), "pa": ("sbuf", [128, 1], "int32"), "col": ("sbuf", [128, 16], "float32"),
     "c16": ("sbuf", [128, 16], "float32"), "LD": ("sbuf", [128, 16], "uint16"),
-    "ck": ("sbuf", [128, 256], "bfloat16"), "q": ("sbuf", [128, 256], "bfloat16"), "q16": ("sbuf", [128, 128], "bfloat16"),
+    "ck": ("sbuf", [128, 256], "bfloat16"), "q": ("sbuf", [128, 256], "bfloat16"), "q16": ("sbuf", [128, 256], "bfloat16"),
     "one": ("sbuf", [128, 128], "bfloat16"), "G": ("sbuf", [128, 40], "bfloat16"), "I": ("sbuf", [128, 256], "bfloat16"),
-    "blk": ("sbuf", [128, 128], "bfloat16"), "If": ("sbuf", [128, 128], "float32"), "In": ("sbuf", [128, 128], "bfloat16"),
+    "blk": ("sbuf", [128, 256], "bfloat16"), "If": ("sbuf", [128, 128], "float32"), "In": ("sbuf", [128, 128], "bfloat16"),
     "Ih": ("sbuf", [128, 128], "bfloat16"),
     "Mi": ("sbuf", [128, 256], "float32"), "Mk": ("sbuf", [128, 128], "bfloat16"), "Dt": ("sbuf", [128, RO, 8, BW], "bfloat16"),
     "ps": ("psum", [128, 8, 512], "float32"),
@@ -374,7 +379,7 @@ def group_program(g, core, rank, helper, T, topo, plan):
         return T.I[:, s:s + 128]
 
     Id = T.I[:, 0:128]
-    MARK, SIGNS, MORE, MISS = 0, 16, 24, 32
+    MARK, SIGNS, MISS = 0, 16, 24
 
     def marks(s):
         return T.G[:, s:s + 8]
@@ -390,7 +395,7 @@ def group_program(g, core, rank, helper, T, topo, plan):
     dma("s", T.xa[:], T.x[:], "lx2", 16, 3000, r=["xe1"], w=["xa"])
     op("g", lambda: g.iota(T.pi[:], [[0, 1]], 0, 1), 130, (), ["pi"])
     iota(T.q[:], [[0, 2], [1, 128]], "q")
-    iota(T.q16[:], [[16, 8], [0, 16]], "q16")
+    iota(T.q16[:], [[16, 16], [0, 16]], "q16")
     iota(T.ck[:], [[0, 16], [1, 16]], "ck")
     iota(T.c16[:], [[1, 16]], "c16")
     iota(T.Rt[:, V:RW], [[0, RW - V]], "Rtb")
@@ -399,16 +404,20 @@ def group_program(g, core, rank, helper, T, topo, plan):
     ts(T.pa[:], T.pi[:], 15, ALU.bitwise_and, r=["pi"], w=["pa"])
     line("v", C[:, 0:1], T.pi[:], 1.0, 0.0, ["pi"], ["c0"])
     line("v", pk, T.pa[:], 1.0, 0.0, ["pa"], ["pk"])
-    line("v", C[:, 3:4], T.pa[:], 1.0, float(V), ["pa"], ["c3"])
+    ts(C[:, 8:16], T.q16[:, 0:128:16], pk, ALU.add, float(V), ALU.add, r=["q16", "pk"], w=["c8"])
     tt(C[:, 4:5], C[:, 0:1], pk, ALU.subtract, ["c0", "pk"], ["c4"])
     ts(T.blk[:], T.q16[:], C[:, 4:5], ALU.is_equal, r=["q16", "c4"], w=["blk"])
     ts(T.I[:], T.q[:], C[:, 0:1], ALU.is_equal, r=["q", "c0"], w=["I"])
-    act(T.one[:], T.q16[:], AF.Exp, scale=0.0, r=["q16"], w=["one"])
+    act(T.one[:], T.q16[:, 0:128], AF.Exp, scale=0.0, r=["q16"], w=["one"])
     for x, src, sc in (("In", "I", -1.0), ("If", "I", 1.0), ("Ih", "I", 0.5)):
         line("a", T[x][:], T[src][:, 0:128], sc, 0.0, [src], [x])
-    for i, sc in enumerate((1.0, 1.0, NR / (2.0 * NR - 16), BIG, 1.0 / (16.5 - TH))):
-        line("a", marks(8 * i), T.blk[:, 0::16], sc, 0.0, ["blk"], ["G%d" % i])
-    GS = ["G%d" % i for i in range(5)]
+    for i, sc in enumerate((1.0, 1.0, NR / (2.0 * NR - 16), 1.0 / (16.5 - TH))):
+        line("a", marks(8 * i), T.blk[:, 0:128:16], sc, 0.0, ["blk"], ["G%d" % i])
+    GS = ["G%d" % i for i in range(4)]
+    op("v", lambda: v.memset(T.GB[:], 0.0), FIX["v"], (), ["GB"])
+    for d in range(NB):
+        for i in range(d, NB):
+            line("a", T.GB[:, 8 * d + i:8 * d + 8:NB], T.blk[:, 16 * (i - d):128:16 * NB], BIG, 0.0, ["blk"], ["GB"])
     for x, ap, c in (("e0", T.e0[:], 0.0), ("e0", T.e0[:, 0::BW], BIG), ("Dt", T.Dt[:], 0.0), ("#D", T.ps[:, 6:8, 272:416], 0.0),
                      ("rep", T.rep[:, :, 0], BIG), ("rep", T.rep[:, :, BW - 1], -BIG)):
         op("v", lambda ap=ap, c=c: v.memset(ap, c), cost("v", ap, 0.5), (), nm(2, x), bk(2) if x == "#D" else ())
@@ -492,6 +501,15 @@ def group_program(g, core, rank, helper, T, topo, plan):
                 calls, rd = [(T.In[:], T[small][:, hs(h)])] * 4, ["xz%d" % h if p == "x" else small]
             w = ["%s.%d" % (key, i)]
             b = (plan[1][key] if plan else 0) + i
+            if SPLIT:
+                if (p == "x") == (n > 0):
+                    cs = [(T.ps[:, b, hs(2 * k + y, 64)], Id, T[wide][:, 2048 * h + 1024 * y + 4 * (j + i) + k:2048 * h + 1024 * (y + 1):16])
+                          for k in range(4) for y in range(2)]
+                else:
+                    cs = [(T.ps[:, b, hs(2 * k + y, 64)], T.In[:], T[small][:, hs(2 * h + y, 64)]) for k in range(4) for y in range(2)]
+                mms(cs, ["I", "In"] + rd, w, (key, m, [i]), 1, n > 0, n == 0)
+                ops[-1]["cost"] -= 40
+                continue
             mms([(T.ps[:, b, hs(k)], l, x) for k, (l, x) in enumerate(calls)], ["I", "In"] + rd, w, (key, m, [i]), 1, n > 0, n == 0)
 
     def test(t, p, h, j):
@@ -560,14 +578,19 @@ def group_program(g, core, rank, helper, T, topo, plan):
         tt(T.uf[:, part(h, 8)], chosen(T.U, h), chosen(T.F, h), ALU.add, nm(h, "U", "F"), nm(h, "uf"), f=2)
         gather(e, T.ub[:, part(h)], T.uf[:, part(h, 8)], T.LD[:, 0:8 * len(halves(h))], nm(h, "uf") + ["LD"], nm(h, "ub"))
 
-    def claim(h):
+    def claim(h, d):
         for x in halves(h):
-            mms([(reg("eq", x), T.blk[:], T.H[:, hs(x)]), (reg("eq", x), Id, T.Mk[:])], ["blk", "I", "Mk"] + nm(x, "H"), slots(x, "eq"), bk(x))
-        tt(T.eq[:, part(h)], reg("eq", h), T.ub[:, part(h)], ALU.is_equal, slots(h, "eq") + nm(h, "ub"), nm(h, "eq"), bk(h))
-        for x in halves(h):
-            mms([(reg("tg", x), T.H[:, hs(x)], marks(MARK)), (reg("tg", x), T.eq[:, hs(x)], marks(MORE))], GS + nm(x, "H", "eq"), slots(x, "tg"), bk(x))
-        s = part(h, 16)
-        ts(T.tg[:, s.start:s.stop:2], reg("tg", h), float(C0 + 1), ALU.add, C[:, 3:4], ALU.min, r=slots(h, "tg") + ["c3"], w=nm(h, "tg"), banks=bk(h))
+            calls = [(T.blk[:, 16 * d:16 * d + 128], T.H[:, hs(x)])] + [(Id, T.Mk[:])] * (d == 0)
+            mms([(reg("eq", x), l, r) for l, r in calls], ["blk", "I", "Mk"] + nm(x, "H"), slots(x, "eq"), bk(x))
+        tt(T.eq[:, part(h, 128, 256 * d)], reg("eq", h), T.ub[:, part(h)], ALU.is_equal, slots(h, "eq") + nm(h, "ub"), nm(h, "eq%d" % d), bk(h))
+
+    def target(h):
+        mms([(reg("tg", h), T.H[:, hs(h)], marks(MARK))] + [(reg("tg", h), T.eq[:, hs(h, 128, 256 * d)], T.GB[:, hs(d, 8)]) for d in range(NB)],
+            GS + ["GB"] + nm(h, "H", *["eq%d" % d for d in range(NB)]), slots(h, "tg"), bk(h))
+        o = REG["tg"][0]
+        for i in range(NB):
+            ts(T.tg[:, 8 * h + i:8 * h + 8:NB], T.ps[:, 6 + h, o + i:o + 8:NB], float(C0 + 1), ALU.add, C[:, 8 + i:9 + i], ALU.min,
+               r=slots(h, "tg") + ["c8"], w=["tg%d%d" % (h, i)], banks=bk(h))
 
     def after(h):
         for x in halves(h):
@@ -580,9 +603,9 @@ def group_program(g, core, rank, helper, T, topo, plan):
             mms([(reg("put", x), l, r) for l, r in calls], ["I", "Ih", "one"] + nm(x, "fT"), slots(x, "put"), bk(x))
 
     def put(h):
-        for b in range(8 * h + 7, 8 * h - 1, -1):
-            tt(T.Rt[:].indirect(T.tg[:, 2 * b:2 * b + 1]), T.old[:, hs(b, 16)], T.pr[:, hs(b, 16)], ALU.subtract,
-               nm(h, "tg", "pr", "old") + ["Rtb"] + ["Rt%d" % i for i in range(NCH)], ["Rt"], f=SCAT)
+        for b in range(8 * (h + 1) // NB - 1, 8 * h // NB - 1, -1):
+            tt(T.Rt[:].indirect(T.tg[:, hs(b, NB)]), T.old[:, hs(b, 16 * NB)], T.pr[:, hs(b, 16 * NB)], ALU.subtract,
+               nm(h, "pr", "old") + ["tg%d%d" % (h, i) for i in range(NB)] + ["Rtb"] + ["Rt%d" % i for i in range(NCH)], ["Rt"], f=SCAT)
 
     def absd(h, j):
         d, rd, bs = piece(("x", h, j))
@@ -600,6 +623,9 @@ def group_program(g, core, rank, helper, T, topo, plan):
         raised["ay%d" % t] = (len(ops), 2 * HOP)
         op("g", lambda: g.remote_dma_fused(trs, local_sem=T.sem["sf%d" % t]), 500, sub("ex%d" % (t % 2), 0, 0, 4) + sub("ex%d" % (t % 2), 1, 0, 4),
            (), tok=("sf%d" % t, len(en)), lat=FOLD)
+        if t > 1 and not SPLIT:
+            ops[-1]["far"].append((raised["ay%d" % (t - 1)][0], 0.0))
+            ops[-1]["soft"] = [("ay%d" % (t - 1), 0.0)]
 
     nys = [0]
 
@@ -686,7 +712,7 @@ def group_program(g, core, rank, helper, T, topo, plan):
         elif c in ("os", "th", "dn", "nk", "ex", "fo"):
             {"os": ask, "th": reply, "dn": steps, "nk": untwin, "ex": expo, "fo": fold}[c](t, *p)
         else:
-            {"sc": choose, "fs": flag, "eq": claim, "np": after, "ft": near, "ab": absd, "sg": sgn, "pu": put, "da": tail_abs,
+            {"sc": choose, "fs": flag, "eq": claim, "ai": target, "np": after, "ft": near, "ab": absd, "sg": sgn, "pu": put, "da": tail_abs,
              "ts": tail_sum, "st": tail_store, "te": tail_exp, "ta": tail_add}[c](*p)
 
     seq = [(t - w.count("-"), w.strip("-")) for t in range(1, RO + 1) for w in {1: SEQ1, RO: SEQL}.get(t, SEQ).split() if t > w.count("-")]

@@ -10,31 +10,32 @@ MW = 272
 B2 = 1.5 * 2.0 ** 25
 BH = 1.5 * 2.0 ** 23
 BIG = 8192.0
-NCH = 4
+CUTS = [0, 960, 1920, 2880, V]
+NCH = len(CUTS) - 1
 POOL = [0, 1, 2, 3, 4, 5]
 BW = 18
-REG = {"Lg": (0, 128, "A"), "dn": (0, 8 * BW, "AB"), "eq": (0, 128, "A"), "S": (0, 128, "A"), "NC": (128, 128, "B"),
+REG = {"Lg": (0, 128, "A"), "dn": (0, 8 * BW, "AB"), "eq": (0, 128, "A"), "S": (0, 128, "A"), "NC": (128, 128, "B"), "xt": (144, 128, "B"),
        "put": (128, 128, "B"), "LT": (272, 8 * BW, "D"), "nP": (272, 128, "D"), "Z": (416, 8, "E"), "tg": (424, 8, "F")}
-CYC, PCYC, GATH, SCAT, FIX, SEM, PLAT, HOP, FOLD = 0.83, 0.42, 1.5, 3.0, {"v": 60, "a": 120, "p": 3}, 100, 150, 2200, 16000
-IDLE = 1.0
-SPAN = [0]
+FOLDS = {1: (1, 2), 2: (1, 2), 3: (1, 2), 4: (2, 1)}
 TAG = [""]
 
-HEAD = ("olv cha osv rr go3a go2v go1a Po122 Do12 cga gg3a gg2v gg0v gg1a to12 No12 Pg122 Dg12 tg12 Ng12 Pg102 Dg10 tg10 Ng10 th1v "
-        "Pg022 Dg02 tg02 Ng02 Pg002 Dg00 tg00 Ng00 th0v go0a gx3a gx2a -ex104 -ex004 -fo ys-- Po102 Do10 to10 No10 dn1 Px122 nk1 sc1 wl1v xz1v "
-        "gx1a gx0a cv Po022 Do02 to02 No02 ")
-SEQ = HEAD + ("Dx12 ab12 sg122 Nx12 Px102 Dx10 Po002 Do00 to00 No00 dn0 nk0 sc0 wl0v xz0v tx10 Nx10 ab10 Px022 Dx02 Px002 Dx00 fs2a od2a np2 ed2 "
-              "eq2 zc2a tx02 Nx02 ft1v pr1 tx00 Nx00 ft0v pr0 pu1 pu0 ab02 ab00")
-SEQ1 = SEQ
-SEQL = HEAD + ("Dx12 ab12 ex122 Px102 Dx10 Po002 Do00 to00 No00 dn0 nk0 sc0 wl0v xz0v ab10 ex102 Px001 Px011 Px021 Px031 ts12 ts13 ts10 ts11 "
-               "st1a Dx00 ab00 te00 Dx01 Dx02 Dx03 da02 da03 ab01 te01 te02 te03 ys- ta0")
-SEQ1 = 'cha osv gg2v olv -ex104 go2a cga go3v gg3a Pg122 Pg102 Po122 Dg12 gg0a Do12 -fo to12 gg1a tg12 Po102 gx0v Dg10 go1a tg10 Pg022 Ng12 Dg02 rr Do10 to10 Pg002 No12 gx1a tg02 No10 go0a Ng10 Po022 th1a Dg00 Do02 tg00 dn1 Ng02 Po002 gx3a Ng00 nk1 gx2a sc1 th0a wl1a xz1a to02 Px122 No02 Do00 dn0 ys-- to00 Px102 Dx10 No00 nk0 tx10 Dx12 sc0 wl0v ab12 Px002 Nx10 xz0v -ex004 Dx00 Px022 Dx02 fs2a np2 sg122 od2v Nx12 eq2 ed2 ft1v tx00 tx02 Nx02 ab00 Nx00 ab10 cv ft0v pr0 pr1 pu1 pu0 zc2v ab02'
-SEQ = 'chv ola go2a go3v Po102 osv Po122 Do12 go1a gg2v cga gx2a to12 gg3a Do10 gg1a Pg102 to10 Pg122 gg0a Po022 go0v rr Dg12 Dg10 Do02 tg12 No12 Ng12 tg10 Pg022 Ng10 th1v Dg02 Pg002 gx3a No10 dn1 nk1 Dg00 ys-- to02 Po002 tg02 tg00 Ng02 No02 sc1 wl1v gx0a Ng00 Px102 -ex104 Do00 xz1v to00 Px122 Dx12 -ex004 th0v Dx10 tx10 No00 gx1a ab12 dn0 nk0 sg122 sc0 fs2v wl0a Px002 xz0a Dx00 np2 Nx10 Nx12 tx00 Px022 od2a Dx02 Nx00 tx02 eq2 Nx02 ft1v ed2 ab00 ab10 -fo pr1 ab02 pu1 cv ft0a pr0 zc2v pu0'
-SEQL = 'cha olv -ex004 osv cga Pg022 gg0v gg1a Dg02 tg02 Po122 gg2a Pg102 Pg122 gg3a go2a go3v go0v Dg10 Dg12 Do12 -ex104 tg10 gx1a cv to12 Pg002 gx2a Ng10 gx3a Dg00 rr tg12 Ng12 th1v tg00 Po102 No12 Do10 Po022 to10 go1v Do02 Po002 Ng02 dn1 Ng00 No10 nk1 sc1 th0a Do00 to02 wl1a xz1a dn0 to00 ys-- No00 Px122 gx0a Dx12 No02 ab12 ex122 nk0 -fo sc0 Px102 wl0v Dx10 Px001 Px021 Px011 xz0v ab10 Dx01 Dx00 ys- ex102 Dx02 ts10 ab00 ts11 da02 Px031 ts12 ab01 te00 Dx03 ts13 da03 te01 st1a te02 te03 ta0'
-SEQ1 = 'cha olc go3a osv cga Pg102 Po122 Po102 gx0v go2a Do10 gg2v Do12 gg3a go1v gg0a gx3a gg1v to10 to12 Pg002 Pg122 Dg10 tg10 Dg12 Pg022 No12 Dg00 tg12 No10 Ng12 Po022 Ng10 tg00 Po002 go0a th1a Ng00 rr Dg02 tg02 Ng02 gx2a Do02 Do00 to02 th0a to00 Px102 nk1 dn1 No02 No00 sc1 dn0 gx1a nk0 sc0 wl0v fs2a wl1a xz1a Px122 Px022 od2v Dx12 ab12 eq20 Px002 xz0a Dx00 tx00 np2 Dx02 Dx10 tx10 cv Nx00 tx02 Nx02 ft0a eq21 ed2 ai1 sg122 ab10 pr0 Nx12 Nx10 ft1a pr1 ab02 pu1 zc2v ab00 ai0 pu0'
-SEQ = 'chv osv cga Pg122 gg2a gg1a Po102 olc go3v gg3v Dg12 -ex102 Po122 -ex022 go2a gg0a Do12 to12 tg12 Do10 Pg102 Pg022 Dg10 Ng12 go0a tg10 Ng10 go1v Pg002 th1v rr No12 Dg02 Dg00 to10 -ex122 dn1 No10 tg02 Po022 nk1 tg00 Ng00 Do02 sc1 gx2a Ng02 Po002 Do00 wl1a -ex002 gx3a th0v to02 xz1a No02 Px102 Dx10 to00 dn0 cv No00 tx10 -fo nk0 gx1a Px122 sc0 wl0v np2 fs2v Dx12 eq20 Nx10 gx0a ab12 xz0v eq21 Px022 od2a Dx02 Px002 tx02 Dx00 ed2 sg122 Nx02 tx00 Nx00 ft0a Nx12 ft1a ys-- ab02 pr0 ab10 ai0 ai1 ab00 pr1 pu1 pu0 zc2v'
-SEQL = '-ex122 chv osv -ex102 -ex022 -ex002 -fo cga Pg122 gg2a gg1a Po102 olc go3v gg3v Dg12 Po122 go2v gg0a Do12 to12 tg12 Do10 Pg102 Pg022 Dg10 Ng12 go0a tg10 Ng10 go1v Pg002 th1v rr No12 Dg02 Dg00 to10 dn1 No10 tg02 Po022 nk1 tg00 Ng00 Do02 sc1 gx2a Ng02 Po002 Do00 wl1a gx3a th0v to02 xz1a No02 Px102 Dx10 to00 dn0 No00 nk0 gx1a Px122 sc0 wl0v Dx12 ab12 ex122 xz0v ys-- gx0a ab10 ex102 Px001 Px021 Px011 Dx01 Dx00 ys- Dx02 ts10 ab00 ts11 da02 Px031 ts12 ab01 te00 Dx03 ts13 da03 te01 st1a te02 te03 ta0'
-SPLIT = False
+STAGES = ("aw dt cv ch ol rr os se cg go gg gx Po Do to No Pg Dg tg Ng th dn nk sc rw wl zc xz xt Px Dx tx ab da sg Nx fs eq ai od np ed ft pr pu "
+          "ex ts st fo ys").split()
+SEQ1 = ("dt aw cv1a cv0v cv2a chv osv ol os:2 dt:2 Po122 Po102 go2a go3v Do10 go1a rr cgv to10 Do12 Pg102 gg2a gg3v gg4a to12 No10 Pg122 Dg12 tg12 "
+        "Dg10 tg10 Pg022 Ng12 Pg002 Ng10 Dg02 th1v Dg00 go0a Po022 Do02 tg02 dn1 No12 tg00 nk1 Ng02 sc1 gx5a Ng00 th0a Po002 Do00 sc1:2 sc1:3 to02 "
+        "dn0 Px102 wl1a xz1v to00 Dx10 No02 gx4a Px122 No00 Dx12 tx10 nk0 sc0 Nx10 np2 sc0:2 eq20 fs2v fs2:2 fs2:3 ab12 sc0:3 wl0v xz0a sg122 eq20:3 "
+        "Px022 eq21 ab10 Dx02 od2v eq21:3 ed2 Px002 Dx00 Nx12 ft1a tx02 Nx02 ft1:2 tx00 cv3a ai2 ai2:3 pr1 pu1 Nx00 ab02 rw2 ft0v pu1:2 pu1:3 ft0:2 "
+        "pr0 pu1:4 pu0 pu0:2 pu0:3 pu0:4 zc2v zc2:2")
+SEQ = ("-ab00 chv ol -ex022 osv os:2 -ex102 go3v Po122 go2a Do12 go0a Po102 Do10 cga Pg122 go1v gg2a gg3v Dg12 to12 Pg102 Dg10 rr No12 tg12 Pg022 "
+       "Ng12 gg4a Dg02 se tg10 to10 Ng10 th1v tg02 Pg002 Dg00 Po022 tg00 -ex002 -ex122 gx3a dn1 No10 nk1 Ng02 sc1 sc1:2 gx2a -fo Do02 Ng00 th0v Po002 "
+       "sc1:3 --ysv wl1a xz1a Do00 to02 Px102 to00 gx4a Dx10 dn0 tx10 No02 No00 nk0 Px122 Dx12 ab12 sc0 fs2v Nx10 np2 sc0:2 sc0:3 eq20 Px022 fs2:2 "
+       "fs2:3 wl0v eq20:3 od2v xz0a eq21 eq21:3 ed2 sg122 Dx02 tx02 Px002 Dx00 tx00 Nx12 ai0 ab10 ft1a ai1 ft1:2 ai1:2 pr1 pu1 Nx02 Nx00 ft0v ab02 "
+       "pu1:2 pu1:3 ft0:2 pr0 ai0:2 pu1:4 pu0 pu0:2 pu0:3 rw2 pu0:4 zc2v zc2:2")
+SEQL = ("-ab00 -ex022 chv osv ol -ex002 os:2 -ex104 -fo go5v Po102 cga Po122 Do12 Pg122 gg2a gg3v Dg12 to12 Pg102 Dg10 go0a Do10 rr tg12 tg10 Ng12 "
+        "Pg022 Ng10 Po002 to10 No12 gg4a gx3v Dg02 Pg002 Dg00 th1a dn1 tg02 tg00 No10 nk1 go1a Po022 Do02 sc1 sc1:2 Ng00 Ng02 sc1:3 th0v to02 Do00 "
+        "wl1v dn0 gx2a Px102 No02 gx1a xz1a to00 Px122 xt1v No00 xt1:2 Dx12 nk0 gx0a sc0 sc0:2 sc0:3 wl0v xz0v Dx10 ab12 xt0v Px011 Px001 ex122 xt0:2 "
+        "Dx01 Dx00 Px021 ab00 Px031 Dx03 Dx02 da10 da10:2 da02 da02:2 da03 da03:2 ts122 ex001 ts001 --ysv ex102 ts102 ab01 ex021 ts021 ex011 ts011 "
+        "ex031 st1v -ysv ts031 st0a")
 
 SCRATCH = {
     "recs": ("sbuf", [128, V], "int32"), "Rt": ("sbuf", [128, RW], "float32"),
@@ -46,25 +47,25 @@ SCRATCH = {
     "do": ("sbuf", [128, 4096], "bfloat16"), "dg": ("sbuf", [128, 4096], "bfloat16"), "dx": ("sbuf", [128, 4096], "bfloat16"),
     "ad": ("sbuf", [128, 4096], "float32"), "ex": ("sbuf", [128, 32, 256], "float32"),
     "rep": ("sbuf", [128, RO * 16, BW], "bfloat16"), "repin": ("sbuf", [128, RO * 16 * BW], "bfloat16"),
-    "nk": ("sbuf", [128, 16 * BW], "bfloat16"), "e0": ("sbuf", [128, 16 * BW], "bfloat16"),
-    "U": ("sbuf", [128, 16 * BW], "float32"), "F": ("sbuf", [128, 16 * BW], "bfloat16"), "H": ("sbuf", [128, 256], "float16"),
-    "uf": ("sbuf", [128, 16], "float32"), "ub": ("sbuf", [128, 256], "float32"), "LU": ("sbuf", [128, 16], "uint16"),
+    "nk": ("sbuf", [128, 16 * BW], "bfloat16"), "U": ("sbuf", [128, 16 * BW], "float32"), "H": ("sbuf", [128, 256], "float16"),
+    "F": ("sbuf", [128, 16 * BW], "bfloat16"), "e0": ("sbuf", [128, 16 * BW], "bfloat16"), "uf": ("sbuf", [128, 16], "float32"),
+    "KC": ("sbuf", [128, 8], "float16"), "ub": ("sbuf", [128, 256], "float32"), "LU": ("sbuf", [128, 16], "uint16"),
     "rw": ("sbuf", [128, 16], "float16"), "zc": ("sbuf", [128, 16], "float16"), "u0": ("sbuf", [128, 16], "float32"),
     "wx": ("sbuf", [128, 256], "float16"), "eq": ("sbuf", [128, 256 * NB], "bfloat16"), "fT": ("sbuf", [128, 256], "bfloat16"),
     "old": ("sbuf", [128, 256], "float32"), "Ed": ("sbuf", [128, 256], "float32"), "pr": ("sbuf", [128, 256], "float32"),
     "xz": ("sbuf", [128, 256], "bfloat16"), "tg": ("sbuf", [128, 16], "uint16"), "GB": ("sbuf", [128, 8 * NB], "bfloat16"),
-    "ng": ("sbuf", [128, 512], "float32"), "acc": ("sbuf", [128, 512], "float32"), "yt": ("sbuf", [128, 256], "float32"),
-    "fl": ("sbuf", [128, RO, 256], "float32"), "yl": ("sbuf", [128, RO, 256], "float32"),
+    "xt": ("sbuf", [128, 256], "bfloat16"), "ng": ("sbuf", [128, 1024], "float32"), "yt": ("sbuf", [128, RO, 256], "float32"),
+    "fl": ("sbuf", [128, RO - 1, 512], "float32"), "yl": ("sbuf", [128, RO - 1, 512], "float32"),
     "pi": ("sbuf", [128, 1], "int32"), "pa": ("sbuf", [128, 1], "int32"), "col": ("sbuf", [128, 16], "float32"),
     "c16": ("sbuf", [128, 16], "float32"), "LD": ("sbuf", [128, 16], "uint16"),
     "ck": ("sbuf", [128, 256], "bfloat16"), "q": ("sbuf", [128, 256], "bfloat16"), "q16": ("sbuf", [128, 256], "bfloat16"),
     "one": ("sbuf", [128, 128], "bfloat16"), "G": ("sbuf", [128, 40], "bfloat16"), "I": ("sbuf", [128, 256], "bfloat16"),
     "blk": ("sbuf", [128, 256], "bfloat16"), "If": ("sbuf", [128, 128], "float32"), "In": ("sbuf", [128, 128], "bfloat16"),
-    "Ih": ("sbuf", [128, 128], "bfloat16"),
+    "Ih": ("sbuf", [128, 128], "bfloat16"), "Gf": ("sbuf", [128, 8], "float32"), "Sel": ("sbuf", [128, 2048], "bfloat16"),
     "Mi": ("sbuf", [128, 256], "float32"), "Mk": ("sbuf", [128, 128], "bfloat16"), "Dt": ("sbuf", [128, RO, 8, BW], "bfloat16"),
-    "ps": ("psum", [128, 8, 512], "float32"),
+    "ps": ("psum", [128, 6, 512], "float32"), "pz": ("psum", [128, 2, 512], "float32"),
 }
-SEMAPHORES = (["cv", "ca", "cp", "cg", "sent", "lw", "lx0", "lx1", "lx2", "ys"] + ["lr%d" % i for i in range(NCH)]
+SEMAPHORES = (["cv", "ca", "cp", "cg", "sent", "lw", "lx0", "lx1", "lx2", "ys", "aw"] + ["lr%d" % i for i in range(NCH)]
               + ["%s%d" % (n, t) for n in ("ao", "ar0", "ar1", "ar2", "af", "ay", "sf") for t in range(1, RO + 1)])
 
 
@@ -85,6 +86,11 @@ def mask_of(engs):
     return m
 
 
+def fold_engines(topo, src, dst, t):
+    n = FOLDS[t][1]
+    return topo.engines(src, dst)[n - 1::n]
+
+
 def rank_program(g, core, T, topo):
     hp = helpers(T, topo)
     rank = T.rank_of(core)
@@ -99,124 +105,48 @@ def rank_program(g, core, T, topo):
 
 def helper_program(g, core, c, T, topo):
     rid, pid, _ = topo.addr(c)
-    en = topo.engines(core, c)[0::2]
-    nf = len(topo.engines(c, core)[1::2])
+    en = topo.engines(core, c)
     for t in range(1, RO):
-        g.wait_ge(T.sem["af%d" % t], nf)
-        g.remote_dma(T.yl[:, t - 1, :], T.fl[:, t - 1, :], T.sem["ay%d" % t], T.sem.sent, pid, rid, mask_of(en))
+        s = slice(0, 256 * FOLDS[t][0])
+        g.wait_ge(T.sem["af%d" % t], len(fold_engines(topo, c, core, t)))
+        g.remote_dma(T.yl[:, t - 1, s], T.fl[:, t - 1, s], T.sem["ay%d" % t], T.sem.sent, pid, rid, mask_of(en))
     g.wait_ge(T.sem.sent, len(en) * (RO - 1))
 
 
 def order(ops):
-    n = len(ops)
-    users = [[] for _ in ops]
+    seq, placed, given, users = [], set(), {}, {}
+    left = {b: 0 for b in POOL}
     for i, o in enumerate(ops):
-        for d in list(o["deps"]) + [d for d, _ in o["far"]]:
-            users[d].append(i)
-    rank = [0.0] * n
-    for i in range(n - 1, -1, -1):
+        if o["piece"]:
+            users.setdefault(o["piece"][0], []).append(i)
+
+    def place(i):
         o = ops[i]
-        rank[i] += o["cost"] + o["lat"]
-        for d in o["deps"]:
-            rank[d] = max(rank[d], rank[i])
-        for d, late in o["far"]:
-            rank[d] = max(rank[d], rank[i] + late)
-    left = [len(o["deps"]) + len(o["far"]) for o in ops]
-    ready, done, free, out = [i for i in range(n) if not left[i]], [0.0] * n, {}, []
-    bank, pool, given, uses = {b: ("", 0.0) for b in range(8)}, set(POOL), {}, {}
-    for o in ops:
+        for d in o["needs"]:
+            if d not in placed:
+                place(d)
         if o["piece"]:
-            uses[o["piece"][0]] = uses.get(o["piece"][0], 0) + 1
+            u, m, _ = o["piece"]
+            while u not in given:
+                free = [b for b in left if b % m == 0 and all(b + x in left for x in range(m))]
+                if free:
+                    given[u] = min(free, key=lambda b: (max(left[b + x] for x in range(m)), b))
+                    for x in range(m):
+                        del left[given[u] + x]
+                else:
+                    for j in list(users[[x for x in given if users[x]][0]]):
+                        if j not in placed:
+                            place(j)
+            users[u].remove(i)
+            if not users[u]:
+                left.update({given[u] + x: len(seq) for x in range(m)})
+        placed.add(i)
+        seq.append(i)
 
-    def banks(o):
-        if not o["piece"]:
-            return o["banks"]
-        u, m, which = o["piece"]
-        if u not in given:
-            can = [b for b in pool if b % m == 0 and pool >= set(range(b, b + m))]
-            if not can:
-                return None
-            b = min(can, key=lambda b: (max(bank[b + x][1] for x in range(m)), b))
-            return [b + x for x in which]
-        return [given[u] + x for x in which]
-
-    def start(i):
-        o = ops[i]
-        s = [free.get(o["q"], 0.0)] + [done[d] + late for d, late in o["far"]]
-        s += [done[d] for d in o["deps"] if not (o["q"] == "p" == ops[d]["q"])]
-        return max(s + [bank[b][1] for b in banks(o) if bank[b][0] != o["q"]])
-
-    while ready:
-        can = [i for i in ready if banks(ops[i]) is not None]
-        st = {i: start(i) for i in can}
-        first = min(can, key=lambda i: st[i] + ops[i]["cost"])
-        mine = [j for j in can if ops[j]["q"] == ops[first]["q"]]
-        i = max((j for j in mine if st[j] < st[first] + ops[first]["cost"]), key=lambda j: (rank[j], -j))
-        for j in sorted(mine, key=lambda j: -rank[j]):
-            end = st[i] + ops[i]["cost"]
-            if rank[j] > rank[i] and st[j] < end and IDLE * (st[j] - st[i]) < min(end - st[j], rank[j] - rank[i]):
-                fit = [x for x in mine if st[x] + ops[x]["cost"] <= st[j]]
-                i = max(fit, key=lambda x: (rank[x], -x)) if fit else j
-                break
-        o = ops[i]
-        bs = banks(o)
-        if o["piece"]:
-            u, m, which = o["piece"]
-            if u not in given:
-                given[u] = bs[0] - which[0]
-                pool.difference_update(range(given[u], given[u] + m))
-            uses[u] -= 1
-            if not uses[u]:
-                pool.update(range(given[u], given[u] + m))
-        free[o["q"]] = st[i] + o["cost"]
-        done[i] = st[i] + o["cost"] + o["lat"]
-        for b in bs:
-            bank[b] = (o["q"], max(done[i], bank[b][1]))
-        out.append(i)
-        ready.remove(i)
-        for u in users[i]:
-            left[u] -= 1
-            if not left[u]:
-                ready.append(u)
-    return out, given
-
-
-def order(ops):
-    begin, done, busy, held, given, since, uses = [], [], {}, {b: [] for b in range(8)}, {}, {}, {}
-    left = {b: 0.0 for b in POOL}
-    for o in ops:
-        if o["piece"]:
-            uses[o["piece"][0]] = uses.get(o["piece"][0], 0) + 1
-    for o in ops:
-        s = max([0.0] + [done[d] + late for d, late in o["far"]]
-                + [begin[d] + ops[d]["cost"] if o["q"] == "p" == ops[d]["q"] else done[d] for d in o["deps"]])
-        bs = o["banks"]
-        if o["piece"]:
-            u, m, which = o["piece"]
-            if u not in given:
-                given[u] = min((b for b in left if b % m == 0 and all(b + x in left for x in range(m))),
-                               key=lambda b: (max([s] + [left[b + x] for x in range(m)]), b))
-                since[u] = max(left.pop(given[u] + x) for x in range(m))
-            s = max(s, since[u])
-            bs = [given[u] + x for x in which]
-        mine = busy.setdefault(o["q"], [])
-        while True:
-            hit = [e for b, e in mine if b < s + o["cost"] and e > s]
-            hit += [e for x in bs for b, e, q in held[x] if q != o["q"] and b < s + o["cost"] + o["lat"] and e > s]
-            if not hit:
-                break
-            s = min(hit)
-        begin.append(s)
-        done.append(s + o["cost"] + o["lat"])
-        mine.append((s, s + o["cost"]))
-        for x in bs:
-            held[x].append((s, done[-1], o["q"]))
-        if o["piece"]:
-            uses[u] -= 1
-            if not uses[u]:
-                left.update({given[u] + x: max(e for _, e, _ in held[given[u] + x]) for x in range(m)})
-    SPAN[:] = [max(done), begin]
-    return sorted(range(len(ops)), key=lambda i: (begin[i], i)), given
+    for i in sorted(range(len(ops)), key=lambda i: (ops[i]["at"], i)):
+        if i not in placed:
+            place(i)
+    return seq, given
 
 
 def group_program(g, core, rank, helper, T, topo, plan):
@@ -224,23 +154,24 @@ def group_program(g, core, rank, helper, T, topo, plan):
     Q = {"v": g.vector, "a": g.scalar, "p": g.tensor, "g": g, "s": g.sync}
     CS = {"v": "cv", "a": "ca", "p": "cp", "g": "cg"}
     ops, lastw, readers, raised = [], {}, {}, {}
+    TAG[0] = ""
 
-    def op(q, fn, cost, r=(), w=(), banks=(), ext=(), tok=None, inc=None, lat=SEM):
+    def users(names):
+        return [d for x in names for d in readers.get(x, []) + ([lastw[x]] if x in lastw else [])]
+
+    def op(q, fn, r=(), w=(), banks=(), ext=(), tok=None, inc=None):
         me = len(ops)
-        deps = set(lastw[x] for x in r if x in lastw)
-        for x in w:
-            deps.update(readers.get(x, []) + ([lastw[x]] if x in lastw else []))
+        deps = set(lastw[x] for x in r if x in lastw) | set(users(w))
         for x in r:
             readers.setdefault(x, []).append(me)
         for x in w:
             lastw[x] = me
             readers[x] = []
-        deps.discard(me)
         pc = banks if banks and isinstance(banks[0], str) else None
         if pc:
             banks = [plan[1][pc[0]] + x for x in pc[2]] if plan else []
         ops.append({"q": q, "piece": pc, "who": q if tok is None else "dma%d" % me, "fn": fn, "deps": deps, "ext": list(ext), "tok": tok, "inc": inc,
-                    "tag": TAG[0], "cost": cost, "lat": lat, "banks": list(banks), "r": list(r), "w": list(w), "far": [raised[s] for s, _ in ext]})
+                    "tag": TAG[0], "at": -1, "banks": list(banks), "far": [raised[s] for s, _ in ext]})
 
     def emit():
         seq, last, need = plan[0], {}, set()
@@ -282,26 +213,17 @@ def group_program(g, core, rank, helper, T, topo, plan):
 
     v, a, pe = g.vector, g.scalar, g.tensor
 
-    def size(ap):
-        n = 1
-        for s in ap.shape[1:]:
-            n *= s
-        return n
-
-    def cost(e, out, f=1.0):
-        return FIX[e] + size(out) * f * CYC
-
-    def ts(out, in0, s1, op0, s2=None, op1=None, r=(), w=(), banks=(), f=1.0):
+    def ts(out, in0, s1, op0, s2=None, op1=None, r=(), w=(), banks=()):
         if op1 is None:
-            op("v", lambda: v.tensor_scalar(out, in0, s1, None, op0), cost("v", out, f), r, w, banks)
+            op("v", lambda: v.tensor_scalar(out, in0, s1, None, op0), r, w, banks)
         else:
-            op("v", lambda: v.tensor_scalar(out, in0, s1, s2, op0, op1), cost("v", out, f), r, w, banks)
+            op("v", lambda: v.tensor_scalar(out, in0, s1, s2, op0, op1), r, w, banks)
 
-    def tt(out, in0, in1, o, r=(), w=(), banks=(), ext=(), f=1.0):
-        op("v", lambda: v.tensor_tensor(out, in0, in1, o), cost("v", in1, f), r, w, banks, ext)
+    def tt(out, in0, in1, o, r=(), w=(), banks=(), ext=()):
+        op("v", lambda: v.tensor_tensor(out, in0, in1, o), r, w, banks, ext)
 
     def act(out, in_, fn, bias=0.0, scale=1.0, r=(), w=(), banks=()):
-        op("a", lambda: a.activation(out, in_, fn, bias=bias, scale=scale), cost("a", out), r, w, banks)
+        op("a", lambda: a.activation(out, in_, fn, bias=bias, scale=scale), r, w, banks)
 
     def line(e, out, in_, scale, bias, r, w, banks=()):
         if e == "v":
@@ -312,36 +234,36 @@ def group_program(g, core, rank, helper, T, topo, plan):
     def gather(e, out, win, off, r, w, add=0.0, ext=()):
         src = win.indirect(off)
         if e == "a":
-            op("a", lambda: a.activation(out, src, AF.Identity, bias=add), cost("v", out, GATH), r, w, (), ext)
+            op("a", lambda: a.activation(out, src, AF.Identity, bias=add), r, w, (), ext)
         elif add:
-            op("v", lambda: v.tensor_scalar(out, src, add, None, ALU.add), cost("v", out, GATH), r, w, (), ext)
+            op("v", lambda: v.tensor_scalar(out, src, add, None, ALU.add), r, w, (), ext)
         else:
-            op("v", lambda: v.tensor_copy(out, src), cost("v", out, GATH), r, w, (), ext)
+            op("v", lambda: v.tensor_copy(out, src), r, w, (), ext)
 
-    def mms(calls, r, w, banks, f=1, start=True, stop=True, each=False):
+    def mms(calls, r, w, banks, start=True, stop=True, each=False):
         def fn():
             for i, (o, l, x) in enumerate(calls):
                 ins = pe.matmul(o, l, x, each or (start and i == 0), each or (stop and i == len(calls) - 1))
             return ins
-        op("p", fn, sum(FIX["p"] + max(64, size(x)) * f * PCYC for _, _, x in calls), r, w, banks, lat=SEM + PLAT)
+        op("p", fn, r, w, banks)
 
-    def dma(q, out, in_, sem, n, late, r=(), w=(), ext=()):
-        op(q, lambda: Q[q].dma_start(out, in_), 100, r, w, (), ext, (sem, n), 16, late)
+    def dma(q, out, in_, sem, n, r=(), w=(), ext=()):
+        op(q, lambda: Q[q].dma_start(out, in_), r, w, (), ext, (sem, n), 16)
 
-    def iota(out, pat, name):
-        op("g", lambda: g.iota(out, pat, 0, 0, allow_small_or_imprecise_dtypes=True), 130 + 2 * CYC * size(out), (), [name])
+    def iota(out, pat, name, base=0, r=()):
+        op("g", lambda: g.iota(out, pat, base, 0, allow_small_or_imprecise_dtypes=True), r, [name])
 
     def select(out, pat, cmp, fill, base, cm, r, w):
-        op("g", lambda: g.affine_select(out, out, pat, cmp, fill, base, cm), 170 + 2 * CYC * size(out), r, w)
+        op("g", lambda: g.affine_select(out, out, pat, cmp, fill, base, cm), r, w)
 
     nsent = [0]
 
     def send(dst, out, in_, sem, r):
         rid, pid, _ = topo.addr(dst)
         en = topo.engines(core, dst)[0::2]
-        raised[sem] = (len(ops), HOP + (2500 if not nsent[0] else 0))
+        raised[sem] = len(ops)
         nsent[0] += len(en)
-        op("g", lambda: g.remote_dma(out, in_, T.sem[sem], T.sem.sent, pid, rid, mask_of(en)), 500, r, (), tok=("sent", nsent[0]), lat=0)
+        op("g", lambda: g.remote_dma(out, in_, T.sem[sem], T.sem.sent, pid, rid, mask_of(en)), r, tok=("sent", nsent[0]))
 
     def hs(h, n=128, base=0):
         return slice(base + h * n, base + (h + 1) * n)
@@ -369,7 +291,7 @@ def group_program(g, core, rank, helper, T, topo, plan):
 
     def reg(x, h):
         s = slice(REG[x][0], REG[x][0] + REG[x][1])
-        return T.ps[:, 6:8, s] if h == 2 else T.ps[:, 6 + h, s]
+        return T.pz[:, 0:2, s] if h == 2 else T.pz[:, h, s]
 
     def bk(h):
         return [6 + i for i in halves(h)]
@@ -384,72 +306,87 @@ def group_program(g, core, rank, helper, T, topo, plan):
     def marks(s):
         return T.G[:, s:s + 8]
 
-    cw = V // NCH
+    def turned(t):
+        mms([(T.pz[:, 0, 256:MW], turn(t), T.zc[:])], ["I"] + nm(2, "zc"), ["#C0"], [6])
+
+    cut = [slice(CUTS[i], CUTS[i + 1]) for i in range(NCH)]
     for i in range(NCH):
         if i == 1:
-            dma("a", T.w0s[:], T.w0[:], "lw", 16, 2000, w=["w0s"])
-        dma("sa"[i % 2], T.recs[:, hs(i, cw)], T.rec[:, hs(i, cw)], "lr%d" % i, 16, 2500 + 1000 * i, w=["recs%d" % i])
+            dma("a", T.w0s[:], T.w0[:], "lw", 16, w=["w0s"])
+        dma("sa"[i % 2], T.recs[:, cut[i]], T.rec[:, cut[i]], "lr%d" % i, 16, w=["recs%d" % i])
     RECS = ["recs%d" % i for i in range(NCH)]
-    dma("s", T.xe[:, XO:XO + V], T.x[:], "lx0", 16, 3000, r=RECS[-1:], w=["xe1"])
-    dma("s", T.xe[:, XO + V:XO + V + 2], T.x[:, 0:2], "lx1", 16, 2000, r=RECS[-1:], w=["xe2"])
-    dma("s", T.xa[:], T.x[:], "lx2", 16, 3000, r=["xe1"], w=["xa"])
-    op("g", lambda: g.iota(T.pi[:], [[0, 1]], 0, 1), 130, (), ["pi"])
+    dma("s", T.xe[:, XO:XO + V], T.x[:], "lx0", 16, r=RECS[1:2], w=["xe1"])
+    dma("s", T.xe[:, XO + V:XO + V + 2], T.x[:, 0:2], "lx1", 16, r=RECS[1:2], w=["xe2"])
+    op("g", lambda: g.iota(T.pi[:], [[0, 1]], 0, 1), (), ["pi"])
     iota(T.q[:], [[0, 2], [1, 128]], "q")
     iota(T.q16[:], [[16, 16], [0, 16]], "q16")
     iota(T.ck[:], [[0, 16], [1, 16]], "ck")
     iota(T.c16[:], [[1, 16]], "c16")
-    iota(T.Rt[:, V:RW], [[0, RW - V]], "Rtb")
+    for i in (0, 1):
+        iota(T.Rt[:, hs(0, 16, i * (V + 16))], [[0, 16]], "Rtb%d" % i)
     C = T.col
     pk = C[:, 1:2]
-    ts(T.pa[:], T.pi[:], 15, ALU.bitwise_and, r=["pi"], w=["pa"])
-    line("v", C[:, 0:1], T.pi[:], 1.0, 0.0, ["pi"], ["c0"])
+    for x, ap, c in (("e0", T.e0[:], 0.0), ("Dt", T.Dt[:], 0.0), ("GB", T.GB[:], 0.0), ("#D", T.pz[:, 0:2, 272:416], 0.0),
+                     ("rep", T.rep[:, :, 0], BIG), ("e0", T.e0[:, 0::BW], BIG), ("rep", T.rep[:, :, BW - 1], -BIG)):
+        op("v", lambda ap=ap, c=c: v.memset(ap, c), (), nm(2, x), bk(2) if x == "#D" else ())
+        if x == "GB":
+            ts(T.pa[:], T.pi[:], 15, ALU.bitwise_and, r=["pi"], w=["pa"])
+            line("v", C[:, 0:1], T.pi[:], 1.0, 0.0, ["pi"], ["c0"])
+        if x == "Dt":
+            act(T.one[:], T.Dt[:, 0, :, 0:16], AF.Exp, scale=0.0, r=nm(2, x), w=["one"])
     line("v", pk, T.pa[:], 1.0, 0.0, ["pa"], ["pk"])
-    ts(C[:, 8:16], T.q16[:, 0:128:16], pk, ALU.add, float(V), ALU.add, r=["q16", "pk"], w=["c8"])
-    tt(C[:, 4:5], C[:, 0:1], pk, ALU.subtract, ["c0", "pk"], ["c4"])
-    ts(T.blk[:], T.q16[:], C[:, 4:5], ALU.is_equal, r=["q16", "c4"], w=["blk"])
     ts(T.I[:], T.q[:], C[:, 0:1], ALU.is_equal, r=["q", "c0"], w=["I"])
-    act(T.one[:], T.q16[:, 0:128], AF.Exp, scale=0.0, r=["q16"], w=["one"])
+    tt(C[:, 4:5], C[:, 0:1], pk, ALU.subtract, ["c0", "pk"], ["c4"])
+    line("v", C[:, 8:9], pk, 1.0, float(V + 16), ["pk"], ["c8"])
+    ts(T.blk[:], T.q16[:], C[:, 4:5], ALU.is_equal, r=["q16", "c4"], w=["blk"])
     for x, src, sc in (("In", "I", -1.0), ("If", "I", 1.0), ("Ih", "I", 0.5)):
         line("a", T[x][:], T[src][:, 0:128], sc, 0.0, [src], [x])
     for i, sc in enumerate((1.0, 1.0, NR / (2.0 * NR - 16), 1.0 / (16.5 - TH))):
         line("a", marks(8 * i), T.blk[:, 0:128:16], sc, 0.0, ["blk"], ["G%d" % i])
+    line("a", T.Gf[:], T.blk[:, 0:128:16], 1.0, 0.0, ["blk"], ["Gf"])
     GS = ["G%d" % i for i in range(4)]
-    op("v", lambda: v.memset(T.GB[:], 0.0), FIX["v"], (), ["GB"])
     for d in range(NB):
         for i in range(d, NB):
-            line("a", T.GB[:, 8 * d + i:8 * d + 8:NB], T.blk[:, 16 * (i - d):128:16 * NB], BIG, 0.0, ["blk"], ["GB"])
-    for x, ap, c in (("e0", T.e0[:], 0.0), ("e0", T.e0[:, 0::BW], BIG), ("Dt", T.Dt[:], 0.0), ("#D", T.ps[:, 6:8, 272:416], 0.0),
-                     ("rep", T.rep[:, :, 0], BIG), ("rep", T.rep[:, :, BW - 1], -BIG)):
-        op("v", lambda ap=ap, c=c: v.memset(ap, c), cost("v", ap, 0.5), (), nm(2, x), bk(2) if x == "#D" else ())
-    ts(T.Mi[:], T.ck[:], pk, ALU.is_equal, BIG, ALU.mult, r=["ck", "pk"], w=["Mi"])
+            line("a", T.GB[:, 8 * d + i:8 * d + 8:NB], T.blk[:, 16 * (i - d):128:16 * NB], -BIG if i else BIG, 0.0, ["blk", "GB0"], ["GB%d%d" % (d, i)])
+    GBS = ["GB%d%d" % (d, i) for d in range(NB) for i in range(d, NB)]
+    ts(T.fT[:, 0:128], T.ck[:, 0:128], pk, ALU.is_equal, BIG, ALU.mult, r=["ck", "pk"], w=["fT0"])
     ts(T.Mk[:], T.ck[:, 0:128], pk, ALU.is_lt, 0.5, ALU.mult, r=["ck", "pk"], w=["Mk"])
-    tt(T.Mk[:], T.Mk[:], T.Mi[:, 0:128], ALU.add, ["Mk", "Mi"], ["Mk"], f=2)
     ts(T.Mi[:], T.ck[:], pk, ALU.is_equal, r=["ck", "pk"], w=["Mi"])
+    tt(T.Mk[:], T.Mk[:], T.fT[:, 0:128], ALU.add, ["Mk", "fT0"], ["Mk"])
     line("v", T.LU[:], T.c16[:], float(BW), float(BW - 1), ["c16"], ["LU"])
     line("v", T.LD[:], T.c16[:], 1.0, 0.0, ["c16"], ["LD"])
-    line("v", T.WL[:, 0:16], T.w0s[:], 1.0, 0.0, ["w0s"], nm(2, "WL1"))
+    line("a", T.KC[:], T.c16[:, 0:8], 0.0, float(C0 + 17), ["c16"], ["KC"])
     line("v", T.zc[:], T.w0s[:], 1.0, float(-C0), ["w0s"], nm(2, "zc"))
+    turned(1)
     ts(T.u0[:], T.w0s[:], float(V - 1), ALU.is_ge, float(-V), ALU.mult, r=["w0s"], w=["u0"])
+    line("v", T.WL[:, 0:16], T.w0s[:], 1.0, 0.0, ["w0s"], nm(2, "WL1"))
     tt(T.u0[:], T.u0[:], T.zc[:], ALU.add, ["u0"] + nm(2, "zc"), ["u0"])
+    line("v", T.Os[:, 256:MW], T.pz[:, 0, 256:MW], 1.0, float(C0), ["#C0"], ["Ow"], [6])
     tt(T.wx[:], T.u0[:].indirect(T.LD[:]), T.Mi[:], ALU.mult, ["u0", "LD", "Mi"], ["wx"])
+
+    def ahead():
+        send(guest(1), T.Oin[:, 256:MW], T.Os[:, 256:MW], "aw", ["Ow"])
 
     def differences():
         for c, fill in ((1, -1.0), (2, 1.0)):
             for m in (0, 1):
-                select(T.Dt[:, :, :, c:c + 16], [[-1, RO], [-16, 8], [1, 16]], ALU.not_equal, fill, -16 * m, 1, ["Os1"], nm(2, "Dt"))
+                select(T.Dt[:, :, :, c:c + 16], [[-1, RO], [-16, 8], [1, 16]], ALU.not_equal, fill, -16 * m, 1, (), nm(2, "Dt"))
         select(T.Dt[:, :, :, 1:18], [[0, RO], [-16, 8], [0, 17]], ALU.is_ge, 0.0, 0, 1, (), nm(2, "Dt"))
         select(T.Dt[:, :, :, 1:18], [[0, RO], [16, 8], [0, 17]], ALU.is_ge, 0.0, 15, -1, (), nm(2, "Dt"))
 
-    def turned(t):
-        mms([(T.ps[:, 6, 256:MW], turn(t), T.zc[:])], ["I"] + nm(2, "zc"), ["#C0"], [6])
+    def spread(t):
+        if t == 2:
+            iota(T.Sel[:], [[0, 2048]], "Sel", 1, ["Os%d" % t])
+        if t == 3:
+            select(T.Sel[:], [[-1, 128], [0, 16]], ALU.is_equal, 0.0, 0, 1, ["Os%d" % t], ["Sel"])
 
-    turned(1)
+    bank, due, counted, before, answer = {}, {}, {}, {}, {}
 
     def lists(t, e, out, off, r, w, add=0.0, ext=()):
         if t == 1:
             gather(e, out, T.recs[:], off, RECS + r, w, add - C0, ext)
         else:
-            gather(e, out, T.Rt[:, 0:V], off, ["Rt"] + r, w, add, ext)
+            gather(e, out, T.Rt[:, 16:16 + V], off, ["Rt"] + r, w, add, ext)
 
     def times(t, h):
         return T.WL[:, part(h, 8, 16 * (t - 1))]
@@ -458,23 +395,21 @@ def group_program(g, core, rank, helper, T, topo, plan):
         return [("ao%d" % t, narr(asker(t)))]
 
     def ask(t, e):
-        s = hs(t - 1, MW)
-        mms([(T.ps[:, 6, 0:256], turn(t), T.ch[:])], ["I", "ch"], ["#A0", "#B0"], [6])
-        line(e, T.Os[:, s], T.ps[:, 6, 0:MW], 1.0, float(C0), ["#A0", "#B0", "#C0"], ["Os%d" % t], [6])
+        n = MW if t > 1 else 256
+        s = hs(0, n, (t - 1) * MW)
+        mms([(T.pz[:, 0, 0:256], turn(t), T.ch[:])], ["I", "ch"], ["#A0", "#B0"], [6])
+        line(e, T.Os[:, s], T.pz[:, 0, 0:n], 1.0, float(C0), ["#A0", "#B0", "#C0"], ["Os%d" % t], [6])
         send(guest(t), T.Oin[:, s], T.Os[:, s], "ao%d" % t, ["Os%d" % t])
-        if t == 1:
-            differences()
 
     def big(t, p, qu, e):
-        s = hs(qu, 1024)
+        qs, n = ([qu], 64) if qu < 4 else ([2 * qu - 8, 2 * qu - 7], 128)
+        s = hs(qu % 4, 16 * n)
         if p == "o":
-            lists(t, e, T.Ro[:, s], T.O[:, hs(qu, 64)], ["O"], ["Ro%d" % qu])
+            lists(t, e, T.Ro[:, s], T.O[:, hs(qu % 4, n)], ["O"], ["Ro%d" % x for x in qs])
         elif p == "g":
-            lists(t, e, T.Rg[:, s], T.Oin[:, hs(qu, 64, (t - 1) * MW)], [], ["Rg%d" % qu], 0.0, arrived(t))
+            lists(t, e, T.Rg[:, s], T.Oin[:, hs(qu % 4, n, (t - 1) * MW)], [], ["Rg%d" % x for x in qs], 0.0, arrived(t))
         else:
-            gather(e, T.xn[:, s], T.xe[:, 16:16 + V], T.O[:, hs(qu, 64)], ["xe1", "xe2", "O"], ["xn%d" % qu])
-
-    bank, due = {}, {}
+            gather(e, T.xn[:, s], T.xe[:, 16:16 + V], T.O[:, hs(qu % 4, n)], ["xe1", "xe2", "O"], ["xn%d" % x for x in qs])
 
     def piece(u):
         key, n = bank[u]
@@ -487,30 +422,26 @@ def group_program(g, core, rank, helper, T, topo, plan):
     def sub(x, h, j, n):
         return ["%s%d%d" % (x, h, j + i) for i in range(n)]
 
-    def diff(u, n=0):
-        p, h, j = u
+    def diff(t, p, h, j, n=0):
+        u = (p, h, j)
         if n:
             bank[u] = (TAG[0], n)
         key, m = bank[u]
         wide, small = {"o": ("Ro", "ch"), "g": ("Rg", "cg"), "x": ("xn", "xz")}[p]
         for i in range(m):
-            if (p == "x") == (n > 0):
-                calls = [(Id, T[wide][:, 2048 * h + 4 * (j + i) + k:2048 * (h + 1):16]) for k in range(4)]
+            ks = range(4 * (j + i), 4 * (j + i + 1))
+            if p == "x" and t == RO and n:
+                calls, rd = [(T.xn[:, hs(k, 128, 2048 * h)], Id) for k in ks], ["xn%d" % (2 * h + (j + i) // 2)]
+            elif p == "x" and t == RO:
+                calls, rd = [(T.Sel[:, hs(k)], T.xt[:, hs(h)]) for k in ks], ["Sel", "xt%d" % h]
+            elif (p == "x") == (n > 0):
+                calls = [(Id, T[wide][:, 2048 * h + k:2048 * (h + 1):16]) for k in ks]
                 rd = ["%s%d" % (wide, 2 * h), "%s%d" % (wide, 2 * h + 1)]
             else:
                 calls, rd = [(T.In[:], T[small][:, hs(h)])] * 4, ["xz%d" % h if p == "x" else small]
             w = ["%s.%d" % (key, i)]
             b = (plan[1][key] if plan else 0) + i
-            if SPLIT:
-                if (p == "x") == (n > 0):
-                    cs = [(T.ps[:, b, hs(2 * k + y, 64)], Id, T[wide][:, 2048 * h + 1024 * y + 4 * (j + i) + k:2048 * h + 1024 * (y + 1):16])
-                          for k in range(4) for y in range(2)]
-                else:
-                    cs = [(T.ps[:, b, hs(2 * k + y, 64)], T.In[:], T[small][:, hs(2 * h + y, 64)]) for k in range(4) for y in range(2)]
-                mms(cs, ["I", "In"] + rd, w, (key, m, [i]), 1, n > 0, n == 0)
-                ops[-1]["cost"] -= 40
-                continue
-            mms([(T.ps[:, b, hs(k)], l, x) for k, (l, x) in enumerate(calls)], ["I", "In"] + rd, w, (key, m, [i]), 1, n > 0, n == 0)
+            mms([(T.ps[:, b, hs(k)], l, x) for k, (l, x) in enumerate(calls)], ["I", "In"] + rd, w, (key, m, [i]), n > 0, n == 0)
 
     def test(t, p, h, j):
         d, rd, bs = piece((p, h, j))
@@ -523,13 +454,21 @@ def group_program(g, core, rank, helper, T, topo, plan):
         act(T.dx[:, cols(h, j, n)], T.ad[:, cols(h, j, n)], AF.Sign, bias=0.5 + 2.0 ** -21, scale=-1.0, r=sub("ad", h, j, n), w=sub("dx", h, j, n))
         due["x", h, j] = (n, SIGNS)
 
+    def into(x, h, j, calls, r):
+        if (x, h) not in counted:
+            counted[x, h], before[x, h] = [], users(slots(h, x))
+        counted[x, h].append("%s%d%d" % (x, h, j))
+        mms(calls, r, counted[x, h][-1:], bk(h), each=True)
+        ops[-1]["deps"].update(before[x, h])
+
+    def filled(h, x):
+        return [n for i in halves(h) for n in counted.pop((x, i))] + slots(h, x)
+
     def count(t, p, h, j):
         x = {"o": "LT", "g": "Lg", "x": "NC"}[p]
         (n, s), (o, wide, _) = due.pop((p, h, j)), REG[x]
-        mms([(T.ps[:, 6 + h, o + (k if p == "x" else (t - k - 1) % 16 + (p == "o")):o + wide:wide // 8], T["d" + p][:, hs(k, 128, 2048 * h)], marks(s))
-             for k in range(4 * j, 4 * (j + n))], GS + sub("d" + p, h, j, n), slots(h, x), bk(h), each=True)
-
-    answer = {}
+        into(x, h, j, [(T.pz[:, h, o + (k if p == "x" else (t - k - 1) % 16 + (p == "o")):o + wide:wide // 8], T["d" + p][:, hs(k, 128, 2048 * h)], marks(s))
+                       for k in range(4 * j, 4 * (j + n))], GS + sub("d" + p, h, j, n))
 
     def reaches(e, out, in_, bound, r, w, banks):
         if e == "v":
@@ -539,7 +478,7 @@ def group_program(g, core, rank, helper, T, topo, plan):
 
     def reply(t, h, e):
         s = part(h, 8, (t - 1) * 16)
-        reaches(e, T.rep[:, s, 1:17], reg("Lg", h), TH, slots(h, "Lg") + nm(h, "rep"), nm(h, "rep%d" % t), bk(h))
+        reaches(e, T.rep[:, s, 1:17], reg("Lg", h), TH, filled(h, "Lg") + nm(h, "rep"), nm(h, "rep%d" % t), bk(h))
         send(asker(t), T.repin[:, BW * s.start:BW * s.stop], T.rep[:, s, :], "ar%d%d" % (h, t), nm(h, "rep%d" % t))
         answer.update({i: h for i in halves(h)})
 
@@ -549,33 +488,32 @@ def group_program(g, core, rank, helper, T, topo, plan):
 
     def steps(t, h):
         o, e8 = reg("dn", h), hs(h, 8)
-        lead = T.ps[:, 6 + h, 1:8 * BW:BW]
+        lead = T.pz[:, h, 1:8 * BW:BW]
         calls = [(o, T.ch[:, hs(h)], T.Dt[:, t - 1]), (o, T.rr[:, hs(h)], T.Dt[:, t - 1])]
         if t == 1:
             calls.append((lead, T.wx[:, hs(h)], marks(MARK)))
         else:
-            ts(T.rw[:, e8], chosen(T.U, h), float(V - 2 - C0), ALU.is_ge, float(-V), ALU.mult, r=nm(h, "U"), w=nm(h, "rw"))
             calls += [(lead, T.If[:], chosen(T.U, h)), (lead, Id, T.rw[:, e8]), (lead, Id, T.one[:, 0:8])]
         mms(calls, ["ch", "rr", "wx", "I", "If", "one"] + GS + nm(2, "Dt") + nm(h, "U", "rw"), slots(h, "dn"), bk(h))
 
     def untwin(t, h):
         ext = [("ar%d%d" % (x, t), narr(guest(t))) for x in sorted(set(answer[i] for i in halves(h)))]
-        tt(T.nk[:, part(h, 8 * BW)], reg("LT", h), T.repin[:, part(h, 8 * BW, (t - 1) * 16 * BW)], ALU.is_ge, slots(h, "LT"), nm(h, "nk"), bk(h), ext)
+        tt(T.nk[:, part(h, 8 * BW)], reg("LT", h), T.repin[:, part(h, 8 * BW, (t - 1) * 16 * BW)], ALU.is_ge, filled(h, "LT"), nm(h, "nk"), bk(h), ext)
 
-    def scan(out, d0, d1, o0, o1, r, w, banks, f):
-        op("v", lambda: v.tensor_tensor_scan(out, d0, d1, 0.0, o0, o1), cost("v", d1, f), r, w, banks)
+    def scan(out, d0, d1, o0, o1, r, w, banks):
+        op("v", lambda: v.tensor_tensor_scan(out, d0, d1, 0.0, o0, o1), r, w, banks)
 
     def choose(h):
         for x in halves(h):
-            scan(T.U[:, hs(x, 8 * BW)], reg("dn", x), T.nk[:, hs(x, 8 * BW)], ALU.add, ALU.mult, slots(x, "dn") + nm(x, "nk"), nm(x, "U"), bk(x), 1)
+            scan(T.U[:, hs(x, 8 * BW)], reg("dn", x), T.nk[:, hs(x, 8 * BW)], ALU.add, ALU.mult, slots(x, "dn") + nm(x, "nk"), nm(x, "U"), bk(x))
         src = T.U[:, part(h, 8 * BW)].indirect(T.LU[:, 0:8 * len(halves(h))])
-        tt(T.H[:, part(h)], src, T.Mi[:, part(h)], ALU.mult, nm(h, "U") + ["LU", "Mi"], nm(h, "H"), f=GATH)
+        tt(T.H[:, part(h)], src, T.Mi[:, part(h)], ALU.mult, nm(h, "U") + ["LU", "Mi"], nm(h, "H"))
         for x in halves(h):
             mms([(reg("Z", x), T.H[:, hs(x)], marks(MARK))], GS + nm(x, "H"), slots(x, "Z"), bk(x))
 
     def flag(h, e):
-        scan(T.F[:, part(h, 8 * BW)], T.nk[:, part(h, 8 * BW)], T.e0[:, part(h, 8 * BW)], ALU.mult, ALU.add, nm(h, "nk", "e0"), nm(h, "F"), (), 0.5)
-        tt(T.uf[:, part(h, 8)], chosen(T.U, h), chosen(T.F, h), ALU.add, nm(h, "U", "F"), nm(h, "uf"), f=2)
+        scan(T.F[:, part(h, 8 * BW)], T.nk[:, part(h, 8 * BW)], T.e0[:, part(h, 8 * BW)], ALU.mult, ALU.add, nm(h, "nk", "e0"), nm(h, "F"), ())
+        tt(T.uf[:, part(h, 8)], chosen(T.U, h), chosen(T.F, h), ALU.add, nm(h, "U", "F"), nm(h, "uf"))
         gather(e, T.ub[:, part(h)], T.uf[:, part(h, 8)], T.LD[:, 0:8 * len(halves(h))], nm(h, "uf") + ["LD"], nm(h, "ub"))
 
     def claim(h, d):
@@ -585,19 +523,17 @@ def group_program(g, core, rank, helper, T, topo, plan):
         tt(T.eq[:, part(h, 128, 256 * d)], reg("eq", h), T.ub[:, part(h)], ALU.is_equal, slots(h, "eq") + nm(h, "ub"), nm(h, "eq%d" % d), bk(h))
 
     def target(h):
-        mms([(reg("tg", h), T.H[:, hs(h)], marks(MARK))] + [(reg("tg", h), T.eq[:, hs(h, 128, 256 * d)], T.GB[:, hs(d, 8)]) for d in range(NB)],
-            GS + ["GB"] + nm(h, "H", *["eq%d" % d for d in range(NB)]), slots(h, "tg"), bk(h))
-        o = REG["tg"][0]
-        for i in range(NB):
-            ts(T.tg[:, 8 * h + i:8 * h + 8:NB], T.ps[:, 6 + h, o + i:o + 8:NB], float(C0 + 1), ALU.add, C[:, 8 + i:9 + i], ALU.min,
-               r=slots(h, "tg") + ["c8"], w=["tg%d%d" % (h, i)], banks=bk(h))
+        for x in halves(h):
+            calls = [(T.H[:, hs(x)], marks(MARK)), (Id, T.KC[:])] + [(T.eq[:, hs(x, 128, 256 * d)], T.GB[:, hs(d, 8)]) for d in range(NB)]
+            mms([(reg("tg", x), l, r) for l, r in calls], GS + GBS + ["I", "KC"] + nm(x, "H", *["eq%d" % d for d in range(NB)]), slots(x, "tg"), bk(x))
+        ts(T.tg[:, part(h, 8)], reg("tg", h), C[:, 8:9], ALU.min, pk, ALU.max, r=slots(h, "tg") + ["c8", "pk"], w=nm(h, "tg"), banks=bk(h))
 
     def after(h):
         for x in halves(h):
             mms([(reg("nP", x), Id, r) for r in (T.ch[:, hs(x)], T.rr[:, hs(x)], T.one[:])], ["I", "ch", "rr", "one"], slots(x, "nP"), bk(x))
 
     def near(h, e):
-        reaches(e, T.fT[:, part(h)], reg("NC", h), NR, slots(h, "NC"), nm(h, "fT"), bk(h))
+        reaches(e, T.fT[:, part(h)], reg("NC", h), NR, filled(h, "NC"), nm(h, "fT"), bk(h))
         for x in halves(h):
             calls = [(T.fT[:, hs(x)], Id)] if e == "v" else [(T.one[:], T.Ih[:]), (T.fT[:, hs(x)], T.Ih[:])]
             mms([(reg("put", x), l, r) for l, r in calls], ["I", "Ih", "one"] + nm(x, "fT"), slots(x, "put"), bk(x))
@@ -605,7 +541,7 @@ def group_program(g, core, rank, helper, T, topo, plan):
     def put(h):
         for b in range(8 * (h + 1) // NB - 1, 8 * h // NB - 1, -1):
             tt(T.Rt[:].indirect(T.tg[:, hs(b, NB)]), T.old[:, hs(b, 16 * NB)], T.pr[:, hs(b, 16 * NB)], ALU.subtract,
-               nm(h, "pr", "old") + ["tg%d%d" % (h, i) for i in range(NB)] + ["Rtb"] + ["Rt%d" % i for i in range(NCH)], ["Rt"], f=SCAT)
+               nm(h, "pr", "old", "tg") + ["Rtb0", "Rtb1"] + ["Rt%d" % i for i in range(NCH)], ["Rt"])
 
     def absd(h, j):
         d, rd, bs = piece(("x", h, j))
@@ -617,63 +553,50 @@ def group_program(g, core, rank, helper, T, topo, plan):
 
     def fold(t):
         rid, pid, _ = topo.addr(helper)
-        en = topo.engines(core, helper)[1::2]
+        en, m = fold_engines(topo, core, helper, t), FOLDS[t][0]
         trs = [RemoteDMATransfer(dst_ids=[DstId(rid=rid, pnc=pid)], dma_engine_mask=mask_of(en), remote_sem=T.sem["af%d" % t],
-                                 srcs=[T.ex[:, 16 * (t % 2) + k, :] for k in range(16)], dsts=[T.fl[:, t - 1, :]], alu_op=1)]
-        raised["ay%d" % t] = (len(ops), 2 * HOP)
-        op("g", lambda: g.remote_dma_fused(trs, local_sem=T.sem["sf%d" % t]), 500, sub("ex%d" % (t % 2), 0, 0, 4) + sub("ex%d" % (t % 2), 1, 0, 4),
-           (), tok=("sf%d" % t, len(en)), lat=FOLD)
-        if t > 1 and not SPLIT:
-            ops[-1]["far"].append((raised["ay%d" % (t - 1)][0], 0.0))
-            ops[-1]["soft"] = [("ay%d" % (t - 1), 0.0)]
+                                 srcs=[T.ex[:, hs(k, m, 16 * (t % 2)), :] for k in range(16 // m)], dsts=[T.fl[:, t - 1, 0:256 * m]], alu_op=1)]
+        raised["ay%d" % t] = len(ops)
+        op("g", lambda: g.remote_dma_fused(trs, local_sem=T.sem["sf%d" % t]), sub("ex%d" % (t % 2), 0, 0, 4) + sub("ex%d" % (t % 2), 1, 0, 4),
+           tok=("sf%d" % t, len(en)))
 
     nys = [0]
 
     def store(cs, src, r=(), ext=()):
         nys[0] += 16
-        dma("s", T.y[:, cs], src, "ys", nys[0], 2000, r=r, ext=ext)
+        dma("s", T.y[:, cs], src, "ys", nys[0], r=r, ext=ext)
+
+    def sums(t, e):
+        ext = [("ay%d" % t, len(topo.engines(helper, core)))]
+        if FOLDS[t][0] == 1:
+            store(hs(t - 1, 256), T.yl[:, t - 1, 0:256], ext=ext)
+        else:
+            tt(T.yt[:, t - 1, :], T.yl[:, t - 1, 0:256], T.yl[:, t - 1, 256:512], ALU.add, (), ["yt%d" % t], (), ext)
+            store(hs(t - 1, 256), T.yt[:, t - 1, :], ["yt%d" % t])
+
+    def turn_xz(h, e):
+        mms([(reg("xt", h), T.xz[:, hs(h)], T.In[:])], ["In"] + nm(h, "xz"), slots(h, "xt"), bk(h))
+        line(e, T.xt[:, hs(h)], reg("xt", h), 1.0, 0.0, slots(h, "xt"), nm(h, "xt"), bk(h))
 
     def tail_abs(h, j):
         d, rd, bs = piece(("x", h, j))
-        line("v", T.ng[:], d, -1.0, 0.0, rd, ["ng"], bs)
-        tt(T.ad[:, cols(h, j)], T.ng[:], d, ALU.max, ["ng"] + rd, sub("ad", h, j, 1), bs)
+        ng = T.ng[:, 0:512 * bs[1]]
+        line("v", ng, d, -1.0, 0.0, rd, ["ng"], bs)
+        tt(T.ad[:, cols(h, j, bs[1])], ng, d, ALU.max, ["ng"] + rd, sub("ad", h, j, bs[1]), bs)
 
-    added = [0]
-
-    def tail_sum(h, j):
-        added[0] += 1
-        mms([(reg("S", h), T.If[:], T.ex[:, 16 * (RO % 2) + k, hs(h)]) for k in range(4 * j, 4 * j + 4)],
-            ["If", "ex%d%d%d" % (RO % 2, h, j)], slots(h, "S"), bk(h), 4, added[0] == 1, added[0] == 4)
+    def tail_sum(h, j, n):
+        into("S", h, j, [(T.pz[:, h, hs(k, 8)], T.ex[:, 16 * (RO % 2) + k, hs(h)], T.Gf[:]) for k in range(4 * j, 4 * (j + n))],
+             ["Gf"] + sub("ex%d" % (RO % 2), h, j, n))
 
     def tail_store(h, e):
-        line(e, T.yt[:, hs(h)], reg("S", h), 1.0, 0.0, slots(h, "S"), nm(h, "yt"), bk(h))
-        store(hs(h, 128, (RO - 1) * 256), T.yt[:, hs(h)], nm(h, "yt"))
-
-    def tail_exp(h, j):
-        d, rd, bs = piece(("x", h, j))
-        if j == 0:
-            act(T.acc[:], T.ad[:, cols(h, 0)], AF.Exp, scale=-1.0, r=sub("ad", h, 0, 1), w=["acc"])
-        else:
-            act(d, T.ad[:, cols(h, j)], AF.Exp, scale=-1.0, r=sub("ad", h, j, 1), w=rd, banks=bs)
-            tt(T.acc[:], T.acc[:], d, ALU.add, ["acc"] + rd, ["acc"], bs)
-
-    def tail_add(h):
-        tt(T.acc[:, 0:256], T.acc[:, 0:256], T.acc[:, 256:512], ALU.add, ["acc"], ["acc"], f=2)
-        tt(T.yt[:, hs(h)], T.acc[:, 0:128], T.acc[:, 128:256], ALU.add, ["acc"], nm(h, "yt"), f=2)
-        store(hs(h, 128, (RO - 1) * 256), T.yt[:, hs(h)], nm(h, "yt"))
-
-    def unit(w):
-        if w[0] in "PD" or w[:2] in ("to", "tg", "tx"):
-            return (w[1], int(w[2]), int(w[3]))
-        if w[:2] in ("ab", "da", "te"):
-            return ("x", int(w[2]), int(w[3]))
-        return None
+        line(e, T.yt[:, RO - 1, hs(h)], reg("S", h), 1.0, 0.0, filled(h, "S"), nm(h, "yh"), bk(h))
+        store(hs(h, 128, (RO - 1) * 256), T.yt[:, RO - 1, hs(h)], nm(h, "yh"))
 
     def run(t, w):
         c, p = w[:2], [int(z) if z.isdigit() else z for z in w[2:]]
         h = p[0] if p else 2
         if c[0] in "PD":
-            diff(unit(w), *p[2:])
+            diff(t, c[1], *p)
         elif c[0] == "N":
             count(t, c[1], *p)
         elif c in ("go", "gg", "gx"):
@@ -681,19 +604,19 @@ def group_program(g, core, rank, helper, T, topo, plan):
         elif c in ("to", "tg", "tx"):
             test(t, c[1], *p)
         elif c == "ol":
-            if h == "c":
-                ts(T.O[:], T.ch[:], float(C0), ALU.add, r=["ch"], w=["O"], f=0.5)
-            else:
-                lists(t, h, T.O[:], times(t, 2), nm(2, "WL%d" % t), ["O"], float(C0))
+            ts(T.O[:], T.ch[:], float(C0), ALU.add, r=["ch"], w=["O"])
         elif c == "ch":
             lists(t, h, T.ch[:], times(t, 2), nm(2, "WL%d" % t), ["ch"])
         elif c == "rr":
-            ts(T.rr[:], T.ch[:], float(C0 - 1), ALU.is_ge, float(-V), ALU.mult, r=["ch"], w=["rr"], f=0.5)
+            ts(T.rr[:], T.ch[:], float(C0 - 1), ALU.is_ge, float(-V), ALU.mult, r=["ch"], w=["rr"])
+        elif c == "rw":
+            ts(T.rw[:, part(h, 8)], chosen(T.U, h), float(V - 2 - C0), ALU.is_ge, float(-V), ALU.mult, r=nm(h, "U"), w=nm(h, "rw"))
         elif c == "cg":
-            lists(t, h, T.cg[:], T.Oin[:, hs(0, 16, (t - 1) * MW + 256)], [], ["cg"], 0.0, arrived(t))
+            lists(t, h, T.cg[:], T.Oin[:, hs(0, 16, (t - 1) * MW + 256)], [], ["cg"], 0.0, arrived(t) if t > 1 else [("aw", narr(asker(t)))])
+            if t == 1:
+                dma("s", T.xa[:], T.x[:], "lx2", 16, w=["xa"], ext=arrived(t))
         elif c == "cv":
-            for i in range(NCH if t == 1 else 0):
-                line("a", T.Rt[:, hs(i, cw)], T.recs[:, hs(i, cw)], 1.0, float(-C0), ["recs%d" % i], ["Rt%d" % i])
+            line(p[1], T.Rt[:, 16 + CUTS[h]:16 + CUTS[h + 1]], T.recs[:, cut[h]], 1.0, float(-C0), ["recs%d" % h], ["Rt%d" % h])
         elif c == "wl":
             line(p[1], times(t + 1, h), reg("Z", h), 1.0, float(C0 + 1), slots(h, "Z"), nm(h, "WL%d" % (t + 1)), bk(h))
         elif c == "zc":
@@ -707,18 +630,21 @@ def group_program(g, core, rank, helper, T, topo, plan):
             tt(T.Ed[:, part(h)], T.old[:, part(h)], reg("nP", h), ALU.subtract, nm(h, "old") + slots(h, "nP"), nm(h, "Ed"), bk(h))
         elif c == "pr":
             tt(T.pr[:, part(h)], T.Ed[:, part(h)], reg("put", h), ALU.mult, nm(h, "Ed") + slots(h, "put"), nm(h, "pr"), bk(h))
-        elif c == "ys":
-            store(hs(t - 1, 256), T.yl[:, t - 1, :], ext=[("ay%d" % t, narr(helper))])
-        elif c in ("os", "th", "dn", "nk", "ex", "fo"):
-            {"os": ask, "th": reply, "dn": steps, "nk": untwin, "ex": expo, "fo": fold}[c](t, *p)
+        elif c in ("os", "th", "dn", "nk", "ex", "fo", "ys", "se"):
+            {"os": ask, "th": reply, "dn": steps, "nk": untwin, "ex": expo, "fo": fold, "ys": sums, "se": spread}[c](t, *p)
         else:
-            {"sc": choose, "fs": flag, "eq": claim, "ai": target, "np": after, "ft": near, "ab": absd, "sg": sgn, "pu": put, "da": tail_abs,
-             "ts": tail_sum, "st": tail_store, "te": tail_exp, "ta": tail_add}[c](*p)
+            {"aw": ahead, "dt": differences, "sc": choose, "fs": flag, "eq": claim, "ai": target, "np": after, "ft": near, "ab": absd,
+             "sg": sgn, "pu": put, "da": tail_abs, "ts": tail_sum, "st": tail_store, "xt": turn_xz}[c](*p)
 
-    seq = [(t - w.count("-"), w.strip("-")) for t in range(1, RO + 1) for w in {1: SEQ1, RO: SEQL}.get(t, SEQ).split() if t > w.count("-")]
-    for i, (t, w) in enumerate(seq):
-        TAG[0] = "%d%s" % (t, w)
+    words = [(t - w.count("-"), w.strip("-")) for t in range(1, RO + 1) for w in {1: SEQ1, RO: SEQL}.get(t, SEQ).split() if t > w.count("-")]
+    for t, _, _, w in sorted((t, STAGES.index(w[:2]), w[2:3] != "1", w) for t, w in words if ":" not in w):
+        TAG[0], first, at = "%d%s" % (t, w), len(ops), words.index((t, w))
         run(t, w)
+        for n, o in enumerate(ops[first:]):
+            later = (t, "%s:%d" % (w.rstrip("va"), n + 1))
+            at = o["at"] = words.index(later) if later in words else at
+    for o in ops:
+        o["needs"] = sorted(o["deps"]) + o["far"]
     if plan:
         emit()
     return ops

from concourse.bass import DstId, RemoteDMATransfer
from concourse.mybir import AluOpType as ALU, ActivationFunctionType as AF

V, K, RO, TH, NR = 3840, 256, 5, 11, 9
C0 = V // 2
NB = 2
RW = V + 16 * NB
XO = 15
MW = 272
B2 = 1.5 * 2.0 ** 25
BH = 1.5 * 2.0 ** 23
BIG = 8192.0
CUTS = [0, 960, 1920, 2880, V]
NCH = len(CUTS) - 1
POOL = [0, 1, 2, 3, 4, 5]
BW = 18
REG = {"Lg": (0, 128, "A"), "dn": (0, 8 * BW, "AB"), "eq": (0, 128, "A"), "S": (0, 128, "A"), "NC": (128, 128, "B"), "xt": (144, 128, "B"),
       "put": (128, 128, "B"), "LT": (272, 8 * BW, "D"), "nP": (272, 128, "D"), "Z": (416, 8, "E"), "tg": (424, 8, "F")}
FOLDS = {1: (1, 2), 2: (1, 2), 3: (1, 2), 4: (2, 1)}
TAG = [""]

STAGES = ("aw dt cv ch ol rr os se cg go gg gx Po Do to No Pg Dg tg Ng th dn nk sc rw wl zc xz xt Px Dx tx ab da sg Nx fs eq ai od np ed ft pr pu "
          "ex ts st fo ys").split()
SEQ1 = ("dt aw cv1a cv0v cv2a chv osv ol os:2 dt:2 Po122 Po102 go2a go3v Do10 go1a rr cgv to10 Do12 Pg102 gg2a gg3v gg4a to12 No10 Pg122 Dg12 tg12 "
        "Dg10 tg10 Pg022 Ng12 Pg002 Ng10 Dg02 th1v Dg00 go0a Po022 Do02 tg02 dn1 No12 tg00 nk1 Ng02 sc1 gx5a Ng00 th0a Po002 Do00 sc1:2 sc1:3 to02 "
        "dn0 Px102 wl1a xz1v to00 Dx10 No02 gx4a Px122 No00 Dx12 tx10 nk0 sc0 Nx10 np2 sc0:2 eq20 fs2v fs2:2 fs2:3 ab12 sc0:3 wl0v xz0a sg122 eq20:3 "
        "Px022 eq21 ab10 Dx02 od2v eq21:3 ed2 Px002 Dx00 Nx12 ft1a tx02 Nx02 ft1:2 tx00 cv3a ai2 ai2:3 pr1 pu1 Nx00 ab02 rw2 ft0v pu1:2 pu1:3 ft0:2 "
        "pr0 pu1:4 pu0 pu0:2 pu0:3 pu0:4 zc2v zc2:2")
SEQ = ("-ab00 chv ol -ex022 osv os:2 -ex102 go3v Po122 go2a Do12 go0a Po102 Do10 cga Pg122 go1v gg2a gg3v Dg12 to12 Pg102 Dg10 rr No12 tg12 Pg022 "
       "Ng12 gg4a Dg02 se tg10 to10 Ng10 th1v tg02 Pg002 Dg00 Po022 tg00 -ex002 -ex122 gx3a dn1 No10 nk1 Ng02 sc1 sc1:2 gx2a -fo Do02 Ng00 th0v Po002 "
       "sc1:3 --ysv wl1a xz1a Do00 to02 Px102 to00 gx4a Dx10 dn0 tx10 No02 No00 nk0 Px122 Dx12 ab12 sc0 fs2v Nx10 np2 sc0:2 sc0:3 eq20 Px022 fs2:2 "
       "fs2:3 wl0v eq20:3 od2v xz0a eq21 eq21:3 ed2 sg122 Dx02 tx02 Px002 Dx00 tx00 Nx12 ai0 ab10 ft1a ai1 ft1:2 ai1:2 pr1 pu1 Nx02 Nx00 ft0v ab02 "
       "pu1:2 pu1:3 ft0:2 pr0 ai0:2 pu1:4 pu0 pu0:2 pu0:3 rw2 pu0:4 zc2v zc2:2")
SEQL = ("-ab00 -ex022 chv osv ol -ex002 os:2 -ex104 -fo go5v Po102 cga Po122 Do12 Pg122 gg2a gg3v Dg12 to12 Pg102 Dg10 go0a Do10 rr tg12 tg10 Ng12 "
        "Pg022 Ng10 Po002 to10 No12 gg4a gx3v Dg02 Pg002 Dg00 th1a dn1 tg02 tg00 No10 nk1 go1a Po022 Do02 sc1 sc1:2 Ng00 Ng02 sc1:3 th0v to02 Do00 "
        "wl1v dn0 gx2a Px102 No02 gx1a xz1a to00 Px122 xt1v No00 xt1:2 Dx12 nk0 gx0a sc0 sc0:2 sc0:3 wl0v xz0v Dx10 ab12 xt0v Px011 Px001 ex122 xt0:2 "
        "Dx01 Dx00 Px021 ab00 Px031 Dx03 Dx02 da10 da10:2 da02 da02:2 da03 da03:2 ts122 ex001 ts001 --ysv ex102 ts102 ab01 ex021 ts021 ex011 ts011 "
        "ex031 st1v -ysv ts031 st0a")

SCRATCH = {
    "recs": ("sbuf", [128, V], "int32"), "Rt": ("sbuf", [128, RW], "float32"),
    "xe": ("sbuf", [128, V + 32], "bfloat16"), "xa": ("sbuf", [128, V], "bfloat16"),
    "w0s": ("sbuf", [128, 16], "int32"), "WL": ("sbuf", [128, (RO + 1) * 16], "uint16"),
    "O": ("sbuf", [128, 256], "uint16"), "Os": ("sbuf", [128, RO * MW], "uint16"), "Oin": ("sbuf", [128, RO * MW], "uint16"),
    "ch": ("sbuf", [128, 256], "float16"), "cg": ("sbuf", [128, 256], "float16"), "rr": ("sbuf", [128, 256], "float16"),
    "Ro": ("sbuf", [128, 4096], "float16"), "Rg": ("sbuf", [128, 4096], "float16"), "xn": ("sbuf", [128, 4096], "bfloat16"),
    "do": ("sbuf", [128, 4096], "bfloat16"), "dg": ("sbuf", [128, 4096], "bfloat16"), "dx": ("sbuf", [128, 4096], "bfloat16"),
    "ad": ("sbuf", [128, 4096], "float32"), "ex": ("sbuf", [128, 32, 256], "float32"),
    "rep": ("sbuf", [128, RO * 16, BW], "bfloat16"), "repin": ("sbuf", [128, RO * 16 * BW], "bfloat16"),
    "nk": ("sbuf", [128, 16 * BW], "bfloat16"), "U": ("sbuf", [128, 16 * BW], "float32"), "H": ("sbuf", [128, 256], "float16"),
    "F": ("sbuf", [128, 16 * BW], "bfloat16"), "e0": ("sbuf", [128, 16 * BW], "bfloat16"), "uf": ("sbuf", [128, 16], "float32"),
    "KC": ("sbuf", [128, 8], "float16"), "ub": ("sbuf", [128, 256], "float32"), "LU": ("sbuf", [128, 16], "uint16"),
    "rw": ("sbuf", [128, 16], "float16"), "zc": ("sbuf", [128, 16], "float16"), "u0": ("sbuf", [128, 16], "float32"),
    "wx": ("sbuf", [128, 256], "float16"), "eq": ("sbuf", [128, 256 * NB], "bfloat16"), "fT": ("sbuf", [128, 256], "bfloat16"),
    "old": ("sbuf", [128, 256], "float32"), "Ed": ("sbuf", [128, 256], "float32"), "pr": ("sbuf", [128, 256], "float32"),
    "xz": ("sbuf", [128, 256], "bfloat16"), "tg": ("sbuf", [128, 16], "uint16"), "GB": ("sbuf", [128, 8 * NB], "bfloat16"),
    "xt": ("sbuf", [128, 256], "bfloat16"), "ng": ("sbuf", [128, 1024], "float32"), "yt": ("sbuf", [128, RO, 256], "float32"),
    "fl": ("sbuf", [128, RO - 1, 512], "float32"), "yl": ("sbuf", [128, RO - 1, 512], "float32"),
    "pi": ("sbuf", [128, 1], "int32"), "pa": ("sbuf", [128, 1], "int32"), "col": ("sbuf", [128, 16], "float32"),
    "c16": ("sbuf", [128, 16], "float32"), "LD": ("sbuf", [128, 16], "uint16"),
    "ck": ("sbuf", [128, 256], "bfloat16"), "q": ("sbuf", [128, 256], "bfloat16"), "q16": ("sbuf", [128, 256], "bfloat16"),
    "one": ("sbuf", [128, 128], "bfloat16"), "G": ("sbuf", [128, 40], "bfloat16"), "I": ("sbuf", [128, 256], "bfloat16"),
    "blk": ("sbuf", [128, 256], "bfloat16"), "If": ("sbuf", [128, 128], "float32"), "In": ("sbuf", [128, 128], "bfloat16"),
    "Ih": ("sbuf", [128, 128], "bfloat16"), "Gf": ("sbuf", [128, 8], "float32"), "Sel": ("sbuf", [128, 2048], "bfloat16"),
    "Mi": ("sbuf", [128, 256], "float32"), "Mk": ("sbuf", [128, 128], "bfloat16"), "Dt": ("sbuf", [128, RO, 8, BW], "bfloat16"),
    "ps": ("psum", [128, 6, 512], "float32"), "pz": ("psum", [128, 2, 512], "float32"),
}
SEMAPHORES = (["cv", "ca", "cp", "cg", "sent", "lw", "lx0", "lx1", "lx2", "ys", "aw"] + ["lr%d" % i for i in range(NCH)]
              + ["%s%d" % (n, t) for n in ("ao", "ar0", "ar1", "ar2", "af", "ay", "sf") for t in range(1, RO + 1)])


def helpers(T, topo):
    out = {}
    for c in T.cores:
        for h in topo.cores_of(c):
            if T.rank_of(h) is None and h not in out.values() and topo.die(h) == topo.die(c):
                out[c] = h
                break
    return out


def mask_of(engs):
    m = 0
    for e in engs:
        m |= 1 << e
    return m


def fold_engines(topo, src, dst, t):
    n = FOLDS[t][1]
    return topo.engines(src, dst)[n - 1::n]


def rank_program(g, core, T, topo):
    hp = helpers(T, topo)
    rank = T.rank_of(core)
    if rank is None:
        for c in T.cores:
            if hp[c] == core:
                helper_program(g, core, c, T, topo)
        return
    plan = order(group_program(g, core, rank, hp[core], T, topo, None))
    group_program(g, core, rank, hp[core], T, topo, plan)


def helper_program(g, core, c, T, topo):
    rid, pid, _ = topo.addr(c)
    en = topo.engines(core, c)
    for t in range(1, RO):
        s = slice(0, 256 * FOLDS[t][0])
        g.wait_ge(T.sem["af%d" % t], len(fold_engines(topo, c, core, t)))
        g.remote_dma(T.yl[:, t - 1, s], T.fl[:, t - 1, s], T.sem["ay%d" % t], T.sem.sent, pid, rid, mask_of(en))
    g.wait_ge(T.sem.sent, len(en) * (RO - 1))


def order(ops):
    seq, placed, given, users = [], set(), {}, {}
    left = {b: 0 for b in POOL}
    for i, o in enumerate(ops):
        if o["piece"]:
            users.setdefault(o["piece"][0], []).append(i)

    def place(i):
        o = ops[i]
        for d in o["needs"]:
            if d not in placed:
                place(d)
        if o["piece"]:
            u, m, _ = o["piece"]
            while u not in given:
                free = [b for b in left if b % m == 0 and all(b + x in left for x in range(m))]
                if free:
                    given[u] = min(free, key=lambda b: (max(left[b + x] for x in range(m)), b))
                    for x in range(m):
                        del left[given[u] + x]
                else:
                    for j in list(users[[x for x in given if users[x]][0]]):
                        if j not in placed:
                            place(j)
            users[u].remove(i)
            if not users[u]:
                left.update({given[u] + x: len(seq) for x in range(m)})
        placed.add(i)
        seq.append(i)

    for i in sorted(range(len(ops)), key=lambda i: (ops[i]["at"], i)):
        if i not in placed:
            place(i)
    return seq, given


def group_program(g, core, rank, helper, T, topo, plan):
    N = len(T.cores)
    Q = {"v": g.vector, "a": g.scalar, "p": g.tensor, "g": g, "s": g.sync}
    CS = {"v": "cv", "a": "ca", "p": "cp", "g": "cg"}
    ops, lastw, readers, raised = [], {}, {}, {}
    TAG[0] = ""

    def users(names):
        return [d for x in names for d in readers.get(x, []) + ([lastw[x]] if x in lastw else [])]

    def op(q, fn, r=(), w=(), banks=(), ext=(), tok=None, inc=None):
        me = len(ops)
        deps = set(lastw[x] for x in r if x in lastw) | set(users(w))
        for x in r:
            readers.setdefault(x, []).append(me)
        for x in w:
            lastw[x] = me
            readers[x] = []
        pc = banks if banks and isinstance(banks[0], str) else None
        if pc:
            banks = [plan[1][pc[0]] + x for x in pc[2]] if plan else []
        ops.append({"q": q, "piece": pc, "who": q if tok is None else "dma%d" % me, "fn": fn, "deps": deps, "ext": list(ext), "tok": tok, "inc": inc,
                    "tag": TAG[0], "at": -1, "banks": list(banks), "far": [raised[s] for s, _ in ext]})

    def emit():
        seq, last, need = plan[0], {}, set()
        place = {i: n for n, i in enumerate(seq)}
        for i in seq:
            o = ops[i]
            for b in o["banks"]:
                o["deps"].update(d for e, d in last.setdefault(b, {}).items() if e != o["q"])
                last[b][o["q"]] = i
            top = {}
            for d in o["deps"]:
                who = ops[d]["who"]
                if not (who == "p" == o["q"]) and (who not in top or place[d] > place[top[who]]):
                    top[who] = d
            o["deps"] = set(top.values())
            need |= o["deps"]
        cnt, seen, totals = {}, {}, {}
        for i in seq:
            o = ops[i]
            if o["tok"] is None and i in need:
                cnt[o["q"]] = cnt.get(o["q"], 0) + 1
                o["tok"], o["inc"] = (CS[o["q"]], cnt[o["q"]]), 1
            want = {}
            for s, n in [ops[d]["tok"] for d in o["deps"]] + o["ext"]:
                want[s] = max(want.get(s, 0), n)
            for s in sorted(want):
                if seen.get((o["q"], s), 0) < want[s]:
                    Q[o["q"]].wait_ge(T.sem[s], want[s])
                    seen[(o["q"], s)] = want[s]
            TAG[0] = o["tag"]
            ins = o["fn"]()
            if o["inc"]:
                ins.then_inc(T.sem[o["tok"][0]], o["inc"])
            if o["tok"] is not None:
                totals[o["tok"][0]] = max(totals.get(o["tok"][0], 0), o["tok"][1])
        for s in sorted(totals):
            if max([n for (q, s2), n in seen.items() if s2 == s] + [0]) < totals[s]:
                g.wait_ge(T.sem[s], totals[s])

    v, a, pe = g.vector, g.scalar, g.tensor

    def ts(out, in0, s1, op0, s2=None, op1=None, r=(), w=(), banks=()):
        if op1 is None:
            op("v", lambda: v.tensor_scalar(out, in0, s1, None, op0), r, w, banks)
        else:
            op("v", lambda: v.tensor_scalar(out, in0, s1, s2, op0, op1), r, w, banks)

    def tt(out, in0, in1, o, r=(), w=(), banks=(), ext=()):
        op("v", lambda: v.tensor_tensor(out, in0, in1, o), r, w, banks, ext)

    def act(out, in_, fn, bias=0.0, scale=1.0, r=(), w=(), banks=()):
        op("a", lambda: a.activation(out, in_, fn, bias=bias, scale=scale), r, w, banks)

    def line(e, out, in_, scale, bias, r, w, banks=()):
        if e == "v":
            ts(out, in_, scale, ALU.mult, bias, ALU.add, r, w, banks)
        else:
            act(out, in_, AF.Identity, bias, scale, r, w, banks)

    def gather(e, out, win, off, r, w, add=0.0, ext=()):
        src = win.indirect(off)
        if e == "a":
            op("a", lambda: a.activation(out, src, AF.Identity, bias=add), r, w, (), ext)
        elif add:
            op("v", lambda: v.tensor_scalar(out, src, add, None, ALU.add), r, w, (), ext)
        else:
            op("v", lambda: v.tensor_copy(out, src), r, w, (), ext)

    def mms(calls, r, w, banks, start=True, stop=True, each=False):
        def fn():
            for i, (o, l, x) in enumerate(calls):
                ins = pe.matmul(o, l, x, each or (start and i == 0), each or (stop and i == len(calls) - 1))
            return ins
        op("p", fn, r, w, banks)

    def dma(q, out, in_, sem, n, r=(), w=(), ext=()):
        op(q, lambda: Q[q].dma_start(out, in_), r, w, (), ext, (sem, n), 16)

    def iota(out, pat, name, base=0, r=()):
        op("g", lambda: g.iota(out, pat, base, 0, allow_small_or_imprecise_dtypes=True), r, [name])

    def select(out, pat, cmp, fill, base, cm, r, w):
        op("g", lambda: g.affine_select(out, out, pat, cmp, fill, base, cm), r, w)

    nsent = [0]

    def send(dst, out, in_, sem, r):
        rid, pid, _ = topo.addr(dst)
        en = topo.engines(core, dst)[0::2]
        raised[sem] = len(ops)
        nsent[0] += len(en)
        op("g", lambda: g.remote_dma(out, in_, T.sem[sem], T.sem.sent, pid, rid, mask_of(en)), r, tok=("sent", nsent[0]))

    def hs(h, n=128, base=0):
        return slice(base + h * n, base + (h + 1) * n)

    def guest(t):
        return T.cores[(rank + 1 + (t - 1) % (N - 1)) % N]

    def asker(t):
        return T.cores[(rank - 1 - (t - 1) % (N - 1)) % N]

    def narr(src):
        return len(topo.engines(src, core)[0::2])

    def part(h, n=128, base=0):
        return slice(base, base + 2 * n) if h == 2 else hs(h, n, base)

    def halves(h):
        return (0, 1) if h == 2 else (h,)

    def nm(h, *names):
        return ["%s%d" % (x, i) for x in names for i in halves(h)]

    def slots(h, x):
        return nm(h, *["#" + s for s in REG[x][2]])

    def reg(x, h):
        s = slice(REG[x][0], REG[x][0] + REG[x][1])
        return T.pz[:, 0:2, s] if h == 2 else T.pz[:, h, s]

    def bk(h):
        return [6 + i for i in halves(h)]

    def turn(t):
        s = (-16 * t) % 128
        return T.I[:, s:s + 128]

    Id = T.I[:, 0:128]
    MARK, SIGNS, MISS = 0, 16, 24

    def marks(s):
        return T.G[:, s:s + 8]

    def turned(t):
        mms([(T.pz[:, 0, 256:MW], turn(t), T.zc[:])], ["I"] + nm(2, "zc"), ["#C0"], [6])

    cut = [slice(CUTS[i], CUTS[i + 1]) for i in range(NCH)]
    for i in range(NCH):
        if i == 1:
            dma("a", T.w0s[:], T.w0[:], "lw", 16, w=["w0s"])
        dma("sa"[i % 2], T.recs[:, cut[i]], T.rec[:, cut[i]], "lr%d" % i, 16, w=["recs%d" % i])
    RECS = ["recs%d" % i for i in range(NCH)]
    dma("s", T.xe[:, XO:XO + V], T.x[:], "lx0", 16, r=RECS[1:2], w=["xe1"])
    dma("s", T.xe[:, XO + V:XO + V + 2], T.x[:, 0:2], "lx1", 16, r=RECS[1:2], w=["xe2"])
    op("g", lambda: g.iota(T.pi[:], [[0, 1]], 0, 1), (), ["pi"])
    iota(T.q[:], [[0, 2], [1, 128]], "q")
    iota(T.q16[:], [[16, 16], [0, 16]], "q16")
    iota(T.ck[:], [[0, 16], [1, 16]], "ck")
    iota(T.c16[:], [[1, 16]], "c16")
    for i in (0, 1):
        iota(T.Rt[:, hs(0, 16, i * (V + 16))], [[0, 16]], "Rtb%d" % i)
    C = T.col
    pk = C[:, 1:2]
    for x, ap, c in (("e0", T.e0[:], 0.0), ("Dt", T.Dt[:], 0.0), ("GB", T.GB[:], 0.0), ("#D", T.pz[:, 0:2, 272:416], 0.0),
                     ("rep", T.rep[:, :, 0], BIG), ("e0", T.e0[:, 0::BW], BIG), ("rep", T.rep[:, :, BW - 1], -BIG)):
        op("v", lambda ap=ap, c=c: v.memset(ap, c), (), nm(2, x), bk(2) if x == "#D" else ())
        if x == "GB":
            ts(T.pa[:], T.pi[:], 15, ALU.bitwise_and, r=["pi"], w=["pa"])
            line("v", C[:, 0:1], T.pi[:], 1.0, 0.0, ["pi"], ["c0"])
        if x == "Dt":
            act(T.one[:], T.Dt[:, 0, :, 0:16], AF.Exp, scale=0.0, r=nm(2, x), w=["one"])
    line("v", pk, T.pa[:], 1.0, 0.0, ["pa"], ["pk"])
    ts(T.I[:], T.q[:], C[:, 0:1], ALU.is_equal, r=["q", "c0"], w=["I"])
    tt(C[:, 4:5], C[:, 0:1], pk, ALU.subtract, ["c0", "pk"], ["c4"])
    line("v", C[:, 8:9], pk, 1.0, float(V + 16), ["pk"], ["c8"])
    ts(T.blk[:], T.q16[:], C[:, 4:5], ALU.is_equal, r=["q16", "c4"], w=["blk"])
    for x, src, sc in (("In", "I", -1.0), ("If", "I", 1.0), ("Ih", "I", 0.5)):
        line("a", T[x][:], T[src][:, 0:128], sc, 0.0, [src], [x])
    for i, sc in enumerate((1.0, 1.0, NR / (2.0 * NR - 16), 1.0 / (16.5 - TH))):
        line("a", marks(8 * i), T.blk[:, 0:128:16], sc, 0.0, ["blk"], ["G%d" % i])
    line("a", T.Gf[:], T.blk[:, 0:128:16], 1.0, 0.0, ["blk"], ["Gf"])
    GS = ["G%d" % i for i in range(4)]
    for d in range(NB):
        for i in range(d, NB):
            line("a", T.GB[:, 8 * d + i:8 * d + 8:NB], T.blk[:, 16 * (i - d):128:16 * NB], -BIG if i else BIG, 0.0, ["blk", "GB0"], ["GB%d%d" % (d, i)])
    GBS = ["GB%d%d" % (d, i) for d in range(NB) for i in range(d, NB)]
    ts(T.fT[:, 0:128], T.ck[:, 0:128], pk, ALU.is_equal, BIG, ALU.mult, r=["ck", "pk"], w=["fT0"])
    ts(T.Mk[:], T.ck[:, 0:128], pk, ALU.is_lt, 0.5, ALU.mult, r=["ck", "pk"], w=["Mk"])
    ts(T.Mi[:], T.ck[:], pk, ALU.is_equal, r=["ck", "pk"], w=["Mi"])
    tt(T.Mk[:], T.Mk[:], T.fT[:, 0:128], ALU.add, ["Mk", "fT0"], ["Mk"])
    line("v", T.LU[:], T.c16[:], float(BW), float(BW - 1), ["c16"], ["LU"])
    line("v", T.LD[:], T.c16[:], 1.0, 0.0, ["c16"], ["LD"])
    line("a", T.KC[:], T.c16[:, 0:8], 0.0, float(C0 + 17), ["c16"], ["KC"])
    line("v", T.zc[:], T.w0s[:], 1.0, float(-C0), ["w0s"], nm(2, "zc"))
    turned(1)
    ts(T.u0[:], T.w0s[:], float(V - 1), ALU.is_ge, float(-V), ALU.mult, r=["w0s"], w=["u0"])
    line("v", T.WL[:, 0:16], T.w0s[:], 1.0, 0.0, ["w0s"], nm(2, "WL1"))
    tt(T.u0[:], T.u0[:], T.zc[:], ALU.add, ["u0"] + nm(2, "zc"), ["u0"])
    line("v", T.Os[:, 256:MW], T.pz[:, 0, 256:MW], 1.0, float(C0), ["#C0"], ["Ow"], [6])
    tt(T.wx[:], T.u0[:].indirect(T.LD[:]), T.Mi[:], ALU.mult, ["u0", "LD", "Mi"], ["wx"])

    def ahead():
        send(guest(1), T.Oin[:, 256:MW], T.Os[:, 256:MW], "aw", ["Ow"])

    def differences():
        for c, fill in ((1, -1.0), (2, 1.0)):
            for m in (0, 1):
                select(T.Dt[:, :, :, c:c + 16], [[-1, RO], [-16, 8], [1, 16]], ALU.not_equal, fill, -16 * m, 1, (), nm(2, "Dt"))
        select(T.Dt[:, :, :, 1:18], [[0, RO], [-16, 8], [0, 17]], ALU.is_ge, 0.0, 0, 1, (), nm(2, "Dt"))
        select(T.Dt[:, :, :, 1:18], [[0, RO], [16, 8], [0, 17]], ALU.is_ge, 0.0, 15, -1, (), nm(2, "Dt"))

    def spread(t):
        if t == 2:
            iota(T.Sel[:], [[0, 2048]], "Sel", 1, ["Os%d" % t])
        if t == 3:
            select(T.Sel[:], [[-1, 128], [0, 16]], ALU.is_equal, 0.0, 0, 1, ["Os%d" % t], ["Sel"])

    bank, due, counted, before, answer = {}, {}, {}, {}, {}

    def lists(t, e, out, off, r, w, add=0.0, ext=()):
        if t == 1:
            gather(e, out, T.recs[:], off, RECS + r, w, add - C0, ext)
        else:
            gather(e, out, T.Rt[:, 16:16 + V], off, ["Rt"] + r, w, add, ext)

    def times(t, h):
        return T.WL[:, part(h, 8, 16 * (t - 1))]

    def arrived(t):
        return [("ao%d" % t, narr(asker(t)))]

    def ask(t, e):
        n = MW if t > 1 else 256
        s = hs(0, n, (t - 1) * MW)
        mms([(T.pz[:, 0, 0:256], turn(t), T.ch[:])], ["I", "ch"], ["#A0", "#B0"], [6])
        line(e, T.Os[:, s], T.pz[:, 0, 0:n], 1.0, float(C0), ["#A0", "#B0", "#C0"], ["Os%d" % t], [6])
        send(guest(t), T.Oin[:, s], T.Os[:, s], "ao%d" % t, ["Os%d" % t])

    def big(t, p, qu, e):
        qs, n = ([qu], 64) if qu < 4 else ([2 * qu - 8, 2 * qu - 7], 128)
        s = hs(qu % 4, 16 * n)
        if p == "o":
            lists(t, e, T.Ro[:, s], T.O[:, hs(qu % 4, n)], ["O"], ["Ro%d" % x for x in qs])
        elif p == "g":
            lists(t, e, T.Rg[:, s], T.Oin[:, hs(qu % 4, n, (t - 1) * MW)], [], ["Rg%d" % x for x in qs], 0.0, arrived(t))
        else:
            gather(e, T.xn[:, s], T.xe[:, 16:16 + V], T.O[:, hs(qu % 4, n)], ["xe1", "xe2", "O"], ["xn%d" % x for x in qs])

    def piece(u):
        key, n = bank[u]
        b = plan[1][key] if plan else 0
        return T.ps[:, b:b + n, :], ["%s.%d" % (key, i) for i in range(n)], (key, n, list(range(n)))

    def cols(h, j, n=1):
        return hs(0, 512 * n, 512 * (4 * h + j))

    def sub(x, h, j, n):
        return ["%s%d%d" % (x, h, j + i) for i in range(n)]

    def diff(t, p, h, j, n=0):
        u = (p, h, j)
        if n:
            bank[u] = (TAG[0], n)
        key, m = bank[u]
        wide, small = {"o": ("Ro", "ch"), "g": ("Rg", "cg"), "x": ("xn", "xz")}[p]
        for i in range(m):
            ks = range(4 * (j + i), 4 * (j + i + 1))
            if p == "x" and t == RO and n:
                calls, rd = [(T.xn[:, hs(k, 128, 2048 * h)], Id) for k in ks], ["xn%d" % (2 * h + (j + i) // 2)]
            elif p == "x" and t == RO:
                calls, rd = [(T.Sel[:, hs(k)], T.xt[:, hs(h)]) for k in ks], ["Sel", "xt%d" % h]
            elif (p == "x") == (n > 0):
                calls = [(Id, T[wide][:, 2048 * h + k:2048 * (h + 1):16]) for k in ks]
                rd = ["%s%d" % (wide, 2 * h), "%s%d" % (wide, 2 * h + 1)]
            else:
                calls, rd = [(T.In[:], T[small][:, hs(h)])] * 4, ["xz%d" % h if p == "x" else small]
            w = ["%s.%d" % (key, i)]
            b = (plan[1][key] if plan else 0) + i
            mms([(T.ps[:, b, hs(k)], l, x) for k, (l, x) in enumerate(calls)], ["I", "In"] + rd, w, (key, m, [i]), n > 0, n == 0)

    def test(t, p, h, j):
        d, rd, bs = piece((p, h, j))
        c = BH if p == "x" else B2
        ts(T["d" + p][:, cols(h, j, bs[1])], d, c, ALU.add, c, ALU.not_equal if p == "o" else ALU.is_equal, r=rd,
           w=sub("d" + p, h, j, bs[1]), banks=bs)
        due[p, h, j] = (bs[1], {"g": t % 8, "o": MISS, "x": MARK}[p])

    def sgn(h, j, n):
        act(T.dx[:, cols(h, j, n)], T.ad[:, cols(h, j, n)], AF.Sign, bias=0.5 + 2.0 ** -21, scale=-1.0, r=sub("ad", h, j, n), w=sub("dx", h, j, n))
        due["x", h, j] = (n, SIGNS)

    def into(x, h, j, calls, r):
        if (x, h) not in counted:
            counted[x, h], before[x, h] = [], users(slots(h, x))
        counted[x, h].append("%s%d%d" % (x, h, j))
        mms(calls, r, counted[x, h][-1:], bk(h), each=True)
        ops[-1]["deps"].update(before[x, h])

    def filled(h, x):
        return [n for i in halves(h) for n in counted.pop((x, i))] + slots(h, x)

    def count(t, p, h, j):
        x = {"o": "LT", "g": "Lg", "x": "NC"}[p]
        (n, s), (o, wide, _) = due.pop((p, h, j)), REG[x]
        into(x, h, j, [(T.pz[:, h, o + (k if p == "x" else (t - k - 1) % 16 + (p == "o")):o + wide:wide // 8], T["d" + p][:, hs(k, 128, 2048 * h)], marks(s))
                       for k in range(4 * j, 4 * (j + n))], GS + sub("d" + p, h, j, n))

    def reaches(e, out, in_, bound, r, w, banks):
        if e == "v":
            ts(out, in_, float(bound), ALU.is_ge, r=r, w=w, banks=banks)
        else:
            act(out, in_, AF.Sign, bias=0.5 - bound, r=r, w=w, banks=banks)

    def reply(t, h, e):
        s = part(h, 8, (t - 1) * 16)
        reaches(e, T.rep[:, s, 1:17], reg("Lg", h), TH, filled(h, "Lg") + nm(h, "rep"), nm(h, "rep%d" % t), bk(h))
        send(asker(t), T.repin[:, BW * s.start:BW * s.stop], T.rep[:, s, :], "ar%d%d" % (h, t), nm(h, "rep%d" % t))
        answer.update({i: h for i in halves(h)})

    def chosen(buf, h):
        s = part(h, 8 * BW)
        return buf[:, s.start + BW - 1:s.stop:BW]

    def steps(t, h):
        o, e8 = reg("dn", h), hs(h, 8)
        lead = T.pz[:, h, 1:8 * BW:BW]
        calls = [(o, T.ch[:, hs(h)], T.Dt[:, t - 1]), (o, T.rr[:, hs(h)], T.Dt[:, t - 1])]
        if t == 1:
            calls.append((lead, T.wx[:, hs(h)], marks(MARK)))
        else:
            calls += [(lead, T.If[:], chosen(T.U, h)), (lead, Id, T.rw[:, e8]), (lead, Id, T.one[:, 0:8])]
        mms(calls, ["ch", "rr", "wx", "I", "If", "one"] + GS + nm(2, "Dt") + nm(h, "U", "rw"), slots(h, "dn"), bk(h))

    def untwin(t, h):
        ext = [("ar%d%d" % (x, t), narr(guest(t))) for x in sorted(set(answer[i] for i in halves(h)))]
        tt(T.nk[:, part(h, 8 * BW)], reg("LT", h), T.repin[:, part(h, 8 * BW, (t - 1) * 16 * BW)], ALU.is_ge, filled(h, "LT"), nm(h, "nk"), bk(h), ext)

    def scan(out, d0, d1, o0, o1, r, w, banks):
        op("v", lambda: v.tensor_tensor_scan(out, d0, d1, 0.0, o0, o1), r, w, banks)

    def choose(h):
        for x in halves(h):
            scan(T.U[:, hs(x, 8 * BW)], reg("dn", x), T.nk[:, hs(x, 8 * BW)], ALU.add, ALU.mult, slots(x, "dn") + nm(x, "nk"), nm(x, "U"), bk(x))
        src = T.U[:, part(h, 8 * BW)].indirect(T.LU[:, 0:8 * len(halves(h))])
        tt(T.H[:, part(h)], src, T.Mi[:, part(h)], ALU.mult, nm(h, "U") + ["LU", "Mi"], nm(h, "H"))
        for x in halves(h):
            mms([(reg("Z", x), T.H[:, hs(x)], marks(MARK))], GS + nm(x, "H"), slots(x, "Z"), bk(x))

    def flag(h, e):
        scan(T.F[:, part(h, 8 * BW)], T.nk[:, part(h, 8 * BW)], T.e0[:, part(h, 8 * BW)], ALU.mult, ALU.add, nm(h, "nk", "e0"), nm(h, "F"), ())
        tt(T.uf[:, part(h, 8)], chosen(T.U, h), chosen(T.F, h), ALU.add, nm(h, "U", "F"), nm(h, "uf"))
        gather(e, T.ub[:, part(h)], T.uf[:, part(h, 8)], T.LD[:, 0:8 * len(halves(h))], nm(h, "uf") + ["LD"], nm(h, "ub"))

    def claim(h, d):
        for x in halves(h):
            calls = [(T.blk[:, 16 * d:16 * d + 128], T.H[:, hs(x)])] + [(Id, T.Mk[:])] * (d == 0)
            mms([(reg("eq", x), l, r) for l, r in calls], ["blk", "I", "Mk"] + nm(x, "H"), slots(x, "eq"), bk(x))
        tt(T.eq[:, part(h, 128, 256 * d)], reg("eq", h), T.ub[:, part(h)], ALU.is_equal, slots(h, "eq") + nm(h, "ub"), nm(h, "eq%d" % d), bk(h))

    def target(h):
        for x in halves(h):
            calls = [(T.H[:, hs(x)], marks(MARK)), (Id, T.KC[:])] + [(T.eq[:, hs(x, 128, 256 * d)], T.GB[:, hs(d, 8)]) for d in range(NB)]
            mms([(reg("tg", x), l, r) for l, r in calls], GS + GBS + ["I", "KC"] + nm(x, "H", *["eq%d" % d for d in range(NB)]), slots(x, "tg"), bk(x))
        ts(T.tg[:, part(h, 8)], reg("tg", h), C[:, 8:9], ALU.min, pk, ALU.max, r=slots(h, "tg") + ["c8", "pk"], w=nm(h, "tg"), banks=bk(h))

    def after(h):
        for x in halves(h):
            mms([(reg("nP", x), Id, r) for r in (T.ch[:, hs(x)], T.rr[:, hs(x)], T.one[:])], ["I", "ch", "rr", "one"], slots(x, "nP"), bk(x))

    def near(h, e):
        reaches(e, T.fT[:, part(h)], reg("NC", h), NR, filled(h, "NC"), nm(h, "fT"), bk(h))
        for x in halves(h):
            calls = [(T.fT[:, hs(x)], Id)] if e == "v" else [(T.one[:], T.Ih[:]), (T.fT[:, hs(x)], T.Ih[:])]
            mms([(reg("put", x), l, r) for l, r in calls], ["I", "Ih", "one"] + nm(x, "fT"), slots(x, "put"), bk(x))

    def put(h):
        for b in range(8 * (h + 1) // NB - 1, 8 * h // NB - 1, -1):
            tt(T.Rt[:].indirect(T.tg[:, hs(b, NB)]), T.old[:, hs(b, 16 * NB)], T.pr[:, hs(b, 16 * NB)], ALU.subtract,
               nm(h, "pr", "old", "tg") + ["Rtb0", "Rtb1"] + ["Rt%d" % i for i in range(NCH)], ["Rt"])

    def absd(h, j):
        d, rd, bs = piece(("x", h, j))
        act(T.ad[:, cols(h, j, bs[1])], d, AF.Abs, r=rd, w=sub("ad", h, j, bs[1]), banks=bs)

    def expo(t, h, j, n):
        act(T.ex[:, hs(0, 4 * n, 16 * (t % 2) + 4 * j), hs(h)], T.ad[:, cols(h, j, n)], AF.Exp, scale=-1.0,
            r=sub("ad", h, j, n), w=sub("ex%d" % (t % 2), h, j, n))

    def fold(t):
        rid, pid, _ = topo.addr(helper)
        en, m = fold_engines(topo, core, helper, t), FOLDS[t][0]
        trs = [RemoteDMATransfer(dst_ids=[DstId(rid=rid, pnc=pid)], dma_engine_mask=mask_of(en), remote_sem=T.sem["af%d" % t],
                                 srcs=[T.ex[:, hs(k, m, 16 * (t % 2)), :] for k in range(16 // m)], dsts=[T.fl[:, t - 1, 0:256 * m]], alu_op=1)]
        raised["ay%d" % t] = len(ops)
        op("g", lambda: g.remote_dma_fused(trs, local_sem=T.sem["sf%d" % t]), sub("ex%d" % (t % 2), 0, 0, 4) + sub("ex%d" % (t % 2), 1, 0, 4),
           tok=("sf%d" % t, len(en)))

    nys = [0]

    def store(cs, src, r=(), ext=()):
        nys[0] += 16
        dma("s", T.y[:, cs], src, "ys", nys[0], r=r, ext=ext)

    def sums(t, e):
        ext = [("ay%d" % t, len(topo.engines(helper, core)))]
        if FOLDS[t][0] == 1:
            store(hs(t - 1, 256), T.yl[:, t - 1, 0:256], ext=ext)
        else:
            tt(T.yt[:, t - 1, :], T.yl[:, t - 1, 0:256], T.yl[:, t - 1, 256:512], ALU.add, (), ["yt%d" % t], (), ext)
            store(hs(t - 1, 256), T.yt[:, t - 1, :], ["yt%d" % t])

    def turn_xz(h, e):
        mms([(reg("xt", h), T.xz[:, hs(h)], T.In[:])], ["In"] + nm(h, "xz"), slots(h, "xt"), bk(h))
        line(e, T.xt[:, hs(h)], reg("xt", h), 1.0, 0.0, slots(h, "xt"), nm(h, "xt"), bk(h))

    def tail_abs(h, j):
        d, rd, bs = piece(("x", h, j))
        ng = T.ng[:, 0:512 * bs[1]]
        line("v", ng, d, -1.0, 0.0, rd, ["ng"], bs)
        tt(T.ad[:, cols(h, j, bs[1])], ng, d, ALU.max, ["ng"] + rd, sub("ad", h, j, bs[1]), bs)

    def tail_sum(h, j, n):
        into("S", h, j, [(T.pz[:, h, hs(k, 8)], T.ex[:, 16 * (RO % 2) + k, hs(h)], T.Gf[:]) for k in range(4 * j, 4 * (j + n))],
             ["Gf"] + sub("ex%d" % (RO % 2), h, j, n))

    def tail_store(h, e):
        line(e, T.yt[:, RO - 1, hs(h)], reg("S", h), 1.0, 0.0, filled(h, "S"), nm(h, "yh"), bk(h))
        store(hs(h, 128, (RO - 1) * 256), T.yt[:, RO - 1, hs(h)], nm(h, "yh"))

    def run(t, w):
        c, p = w[:2], [int(z) if z.isdigit() else z for z in w[2:]]
        h = p[0] if p else 2
        if c[0] in "PD":
            diff(t, c[1], *p)
        elif c[0] == "N":
            count(t, c[1], *p)
        elif c in ("go", "gg", "gx"):
            big(t, c[1], *p)
        elif c in ("to", "tg", "tx"):
            test(t, c[1], *p)
        elif c == "ol":
            ts(T.O[:], T.ch[:], float(C0), ALU.add, r=["ch"], w=["O"])
        elif c == "ch":
            lists(t, h, T.ch[:], times(t, 2), nm(2, "WL%d" % t), ["ch"])
        elif c == "rr":
            ts(T.rr[:], T.ch[:], float(C0 - 1), ALU.is_ge, float(-V), ALU.mult, r=["ch"], w=["rr"])
        elif c == "rw":
            ts(T.rw[:, part(h, 8)], chosen(T.U, h), float(V - 2 - C0), ALU.is_ge, float(-V), ALU.mult, r=nm(h, "U"), w=nm(h, "rw"))
        elif c == "cg":
            lists(t, h, T.cg[:], T.Oin[:, hs(0, 16, (t - 1) * MW + 256)], [], ["cg"], 0.0, arrived(t) if t > 1 else [("aw", narr(asker(t)))])
            if t == 1:
                dma("s", T.xa[:], T.x[:], "lx2", 16, w=["xa"], ext=arrived(t))
        elif c == "cv":
            line(p[1], T.Rt[:, 16 + CUTS[h]:16 + CUTS[h + 1]], T.recs[:, cut[h]], 1.0, float(-C0), ["recs%d" % h], ["Rt%d" % h])
        elif c == "wl":
            line(p[1], times(t + 1, h), reg("Z", h), 1.0, float(C0 + 1), slots(h, "Z"), nm(h, "WL%d" % (t + 1)), bk(h))
        elif c == "zc":
            line(p[1], T.zc[:, part(h, 8)], reg("Z", h), 1.0, 1.0, slots(h, "Z"), nm(h, "zc"), bk(h))
            turned(t + 1)
        elif c == "xz":
            gather(p[1], T.xz[:, part(h)], T.xa[:], times(t + 1, h), ["xa"] + nm(h, "WL%d" % (t + 1)), nm(h, "xz"))
        elif c == "od":
            lists(t, p[1], T.old[:, part(h)], times(t + 1, h), nm(h, "WL%d" % (t + 1)), nm(h, "old"))
        elif c == "ed":
            tt(T.Ed[:, part(h)], T.old[:, part(h)], reg("nP", h), ALU.subtract, nm(h, "old") + slots(h, "nP"), nm(h, "Ed"), bk(h))
        elif c == "pr":
            tt(T.pr[:, part(h)], T.Ed[:, part(h)], reg("put", h), ALU.mult, nm(h, "Ed") + slots(h, "put"), nm(h, "pr"), bk(h))
        elif c in ("os", "th", "dn", "nk", "ex", "fo", "ys", "se"):
            {"os": ask, "th": reply, "dn": steps, "nk": untwin, "ex": expo, "fo": fold, "ys": sums, "se": spread}[c](t, *p)
        else:
            {"aw": ahead, "dt": differences, "sc": choose, "fs": flag, "eq": claim, "ai": target, "np": after, "ft": near, "ab": absd,
             "sg": sgn, "pu": put, "da": tail_abs, "ts": tail_sum, "st": tail_store, "xt": turn_xz}[c](*p)

    words = [(t - w.count("-"), w.strip("-")) for t in range(1, RO + 1) for w in {1: SEQ1, RO: SEQL}.get(t, SEQ).split() if t > w.count("-")]
    for t, _, _, w in sorted((t, STAGES.index(w[:2]), w[2:3] != "1", w) for t, w in words if ":" not in w):
        TAG[0], first, at = "%d%s" % (t, w), len(ops), words.index((t, w))
        run(t, w)
        for n, o in enumerate(ops[first:]):
            later = (t, "%s:%d" % (w.rstrip("va"), n + 1))
            at = o["at"] = words.index(later) if later in words else at
    for o in ops:
        o["needs"] = sorted(o["deps"]) + o["far"]
    if plan:
        emit()
    return ops
